import numpy as np, ml_dtypes
CORES = [35,38,43,46]
N = 4
BF = ml_dtypes.bfloat16
def gentries(a):
    return np.ascontiguousarray(a.reshape(8, 16, -1).transpose(0, 2, 1)).reshape(8, -1)
def gtable(e):
    e = np.asarray(e); return np.ascontiguousarray(e.reshape(8, -1, 16).transpose(0, 2, 1)).reshape(128, -1).astype(np.int32)
W, K, O, TH, CAP, RO = 8192, 8, 256, 200, 32, 5
def ring(rng):
    gap = rng.integers(0, W // K, (N, 8, K, O)) + 1; gap[:, :, 0] = rng.integers(0, W, (N, 8, O))
    return np.add.accumulate(gap, axis=2) & (W - 1)
def held(c, want, pri):
    h = np.zeros(c.shape, np.int64)
    for q in range(N):
        for g in range(8):
            p = np.broadcast_to(pri[q, g], (K, O)); low = np.full(W, O); w = want[q, g]
            np.minimum.at(low, c[q, g][w], p[w]); h[q, g] = w & (low[c[q, g]] == p)
    return h
def crew(rng):
    c = ring(rng); lv = rng.choice(np.array([0, K // 2, K - 2, K - 1, K]), (8, O)); pri = np.zeros((8, O), np.int64); cls = np.zeros((8, 1, O), bool)
    nf = rng.permutation(8 + (O * 45 // 100 - 8) * np.arange(8) // 7)
    for g in range(8):
        n = int(nf[g]); o = rng.permutation(O); lv[g, o[:n]] = K; pri[g, o] = np.arange(O); cls[g, 0, o[:n]] = True
        for q in range(N):
            own = rng.permutation(W)[:n * K].reshape(K, n); c[q, g][:, o[:n]] = own
            rest = c[q, g][:, o[n:]]; t = rng.choice(own.reshape(-1), O - n); k = rng.integers(0, K, O - n)
            ok = (rng.random(O - n) < 0.3) & ~np.any(rest == t, axis=0)
            rest[k[ok], np.flatnonzero(ok)] = t[ok]; c[q, g][:, o[n:]] = rest
    want = (np.arange(K)[:, None] < lv[:, None, :]) & (cls | (rng.random((N, 8, K, O)) < 0.95))
    return c, held(c, want, np.broadcast_to(pri, (N, 8, O)))
def far(rng, m, share, over):
    k = rng.integers(0, K, (N, 8, O)); k = np.where(rng.random(k.shape) < 0.5, k, (K - 1) * rng.integers(0, 2, k.shape))
    hit = (rng.random((N, 8, 1, O)) < share) & (np.arange(K)[:, None] == k[:, :, None, :])
    return np.where(hit, TH + rng.integers(1, over + 1, m.shape), m)
def naps(rng, share):
    return np.add.reduce((rng.random((N, 8, O, RO)) < share).astype(np.int64) << np.arange(RO), axis=3)
def pack(x, c, h, m, wk, lump=None):
    ix = c.reshape(N, 8, 1, K * O); xc = np.take_along_axis(x, ix, 3); m = m.reshape(N, 8, 1, K * O)
    d = (m >> 4) + (((np.arange(16).reshape(16, 1) + ix) & 15) < (m & 15))
    if lump is not None:
        s = lump.reshape(N, 8, 1, K * O); i = (np.arange(16).reshape(16, 1) + s) & 15
        most = np.take_along_axis(np.maximum(xc, 255 - xc), i, 2).astype(np.int64); before = np.add.accumulate(most, axis=2) - most
        u = np.zeros(i.shape, np.int64); np.put_along_axis(u, i, np.minimum(np.maximum(m - before, 0), most), 2)
        d = np.where(s < 16, u, d)
    e = np.where(xc < 128, xc + d, xc - d)
    return {"x": np.ascontiguousarray(x.reshape(N, 128, W)).astype(np.float32).astype(BF), "snap": np.ascontiguousarray(e.reshape(N, 128, K * O)).astype(np.float32).astype(BF),
            "cs": np.stack([gtable(a.reshape(8, -1)) for a in c]), "hold": np.stack([gtable(a.reshape(8, -1)) for a in h]), "wake": np.stack([gtable(a) for a in wk])}
def cells(rng):
    return rng.integers(0, 256, (N, 8, 16, W), dtype=np.int32)
def setup_inputs(rng):
    x = cells(rng); c, h = crew(rng); m = far(rng, rng.integers(0, TH + 1, c.shape), 0.08, 600)
    return pack(x, c, h, m, naps(rng, rng.choice(np.array([0.5, 0.7, 0.9]), (N, 8, 1, 1))))
def setup_inputs_room(rng):
    x = cells(rng); c = np.zeros((N, 8, K, O), np.int64); h = np.ones((N, 8, K, O), np.int64); m = rng.integers(0, TH + 1, c.shape); wk = naps(rng, 0.7)
    cnt = rng.permutation(np.array([0, 1, CAP - 1, CAP, CAP + 1, 2 * CAP, O - 1, O]))
    for g in range(8):
        n = int(cnt[g]); o = rng.permutation(O)
        if n == 0: wk[:, g] = 1
        for q in range(N):
            c[q, g] = rng.permutation(W)[:K * O].reshape(K, O)
            rest = o[n:] if q & 1 else o[n:][rng.random(O - n) < 0.5]
            h[q, g][rng.integers(0, K, len(rest)), rest] = 0
            if q & 1 == 0 and n > 0: m[q, g][rng.integers(0, K), rest[rng.random(len(rest)) < 0.15]] = TH + 1
    return pack(x, c, h, m, wk)
def setup_inputs_storm(rng):
    x = cells(rng); c = ring(rng); m = rng.integers(0, TH + 1, c.shape); want = rng.random(c.shape) < 0.5; wk = naps(rng, 0.8)
    pri = np.argsort(rng.random((N, 8, O)), axis=-1); deal = rng.permutation(8); role = deal & 3
    for g in range(8):
        if deal[g] == 0:
            want[:, g] = True
            for q in range(N): c[q, g] = rng.permutation(W)[:K * O].reshape(K, O)
        if role[g] == 0: m[:, g, rng.integers(0, K)] = TH + 1 + rng.integers(0, 600, (N, O))
        if role[g] == 1: m[::2, g, 0, ::2] = TH + 1
        if role[g] == 2:
            o = int(rng.integers(0, O))
            for q in range(N):
                v = int(rng.integers(0, W)); k = rng.integers(0, K, O); ok = ~np.any(c[q, g] == v, axis=0)
                c[q, g][k[ok], np.flatnonzero(ok)] = v; x[q, g, :, v] = rng.integers(0, 16, 16) + 240 * (q & 1)
                want[q, g, :, o] = True; i = int(np.flatnonzero(pri[q, g] == 0)[0]); pri[q, g, i] = pri[q, g, o]; pri[q, g, o] = 0
        if role[g] == 3: want[:, g] = False; wk[:, g] = wk[:, g] & ~1
    p = 2 * int(rng.integers(0, N // 2)); m[p:p + 2] = far(rng, m, 1.0, 600)[p:p + 2]
    return pack(x, c, held(c, want, pri), m, wk)
def setup_inputs_crowd(rng):
    x = cells(rng); c = np.zeros((N, 8, K, O), np.int64)
    for q in range(N):
        for g in range(8):
            P = 64 if g & 1 else 256
            pool = rng.permutation(np.concatenate([np.array([0, W - 1]), 1 + rng.permutation(W - 2)[:P - 2]]))
            c[q, g] = pool[(rng.integers(0, P, O) + np.arange(K)[:, None] * (2 * rng.integers(0, P // 2, O) + 1)) & (P - 1)]
    pri = np.argsort(rng.random((8, O)), axis=-1); lv = np.where(pri < 3, K, rng.integers(0, K + 1, (8, O)))
    lv[rng.permutation(8)[:4]] = 0
    want = np.broadcast_to(np.arange(K)[:, None] < lv[:, None, :], (N, 8, K, O))
    m = far(rng, rng.integers(0, TH + 1, c.shape), 0.01, 600)
    return pack(x, c, held(c, want, np.broadcast_to(pri, (N, 8, O))), m, naps(rng, rng.choice(np.array([0.6, 1.0]), (N, 8, 1, 1))))
def setup_inputs_ties(rng):
    x = cells(rng); z = rng.random((N, 8, 1, W)); x = np.where(z < 0.06, 0, np.where(z < 0.12, 255, x)).astype(np.int32)
    c, h = crew(rng); m = far(rng, rng.choice(np.array([0, TH - 1, TH]), c.shape), 0.12, 1)
    wk = naps(rng, 0.75) & ~(1 << int(rng.integers(1, 3)))
    return pack(x, c, h, m, wk, np.minimum(rng.integers(0, 32, c.shape), 16))
def setup_inputs_spread(rng):
    x = np.minimum((np.exp2(8.01 * rng.random((N, 8, 1, W))) * rng.random((N, 8, 16, W))).astype(np.int32), 255)
    c, h = crew(rng); m = far(rng, (TH * rng.random(c.shape) ** 4).astype(np.int64), 0.1, 1000)
    share = np.ones((N, 1, 1, 1)) * rng.permutation(np.array([0.0, 0.2, 0.4, 0.6, 0.8, 0.9, 1.0, 1.0])).reshape(1, 8, 1, 1)
    return pack(x, c, h, m, naps(rng, share))
def check_inputs(d):
    bad = []
    for k in ("x", "snap"):
        v = np.asarray(d[k]).astype(np.float32)
        if not (np.all(v >= 0) and np.all(v <= 255) and np.all(v == np.floor(v))): bad.append("range of " + k)
    for k, hi in (("cs", W - 1), ("hold", 1), ("wake", 2 ** RO - 1)):
        if np.min(d[k]) < 0 or np.max(d[k]) > hi: bad.append("range of " + k)
    c = np.stack([gentries(a) for a in d["cs"]]).reshape(N, 8, K, O); h = np.stack([gentries(a) for a in d["hold"]]).reshape(N, 8, K, O)
    s = np.sort(c, axis=2)
    if np.any(s[:, :, 1:] == s[:, :, :-1]): bad.append("cells of an operation differ")
    for q in range(N):
        for g in range(8):
            v = c[q, g][h[q, g] == 1]
            if len(np.unique(v)) != len(v) and "a cell has one holder" not in bad: bad.append("a cell has one holder")
    return bad
def reference(x, snap, cs, hold, wake):
    v = np.zeros((N, 8, 16, W + 1), np.int32)
    v[..., :W] = x.astype(np.float32).astype(np.int32).reshape(N, 8, 16, W)
    e = snap.astype(np.float32).astype(np.int32).reshape(N, 8, 16, K * O)
    c = np.stack([gentries(a) for a in cs]).astype(np.int64).reshape(N, 8, K, O); h = np.stack([gentries(a) for a in hold]).reshape(N, 8, K, O)
    wk = np.stack([gentries(a) for a in wake]).astype(np.int64)
    own = np.arange(O) + 1; lane = np.broadcast_to(np.arange(O), (N, 8, O)); cur = np.array(lane)
    lock = np.zeros((N, 8, W + 1), np.int64)
    np.put_along_axis(lock, np.where(h == 1, c, W).reshape(N, 8, -1), np.broadcast_to(own, c.shape).reshape(N, 8, -1), 2)
    for t in range(RO):
        twin = np.arange(N) ^ (1 + t % (N - 1))
        got = np.take_along_axis(v, c.reshape(N, 8, 1, -1), 3)
        dist = np.add.reduce(np.abs(got - e), axis=2).reshape(N, 8, K, O)
        who = np.take_along_axis(lock, c.reshape(N, 8, -1), 2).reshape(N, 8, K, O); mine = who == own
        bad = np.any(dist > TH, axis=2); full = np.all(mine, axis=2)
        abort = bad | bad[twin]; ready = full & full[twin] & ~abort
        before = np.add.accumulate(ready.astype(np.int64), axis=2) - ready
        commit = ready & (before < CAP); done = abort | commit
        first = np.argmin(mine, axis=2)[:, :, None, :]
        cell = np.take_along_axis(np.take_along_axis(c, first, 2)[:, :, 0], cur, 2); by = np.take_along_axis(np.take_along_axis(who, first, 2)[:, :, 0], cur, 2)
        gone = np.take_along_axis(done, cur, 2); act = (((wk >> t) & 1) == 1) & ~gone & ~np.take_along_axis(full, cur, 2)
        np.put_along_axis(lock, np.where(done[:, :, None, :] & mine, c, W).reshape(N, 8, -1), 0, 2)
        for q in range(N):
            for g in range(8):
                w = np.flatnonzero(act[q, g] & (by[q, g] == 0)); low = np.full(W, O); a = cell[q, g][w]
                np.minimum.at(low, a, w); win = low[a] == w
                lock[q, g][a[win]] = cur[q, g][w[win]] + 1
        cur = np.where(gone, lane, np.where(act & (by > 0), by - 1, cur))
        cm = np.broadcast_to(commit[:, :, None, :], (N, 8, K, O)); dn = np.broadcast_to(done[:, :, None, :], (N, 8, K, O)).reshape(N, 8, 1, -1)
        d = np.where(cm.reshape(N, 8, 1, -1), got[twin], e)
        np.put_along_axis(v, np.where(cm, c, W).reshape(N, 8, 1, -1), d, 3)
        u = np.add.reduce(d.reshape(N, 8, 2, 8, K, O).astype(np.int64), axis=3); hs = (u[:, :, 0] * u[:, :, 1]) >> 3
        new = np.zeros((N, 8, K, O), np.int64); new[:, :, 0] = hs[:, :, 0] & (W - 1)
        for k in range(1, K): new[:, :, k] = (new[:, :, k - 1] + 1 + (hs[:, :, k] & (W // K - 1))) & (W - 1)
        c = np.where(done[:, :, None, :], new, c)
        e = np.where(dn, np.take_along_axis(v, c.reshape(N, 8, 1, -1), 3), e)
    lock[..., W] = 0
    mine = np.take_along_axis(lock, c.reshape(N, 8, -1), 2).reshape(N, 8, K, O) == own
    ys = np.add.reduce(v[..., :W] * np.arange(1, 17, dtype=np.int32).reshape(16, 1), axis=2)
    return {"ys": ys.astype(np.float32), "yc": np.stack([gtable(a.reshape(8, -1)) for a in c]).astype(np.float32),
            "yh": np.stack([gtable(a.reshape(8, -1)) for a in mine]).astype(np.float32), "yl": np.stack([gtable(a) for a in cur]).astype(np.float32)}

@@ -1,0 +1,615 @@
+from concourse.mybir import AluOpType as OP, ActivationFunctionType as AF
+
+NS = 5
+E0, VB, E1 = 0, 2048, 10496
+F, B, I, U16 = "float32", "bfloat16", "int32", "uint16"
+SCRATCH = {}
+
+
+def _buf(names, n, d):
+    for x in names.split():
+        SCRATCH[x] = ("sbuf", [128, n], d)
+
+
+_buf("VW", 12544, B)
+_buf("TT", 10240, F)
+_buf("YY", 8448, F)
+_buf("ad SEL WR", 2048, B)
+_buf("df gt", 1024, B)
+_buf("XO EQ", 4096, B)
+_buf("SELF WH", 2048, F)
+_buf("pI rI gI", 1, I)
+_buf("pF rF gF g15 lo8 r1", 1, F)
+_buf("uF sG sH ys8 tau tauL cdR clR", 256, F)
+_buf("mI mG hI", 128, I)
+_buf("ZB ZA ZH", 144, B)
+_buf("BO ID IN I8 NI LL TRI LT WY I64", 128, B)
+_buf("RM OW J16 JG cur1", 16, F)
+_buf("IG CT z256 taub vR dR gR cnR", 256, B)
+_buf("JE JE8 JE9 AGs oc oh fc", 128, F)
+_buf("WHT", 1024, F)
+_buf("thR", 264, F)
+_buf("ST", 1280, B)
+_buf("aw", 80, F)
+_buf("awI", 80, I)
+_buf("z32", 32, B)
+_buf("OWb", 16, B)
+_buf("wI", 16, I)
+_buf("clU", 256, U16)
+_buf("GG", 512, B)
+_buf("tw", 2200, F)
+_buf("tx", 3400, F)
+_buf("ti", 3000, I)
+_buf("tb", 2400, B)
+_buf("tu", 1400, U16)
+_buf("FL FR", 32 * NS, B)
+_buf("NG NR", 128 * NS, I)
+_buf("CO CR", 256 * NS, B)
+for _n in ("D1", "D2", "PA", "X1", "MK", "M1", "M2", "M3"):
+    SCRATCH["ps" + _n] = ("psum", [128, 512], F)
+LOADS = ["dcs", "dho", "dwk", "dsn", "dx"]
+SEMAPHORES = ["sv", "ss", "st", "sg", "lsem", "oc_", "oh_", "ol_", "oy_"] + LOADS + [k + str(t) for k in "fnc" for t in range(NS)]
+CY = 0.00083 * 1.15
+
+
+def rank_program(g, core, T, topo):
+    rank = T.rank_of(core)
+    if rank is None:
+        return
+    eng = {"v": g.vector, "s": g.scalar, "t": g.tensor, "g": g, "y": g.sync}
+    esem = {"v": "sv", "s": "ss", "t": "st", "g": "sg"}
+    ops = []
+
+    def A(name, a=0, b=None, step=1):
+        b = SCRATCH[name][1][1] if b is None else b
+        return ((T[name][:, a:b] if step == 1 else T[name][:, a:b:step]), ((name, a, b),), (b - a + step - 1) // step,
+                SCRATCH[name][2] in (B, U16), "ps" if name[:2] == "ps" else "sb")
+
+    def IND(w, off):
+        wn, a, b = w
+        on, c, d = off[1][0]
+        return T[wn][:, a:b].indirect(off[0]), ((wn, a, b), (on, c, d)), 16 * (d - c), SCRATCH[wn][2] == B, "ind"
+
+    def part(o, a, b):
+        name, s, _e = o[1][0]
+        return A(name, s + a, s + b)
+
+    def op(e, call, outs, ins, cost, sem=None, inc=1, arr=None):
+        rd = [x for o in ins for x in o[1]]
+        wr = []
+        for o in outs:
+            wr.append(o[1][0])
+            rd += list(o[1][1:])
+        ops.append({"e": e, "call": call, "rd": rd, "wr": wr, "cost": cost, "sem": sem or esem.get(e), "inc": inc, "arr": arr, "mm": None})
+
+    def vcost(o, ins, n, two=False):
+        if o[4] == "ind":
+            return 0.05 + n * 3.0 * CY
+        if any(x[4] == "ind" for x in ins):
+            return 0.05 + n * 1.5 * CY
+        return max(64, n * (2 if two and all(x[4] == "sb" for x in ins) else 0.5 if not two and o[3] and ins[0][3] else 1)) * CY
+
+    def tt(o, a, b, f):
+        op("v", lambda: g.vector.tensor_tensor(o[0], a[0], b[0], f), [o], [a, b], vcost(o, [a, b], b[2], True))
+
+    def ts(o, a, s1, f1, s2=None, f2=None):
+        col = [s1] if isinstance(s1, tuple) else []
+        x1 = s1[0] if col else s1
+        if f2 is None:
+            op("v", lambda: g.vector.tensor_scalar(o[0], a[0], x1, None, f1), [o], [a] + col, vcost(o, [a], a[2]))
+        else:
+            op("v", lambda: g.vector.tensor_scalar(o[0], a[0], x1, s2, f1, f2), [o], [a] + col, vcost(o, [a], a[2]))
+
+    def cp(o, a):
+        op("v", lambda: g.vector.tensor_copy(o[0], a[0]), [o], [a], vcost(o, [a], a[2]))
+
+    def ms(o, v):
+        op("v", lambda: g.vector.memset(o[0], v), [o], [], max(64, o[2] * (0.5 if o[3] else 1)) * CY)
+
+    def act(o, a, func=AF.Copy, bias=0.0, scale=1.0):
+        c = 0.065 + a[2] * (3.0 if o[4] == "ind" else 1.5) * CY if "ind" in (o[4], a[4]) else max(64, a[2]) * CY
+        col = [scale] if isinstance(scale, tuple) else []
+        x = scale[0] if col else scale
+        if not col and bias == 0.0 and scale == 1.0:
+            op("s", lambda: g.scalar.activation(o[0], a[0], func), [o], [a], c)
+        else:
+            op("s", lambda: g.scalar.activation(o[0], a[0], func, bias=bias, scale=x), [o], [a] + col, c)
+
+    def mm(lst, first=True, last=True):
+        c = sum(max(64, x[2][2]) * (1 if x[1][3] else 4) for x in lst) * 0.00042 * 1.15
+        op("t", None, [x[0] for x in lst], [y for x in lst for y in x[1:]], c)
+        ops[-1]["mm"] = (lst, first, last)
+
+    def win(z, i):
+        return A(z, 15 - i, 143 - i)
+
+    def to_w(o, src, sel="SEL"):
+        n = 2 if sel == "SELF" else 16
+        for j in range(0, 16, n):
+            mm([(o, A(sel, 128 * i, 128 * i + 128), A(src, i, 256, 16)) for i in range(j, j + n)], j == 0, j + n == 16)
+
+    def to_r(on, a, srcs):
+        lst = []
+        for i in range(16):
+            lst.append([(A(on, a + i, a + 256, 16), A("WR", 128 * i, 128 * i + 128), s) for s in srcs])
+        op("t", None, [A(on, a, a + 256)], [A("WR")] + srcs, 16 * len(srcs) * 64 * 0.00042 * 1.15)
+        ops[-1]["mm"] = (lst, True, True)
+
+    def rep(on, a, src):
+        op("t", None, [A(on, a, a + 128)], [A("ID"), src], 8 * 64 * 0.00042 * 1.15)
+        ops[-1]["mm"] = ([[(A(on, a + 16 * k, a + 16 * k + 16), A("ID"), src)] for k in range(8)], True, True)
+
+    def load(e, sem, o, tin):
+        op(e, lambda: eng[e].dma_start(o[0], tin), [o], [], 0.1, sem, 16, 2.5 + o[2] * (2 if o[3] else 4) * 128 / 200e3)
+        ops[-1]["load"] = True
+
+    twins = [T.cores[rank ^ (1 + t % 3)] for t in range(NS)]
+    narr = [len(topo.engines(d, core)[:8]) for d in twins]
+    nsent = [0]
+
+    def send(t, sb, rb, w, key):
+        dst = twins[t]
+        rid, pid, _se = topo.addr(dst)
+        es = topo.engines(core, dst)[:8]
+        s, r = A(sb, w * t, w * t + w), A(rb, w * t, w * t + w)
+        op("g", lambda: g.remote_dma(out_ap=r[0], in_ap=s[0], remote_sem=T.sem[key + str(t)], local_sem=T.sem.lsem, pid=pid, routing_id=rid,
+                                     dma_engine_mask=sum(1 << x for x in es)), [], [s], 0.8, "lsem", len(es))
+        op("a", None, [(None, ((rb, w * t, w * t + w),))], [s], 0.0, key + str(t), narr[t], 2.0 + w / 256.0)
+        ops[-1]["send"] = len(ops) - 2
+        nsent[0] += len(es)
+
+    tops = {"tw": 0, "tx": 0, "ti": 0, "tb": 0, "tu": 0}
+
+    def new(k, n):
+        a = tops[k]
+        if a + n > SCRATCH[k][1][1]:
+            a = 0
+        tops[k] = a + (n + 15) // 16 * 16
+        return A(k, a, a + n)
+
+    cI, cU = new("ti", 128), new("tu", 128)
+    load("s", "dcs", cI, T.cs[:])
+    load("s", "dho", A("hI"), T.hold[:])
+    load("y", "dsn", A("VW", E0, E0 + 2048), T.snap[:])
+    load("y", "dx", A("VW", VB, VB + 8192), T.x[:])
+    load("s", "dwk", A("wI"), T.wake[:])
+
+    def iota(o, pattern, base, cm, flag=True):
+        c = 0.13 + 2 * o[2] * CY
+        if flag:
+            op("g", lambda: g.iota(o[0], pattern, base, cm, allow_small_or_imprecise_dtypes=True), [o], [], c)
+        else:
+            op("g", lambda: g.iota(o[0], pattern, base, cm), [o], [], c)
+    iota(A("pI"), [[1, 1]], 0, 1, False)
+    iota(A("uF"), [[1, 256]], 0, 0)
+    iota(A("mI"), [[1, 128]], 0, 0, False)
+    iota(A("JE"), [[16, 128]], 0, 0)
+    iota(A("sG"), [[16, 2], [0, 8], [1, 16]], 936, 0)
+    iota(A("WH"), [[0, 8], [1, 256]], 33, 0)
+    ms(A("TT", 0, 4096), 0.0)
+    ts(A("rI"), A("pI"), 15, OP.bitwise_and)
+    ts(A("gI"), A("pI"), 112, OP.bitwise_and)
+    ts(A("mG"), A("mI"), 112, OP.bitwise_and)
+    cp(A("pF"), A("pI"))
+    cp(A("rF"), A("rI"))
+    cp(A("gF"), A("gI"))
+    ts(A("g15"), A("gF"), 15.0, OP.add)
+    ts(A("lo8"), A("rF"), 8.0, OP.is_lt)
+    ts(A("r1"), A("rF"), 1.0, OP.add)
+    ts(A("JE"), A("JE"), A("rF"), OP.add)
+    cp(A("OW"), A("JE", 0, 16))
+    ts(A("OWb"), A("OW"), 1.0, OP.add)
+    ts(A("J16"), A("JE", 0, 16), 8192.0, OP.add)
+    ts(A("JE8"), A("JE"), 8192.0, OP.add)
+    ts(A("JE9"), A("JE"), 8448.0, OP.add)
+    for q in range(4):
+        act(A("TT", 4096 + 1024 * q, 5120 + 1024 * q), A("TT", 1024 * q, 1024 * q + 1024))
+    x1, x2, x3, tl = new("tx", 128), new("tx", 128), new("tx", 128), new("tu", 128)
+    tt(x1, cI, A("JE8"), OP.subtract)
+    tt(x2, x1, A("hI"), OP.mult)
+    tt(x3, x2, A("JE8"), OP.add)
+    cp(tl, x3)
+    act(IND(("TT", 0, 10240), tl), A("WH"), AF.Silu)
+    cp(cU, cI)
+    Uh = new("tb", 128)
+    ts(Uh, A("hI"), -1.0, OP.mult, 1.0, OP.add)
+    ts(A("ZB"), A("uF", 0, 144), A("g15"), OP.is_equal)
+    ts(A("ZA"), A("ZB"), A("lo8"), OP.mult)
+    tt(A("ZH"), A("ZB"), A("ZA"), OP.subtract)
+    ts(A("BO"), A("mG"), A("gF"), OP.is_equal)
+    op("g", lambda: g.affine_select(T.LL[:], T.BO[:], [[-1, 128]], OP.is_ge, 0.0, 0, 1), [A("LL")], [A("BO")], 0.4)
+    ts(A("ID"), A("uF", 0, 128), A("pF"), OP.is_equal)
+    ts(A("I8"), A("ID"), 8.0, OP.mult)
+    ts(A("IN"), A("ID"), -1.0, OP.mult)
+    ts(A("NI"), A("ID"), -4096.0, OP.mult)
+    ts(A("RM"), A("uF", 0, 16), A("rF"), OP.is_equal)
+    ts(A("WY"), A("BO"), A("r1"), OP.mult)
+    for i in range(16):
+        ts(A("WR", 128 * i, 128 * i + 128), A("BO"), A("RM", i, i + 1), OP.mult)
+        ts(A("SEL", 128 * i, 128 * i + 128), A("ID"), A("RM", i, i + 1), OP.mult)
+        act(A("SELF", 128 * i, 128 * i + 128), A("ID"), AF.Copy, 0.0, A("RM", i, i + 1))
+    ts(A("I64"), A("ID"), -64.0, OP.mult)
+    tt(A("TRI"), A("I64"), A("LL"), OP.subtract)
+    tt(A("LT"), A("BO"), A("LL"), OP.subtract)
+    for h in range(2):
+        tt(A("sH", 128 * h, 128 * h + 128), A("sG", 128 * h, 128 * h + 128), A("BO"), OP.mult)
+    ts(A("IG"), A("sH"), -1000.0, OP.add)
+    ts(A("JG"), A("OW"), 256.0, OP.add)
+    ms(A("thR"), 1000000.0)
+    thW = new("tb", 16)
+    ms(thW, 0.0)
+    ts(A("thR", 1, 257), A("uF"), 33.0 - 1.0 / 128, OP.add)
+    ms(A("z32"), 0.0)
+    ms(A("z256"), 0.0)
+    ms(A("VW", VB + 8192, VB + 8448), 0.0)
+    ms(A("GG"), 0.0)
+    for t in range(NS):
+        ms(A("ST", 256 * t, 256 * t + 256), float(t + 1))
+        ts(A("awI", 16 * t, 16 * t + 16), A("wI"), t, OP.arith_shift_right, 1, OP.bitwise_and)
+        if t < NS - 1:
+            ts(A("WHT", 256 * t, 256 * t + 256), A("WH", 0, 256), (t + 1) / 64.0, OP.add)
+    cp(A("aw"), A("awI"))
+    cur, curU, cur1 = A("OW"), new("tu", 16), A("cur1")
+    cp(curU, A("OW"))
+    ts(cur1, A("OW"), 1.0, OP.add)
+
+    def sums(src, a, n, c, last=False):
+        for z, p in (("ZA", 0), ("ZH", 128)):
+            mm([(A("psPA", p + c, p + c + n // 16), win(z, i), A(src, a + i, a + n, 16)) for i in range(16)], False, last and p > 0)
+
+    def zero():
+        mm([(A("psPA", 0, 256), A("ID"), A("z256"))], True, False)
+
+    def hashes(o):
+        act(A("AGs"), A("psPA", 0, 128))
+        pr, hh = new("ti", 128), new("ti", 128)
+        tt(pr, A("psPA", 128, 256), A("AGs"), OP.mult)
+        ts(part(hh, 0, 16), part(pr, 0, 16), 3, OP.arith_shift_right, 8191, OP.bitwise_and)
+        ts(part(hh, 16, 128), part(pr, 16, 128), 3, OP.arith_shift_right, 1023, OP.bitwise_and)
+        ts(part(hh, 16, 128), part(hh, 16, 128), 1.0, OP.add)
+        for k in range(1, 8):
+            tt(part(hh, 16 * k, 16 * k + 16), part(hh, 16 * k, 16 * k + 16), part(hh, 16 * k - 16, 16 * k), OP.add)
+        ts(o, hh, 8191, OP.bitwise_and)
+
+    def split_cells():
+        lo, x = new("ti", 128), new("tx", 128)
+        ts(lo, cI, 63, OP.bitwise_and)
+        tt(x, cI, lo, OP.subtract)
+        cp(A("CT", 128, 256), lo)
+        act(A("CT", 0, 128), x, AF.Copy, -16384.0)
+
+    def claimed(t):
+        x = new("tx", 128)
+        o = new("tb", 128)
+        ts(st["cl"], A("psM2", 80, 96), float(t + 1), OP.is_equal)
+        rep("psM3", 256, st["cl"])
+        tt(x, A("psM3", 256, 384), st["fm"], OP.mult)
+        tt(o, st["U1"], x, OP.subtract)
+        return o
+
+    def lock(t):
+        x, y, z, l = new("tw", 16), new("tw", 16), new("tw", 16), new("tu", 16)
+        tt(x, st["cf"], A("J16"), OP.subtract)
+        tt(y, x, st["cl"], OP.mult)
+        tt(z, y, A("J16"), OP.add)
+        cp(l, z)
+        act(IND(("TT", 0, 10240), l), A("WHT", 256 * t, 256 * t + 256), AF.Silu)
+
+    st = {}
+    zero()
+    sums("VW", E0, 2048, 0, True)
+    NE = new("ti", 128)
+    hashes(NE)
+    split_cells()
+    dec = None
+
+    for t in range(NS):
+        eb = (E0, E0, E1, E0, E1)[t]
+        lastt = t == NS - 1
+        zero()
+        sums("VW", eb, 1024, 0)
+        if t > 0:
+            Uh = claimed(t - 1)
+        for p in range(2):
+            j = 512 * p
+            tt(A("df", j, j + 512), IND(("VW", VB, VB + 8192), part(cU, 32 * p, 32 * p + 32)), A("VW", eb + j, eb + j + 512), OP.subtract)
+            act(A("gt", j, j + 512), IND(("VW", VB, VB + 8192), part(cU, 64 + 32 * p, 96 + 32 * p)))
+            x = ("psX1", "psD2")[p]
+            mm([(A(x), A("IN"), A("VW", eb + 1024 + j, eb + 1536 + j))], True, False)
+            mm([(A(x), A("ID"), A("gt", j, j + 512))], False, True)
+        for p in range(2):
+            act(A("ad", 512 * p, 512 * p + 512), A("df", 512 * p, 512 * p + 512), AF.Abs)
+        mm([(A("psD1", 0, 64), win("ZB", i), A("ad", i, 1024, 16)) for i in range(16)], True, t == 0)
+        if t > 0:
+            mm([(A("psD1", 16 * k, 16 * k + 16), A("NI"), dec) for k in range(4)], False, True)
+        b1 = new("tx", 64)
+        act(b1, A("psD1", 0, 64))
+        for p in range(2):
+            act(A("ad", 1024 + 512 * p, 1536 + 512 * p), A(("psX1", "psD2")[p]), AF.Abs)
+        mm([(A("psM2", 128, 192), win("ZB", i), A("ad", 1024 + i, 2048, 16)) for i in range(16)], True, t == 0)
+        if t > 0:
+            mm([(A("psM2", 128 + 16 * k, 144 + 16 * k), A("NI"), dec) for k in range(4)], False, True)
+        mm([(A("psM3", 16 * s, 128), A("ID" if s == 0 else "I8"), part(Uh, 0, 128 - 16 * s)) for s in range(8)])
+        mm([(A("psM3", 128, 144), A("ID"), part(Uh, 16 * k, 16 * k + 16)) for k in range(8)])
+        Ft, nf, fm = new("tw", 16), new("tw", 16), new("tb", 128)
+        act(Ft, A("psM3", 128, 144), AF.Copy, 200.5, -30000.0)
+        act(nf, A("psM3", 128, 144), AF.Sign)
+        ts(fm, A("psM3", 0, 128), 1.0, OP.is_equal)
+        m1, m2, m3 = new("tx", 64), new("tx", 32), new("tw", 16)
+        tt(m1, A("psM2", 128, 192), b1, OP.max)
+        tt(m2, part(m1, 0, 32), part(m1, 32, 64), OP.max)
+        tt(m3, part(m2, 0, 16), part(m2, 16, 32), OP.max)
+        f = 32 * t
+        tt(A("FL", f, f + 16), Ft, m3, OP.is_gt)
+        ts(A("FL", f + 16, f + 32), m3, 200.0, OP.is_gt)
+        send(t, "FL", "FR", 32, "f")
+        sums("df", 0, 1024, 0)
+        sums("gt", 0, 1024, 64, True)
+        NG = A("NG", 128 * t, 128 * t + 128)
+        hashes(NG)
+        send(t, "NG", "NR", 128, "n")
+        if lastt:
+            for q in range(16):
+                b = ("psX1", "psPA")[q & 1]
+                mm([(A(b), A("WY"), A("VW", VB + 512 * q, VB + 512 * q + 512))])
+                (act if q % 8 < 5 else cp)(A("YY", 512 * q, 512 * q + 512), A(b))
+        if t > 0:
+            lock(t - 1)
+        cf, cfU, who = new("tw", 16), new("tu", 16), new("tu", 16)
+        fc = A("fc")
+        tt(fc, fm, cI, OP.mult)
+        tt(part(fc, 0, 64), part(fc, 0, 64), part(fc, 64, 128), OP.add)
+        tt(part(fc, 0, 32), part(fc, 0, 32), part(fc, 32, 64), OP.add)
+        tt(cf, part(fc, 0, 16), part(fc, 16, 32), OP.add)
+        cp(cfU, cf)
+        act(A("tau"), IND(("TT", 0, 8192), cfU))
+        act(A("taub"), IND(("tau", 0, 256), curU), AF.Copy, -32.0)
+        act(A("tauL"), IND(("tau", 0, 256), curU))
+        to_w(A("psM2", 96, 112), "taub")
+        cp(who, A("psM2", 96, 112))
+        tt(A("vR"), IND(("thR", 0, 264), who), A("tauL"), OP.is_le)
+        to_w(A("psM2", 112, 128), "vR")
+        cf1, k1, k2, kb = new("tw", 16), new("ti", 16), new("ti", 16), new("tb", 32)
+        act(cf1, cf, AF.Copy, 1.0)
+        tt(k1, cf1, nf, OP.mult)
+        ts(k2, k1, 127, OP.bitwise_and)
+        cp(part(kb, 16, 32), k2)
+        tt(part(kb, 0, 16), k1, k2, OP.subtract)
+        to_r("psM1", 256, [part(kb, 0, 16), part(kb, 16, 32)])
+        act(A("cdR"), A("psM1", 256, 512))
+        act(A("clR"), IND(("cdR", 0, 256), curU))
+        to_w(A("psM3", 160, 176), "clR", "SELF")
+        ts(A("clU"), A("clR"), 0.0, OP.add)
+        if t > 0:
+            x1, x2, o = new("tx", 128), new("tx", 128), new("ti", 128)
+            tt(x1, A("psMK", 384, 512), NG, OP.mult)
+            tt(x2, A("psMK", 256, 384), NE, OP.mult)
+            tt(o, x1, x2, OP.add)
+            NE = o
+            if not lastt:
+                x3, x4, x5, EL = new("tx", 128), new("tx", 128), new("tx", 128), new("tu", 128)
+                ts(x3, cI, 2048.0 if eb == E0 else -16384.0, OP.add)
+                tt(x4, A("psMK", 384, 512), x3, OP.mult)
+                if eb == E0:
+                    tt(x5, x4, A("JE"), OP.max)
+                else:
+                    ts(x3, x4, 16384.0, OP.add)
+                    tt(x5, x3, A("JE9"), OP.min)
+                cp(EL, x5)
+                for p in range(4):
+                    o, w0, w1 = (E1, E0, VB + 8192) if eb == E0 else (E0, VB, E1 + 2048)
+                    act(A("VW", o + 512 * p, o + 512 * p + 512), IND(("VW", w0, w1), part(EL, 32 * p, 32 * p + 32)))
+        aw = A("aw", 16 * t, 16 * t + 16)
+        lc = A("psM3", 160, 176)
+        w = [new("tw", 16) for _ in range(10)]
+        want, stay, home, back = w[2], w[7], w[8], w[9]
+        tt(w[0], A("psM2", 112, 128), aw, OP.mult)
+        tt(w[1], aw, w[0], OP.subtract)
+        tt(want, lc, w[1], OP.mult)
+        act(w[3], lc, AF.Sign)
+        tt(w[4], w[0], w[3], OP.mult)
+        cp(w[5], who)
+        tt(w[6], w[5], cur1, OP.subtract)
+        tt(w[6], w[6], w[4], OP.mult)
+        tt(stay, w[6], cur, OP.add)
+        tt(home, A("OW"), stay, OP.subtract)
+        tt(back, cur, A("JG"), OP.subtract)
+        rdy, cum, ab, cm, dec, keep = [new("tb", 16) for _ in range(6)]
+        tt(rdy, A("FL", f, f + 16), A("FR", f, f + 16), OP.mult)
+        (lambda c, r: op("v", lambda: g.vector.tensor_tensor_scan(c[0], r[0], T.z32[:, 0:16], 0.0, OP.add, OP.add), [c], [r, A("z32")], 64 * CY))(cum, rdy)
+        tt(ab, A("FL", f + 16, f + 32), A("FR", f + 16, f + 32), OP.max)
+        mm([(A("psD2", 64, 80), A("TRI"), rdy), (A("psD2", 64, 80), A("BO"), cum)])
+        ts(cm, A("psD2", 64, 80), -32.0, OP.is_lt)
+        tt(dec, ab, cm, OP.max)
+        mm([(A("psD1", 128, 160), A("ID"), A("z32"))], True, False)
+        for c in range(16):
+            ts(A("XO", 256 * c, 256 * c + 256), A("IG"), A("psD2", 64 + c, 65 + c), OP.is_equal)
+            mm([(A("psD1", 128 + h, 160, 2), A("XO", 256 * c + 128 * h, 256 * c + 128 * h + 128), A("CT", c, 256, 16)) for h in range(2)], False, c == 15)
+        z1, z2, z3, zU = new("tw", 16), new("tw", 16), new("tw", 16), new("tu", 16)
+        act(z1, A("psD1", 144, 160), AF.Copy, 16384.0)
+        tt(z2, A("psD1", 128, 144), z1, OP.add)
+        tt(z3, z2, A("J16"), OP.min)
+        cp(zU, z3)
+        cp(A("CO", 256 * t, 256 * t + 256), IND(("VW", VB, VB + 8448), zU))
+        send(t, "CO", "CR", 256, "c")
+        act(keep, dec, AF.Copy, 1.0, -1.0)
+        for q, s in enumerate((ab, cm, keep, dec)):
+            rep("psMK", 128 * q, s)
+        x1, x2, x3, x4, o, ou, u1 = [new("tx", 128) for _ in range(4)] + [new("ti", 128), new("tu", 128), new("tb", 128)]
+        tt(x1, A("psMK", 0, 128), NE, OP.mult)
+        tt(x2, A("psMK", 128, 256), A("NR", 128 * t, 128 * t + 128), OP.mult)
+        tt(x3, x1, x2, OP.max)
+        tt(x4, A("psMK", 256, 384), cI, OP.mult)
+        tt(o, x3, x4, OP.max)
+        cI = o
+        if not lastt:
+            cU = ou
+            cp(cU, cI)
+            split_cells()
+        tt(u1, A("psMK", 384, 512), Uh, OP.max)
+        to_r("psM1", 0, [dec])
+        act(A("dR"), A("psM1", 0, 256))
+        act(A("gR"), IND(("dR", 0, 256), curU))
+        gone = A("psM2", 32, 48)
+        to_w(gone, "gR")
+        al, ca, wn, hm, nc, ncu = [new("tw", 16) for _ in range(5)] + [new("tu", 16)]
+        act(al, gone, AF.Copy, 1.0, -1.0)
+        tt(ca, want, al, OP.mult)
+        act(wn, ca, AF.Sign)
+        tt(hm, gone, home, OP.mult)
+        tt(nc, hm, stay, OP.add)
+        cur, curU, cur1 = nc, ncu, new("tw", 16)
+        cp(curU, cur)
+        act(cur1, cur, AF.Copy, 1.0)
+        for c in range(16):
+            ts(A("EQ", 272 * c, 256 * c + 256), A("clU", 16 * c, 256), part(ca, c, c + 1), OP.is_equal)
+        mm([(A("psM1", 0, 256), A("LT"), A("EQ", 0, 256)), (A("psM1", 16, 256), A("LL"), A("EQ", 16, 256))], True, False)
+        for c in range(1, 16):
+            l = [(A("psM1", 16 * c + 16, 256), A("BO"), A("EQ", 272 * c + 16, 256 * c + 256))] if c < 15 else []
+            mm(l + [(A("psM1", 16 * c, 16 * c + 16), A("LT"), A("EQ", 272 * c, 272 * c + 16))], False, c == 15)
+        act(A("cnR"), A("psM1", 0, 256))
+        to_w(A("psM2", 64, 80), "cnR")
+        w = [new("tw", 16) for _ in range(4)]
+        gU = new("tu", 16)
+        ts(w[0], A("psM2", 64, 80), 0.0, OP.is_equal)
+        tt(w[1], w[0], wn, OP.mult)
+        tt(w[2], w[1], back, OP.mult)
+        tt(w[3], w[2], A("JG"), OP.add)
+        cp(gU, w[3])
+        cp(IND(("GG", 0, 512), gU), A("ST", 256 * t, 256 * t + 256))
+        to_w(A("psM2", 80, 96), "GG")
+        st = {"cl": new("tb", 16), "cf": cf, "fm": fm, "U1": u1}
+        if lastt:
+            mm([(A("psD1", 0, 256), A("WY"), A("CR", 256 * t, 256 * t + 256))])
+            act(A("ys8"), A("psD1", 0, 256))
+            cp(A("oc"), cI)
+            ts(A("oh"), claimed(t), -1.0, OP.mult, 1.0, OP.add)
+            cp(IND(("YY", 0, 8448), zU), A("ys8"))
+        else:
+            cp(IND(("VW", VB, VB + 8448), zU), A("CR", 256 * t, 256 * t + 256))
+            x, y = new("tw", 16), new("tb", 16)
+            act(x, dec, AF.Copy, 0.0, (t + 2) / 64.0)
+            tt(y, thW, x, OP.max)
+            thW = y
+            to_r("psM1", 256, [A("OWb"), thW])
+            act(A("thR", 1, 257), A("psM1", 256, 512), AF.Copy, 32.0 - 1.0 / 128)
+    for sem, tout, o in (("oc_", T.yc[:], A("oc")), ("ol_", T.yl[:], cur), ("oh_", T.yh[:], A("oh"))):
+        (lambda sem, tout, o: op("y", lambda: g.sync.dma_start(tout, o[0]), [], [o], 0.1, sem, 16, 2.5))(sem, tout, o)
+    yo = (T.YY[0:128:16, 0:8192], (("YY", 0, 8192),), 8192, False, "sb")
+    op("y", lambda: g.sync.dma_start(T.ys[:], yo[0]), [], [yo], 0.1, "oy_", 16, 2.5)
+
+    n = len(ops)
+    deps = [set() for _ in range(n)]
+    log = {}
+    for i, o in enumerate(ops):
+        for w, acc in ((False, o["rd"]), (True, o["wr"])):
+            for name, a, b in acc:
+                ps = name[:2] == "ps"
+                for a2, b2, w2, k in log.get(name, []):
+                    if k != i and ((ps and (ops[k]["e"] != o["e"] or o["e"] == "t")) or (a < b2 and a2 < b and (w or w2))):
+                        deps[i].add(k)
+        for w, acc in ((False, o["rd"]), (True, o["wr"])):
+            for name, a, b in acc:
+                old = log.get(name, [])
+                if w:
+                    old = [r for r in old if not (a <= r[0] and r[1] <= b)]
+                log[name] = old + [(a, b, w, i)]
+        if "send" in o:
+            deps[i].add(o["send"])
+    succ = [[] for _ in range(n)]
+    for i in range(n):
+        for k in deps[i]:
+            succ[k].append(i)
+    lat = [(o["arr"] if o["arr"] is not None else 0.13) for o in ops]
+    prio = [0.0] * n
+    for i in range(n - 1, -1, -1):
+        prio[i] = ops[i]["cost"] + max([lat[i] + prio[k] if ops[k]["e"] != ops[i]["e"] or ops[i]["e"] != "t" else prio[k] for k in succ[i]] + [0.0])
+    for i in range(n):
+        if "load" in ops[i]:
+            prio[i] = 1e6 - i
+    left = [len(d) for d in deps]
+    ready = {}
+    rt = [0.0] * n
+    for i in range(n):
+        if not left[i]:
+            ready.setdefault(ops[i]["e"], []).append(i)
+    free = {e: 0.0 for e in "vstgya"}
+    order = []
+    while len(order) < n:
+        best = None
+        for e, l in ready.items():
+            if not l:
+                continue
+            t0 = max(free[e], min(rt[i] for i in l))
+            if best is None or t0 < best[0]:
+                best = (t0, e)
+        t0, e = best
+        i = max([i for i in ready[e] if rt[i] <= t0 + 1e-9], key=lambda i: (prio[i], -i))
+        ready[e].remove(i)
+        order.append(i)
+        if e != "a":
+            free[e] = t0 + ops[i]["cost"]
+        for k in succ[i]:
+            d = 0.0 if ops[i]["e"] == ops[k]["e"] == "t" else 0.0 if ops[i]["e"] == "g" and ops[k]["e"] == "a" else lat[i]
+            rt[k] = max(rt[k], t0 + ops[i]["cost"] + d)
+            left[k] -= 1
+            if not left[k]:
+                ready.setdefault(ops[k]["e"], []).append(k)
+
+    cnt = {}
+    known = {e: {} for e in "vstgya"}
+    clocks = {}
+    log = {}
+
+    def waits(e, acc, w):
+        own = esem.get(e)
+        for name, a, b in acc:
+            ps = name[:2] == "ps"
+            for a2, b2, w2, sem, m in log.get(name, []):
+                ov = a < b2 and a2 < b
+                if (ov and w2 and (e != "t" or not w)) if sem == own else (ps or (ov and (w or w2))):
+                    if known[e].get(sem, 0) < m:
+                        eng[e].wait_ge(T.sem[sem], m)
+                        for q, v in list(clocks[(sem, m)].items()):
+                            known[e][q] = max(known[e].get(q, 0), v)
+
+    def note(sem, m, acc, w):
+        for name, a, b in acc:
+            ps = name[:2] == "ps"
+            log[name] = [r for r in log.get(name, []) if not ((w and a <= r[0] and r[1] <= b) or (ps and r[3] != sem)
+                                                              or (r[3] == sem and r[2] == w and a <= r[0] and r[1] <= b))] + [(a, b, w, sem, m)]
+
+    for i in order:
+        o = ops[i]
+        e, sem = o["e"], o["sem"]
+        m = cnt[sem] = cnt.get(sem, 0) + o["inc"]
+        if e == "a":
+            clocks[(sem, m)] = {sem: m}
+            note(sem, m, o["wr"], True)
+            continue
+        if o["mm"] is None:
+            waits(e, o["rd"], False)
+            waits(e, o["wr"], True)
+            x = o["call"]()
+            if sem != "lsem":
+                x.then_inc(T.sem[sem], o["inc"])
+        else:
+            lst, first, last = o["mm"]
+            runs = lst if isinstance(lst[0], list) else [lst]
+            for run in runs:
+                for q, (po, pl, pr) in enumerate(run):
+                    waits(e, pl[1] + pr[1], False)
+                    waits(e, po[1], True)
+                    x = g.tensor.matmul(po[0], pl[0], pr[0], first and q == 0, last and q == len(run) - 1)
+            x.then_inc(T.sem.st, 1)
+        if sem == "lsem":
+            continue
+        clocks[(sem, m)] = dict(known[e])
+        clocks[(sem, m)][sem] = m
+        note(sem, m, o["rd"], False)
+        note(sem, m, o["wr"], True)
+    for s in ("oc_", "ol_", "oh_", "oy_"):
+        g.sync.wait_ge(T.sem[s], 16)
+    g.wait_ge(T.sem.lsem, nsent[0])
+    for s in ("sv", "ss", "st", "sg"):
+        g.wait_ge(T.sem[s], cnt[s])

@@ -1,8 +1,10 @@
 from concourse.mybir import AluOpType as OP, ActivationFunctionType as AF
 
 NS = 5
-E0, VB, E1 = 0, 2048, 10496
+EA, GT, EB = 0, 2048, 4096
 F, B, I, U16 = "float32", "bfloat16", "int32", "uint16"
+BASE, HELD = 131072.0, 262144.0
+BIG = 2.0 ** 95
 SCRATCH = {}
 
 
@@ -11,45 +13,51 @@ def _buf(names, n, d):
         SCRATCH[x] = ("sbuf", [128, n], d)
 
 
-_buf("VW", 12544, B)
-_buf("TT", 10240, F)
-_buf("YY", 8448, F)
-_buf("ad SEL WR", 2048, B)
-_buf("df gt", 1024, B)
-_buf("XO EQ", 4096, B)
-_buf("SELF WH", 2048, F)
-_buf("pI rI gI", 1, I)
-_buf("pF rF gF g15 lo8 r1", 1, F)
-_buf("uF sG sH ys8 tau tauL cdR clR", 256, F)
-_buf("mI mG hI", 128, I)
-_buf("ZB ZA ZH", 144, B)
-_buf("BO ID IN I8 NI LL TRI LT WY I64", 128, B)
-_buf("RM OW J16 JG cur1", 16, F)
-_buf("IG CT z256 taub vR dR gR cnR", 256, B)
-_buf("JE JE8 JE9 AGs oc oh fc", 128, F)
-_buf("WHT", 1024, F)
-_buf("thR", 264, F)
-_buf("ST", 1280, B)
-_buf("aw", 80, F)
-_buf("awI", 80, I)
+_buf("VW", 8448, B)
+_buf("EW", 6144, B)
+_buf("TT YY", 8448, F)
+_buf("ad WR LO", 2048, B)
+_buf("Z2", 16 * 144, B)
+_buf("EQ", 4096, B)
+_buf("pI rI gI kI sI bI", 1, I)
+_buf("pF rF gF g15 g7 lo8 hi8 r1 kF sF bF gx c1 c2", 1, F)
+_buf("uF CK ys8 u16F u2F", 256, F)
+_buf("mI mG cI hI", 128, I)
+_buf("ZB ZA ZH ZW ZC", 144, B)
+_buf("BO ID IN LL TRI WY HI IG wr", 128, B)
+_buf("DL DH JO POS M01 RS HS AGs oc oh iA iB", 128, F)
+_buf("DW", 240, B)
+_buf("GI", 8, B)
+_buf("RM OW J16 o8 o64 wT ol", 16, F)
+_buf("K1 Kr", 16, B)
+_buf("MX NM A16 RO vX Er tau vR cdR yR", 256, B)
+_buf("SL", 768, F)
+_buf("SLd P01", 32, F)
+_buf("WHT", 256 * NS, F)
+_buf("thR", 272, B)
+_buf("aw8 naw ct wa", 16 * NS, F)
+_buf("awI", 16 * NS, I)
 _buf("z32", 32, B)
-_buf("OWb", 16, B)
 _buf("wI", 16, I)
-_buf("clU", 256, U16)
-_buf("GG", 512, B)
-_buf("tw", 2200, F)
-_buf("tx", 3400, F)
-_buf("ti", 3000, I)
-_buf("tb", 2400, B)
-_buf("tu", 1400, U16)
-_buf("FL FR", 32 * NS, B)
-_buf("NG NR", 128 * NS, I)
+_buf("cfR", 256, U16)
+_buf("PI PO", 8, U16)
+_buf("X1 X2", 16, U16)
+_buf("YT", 512, F)
+_buf("tw", 3600, F)
+_buf("tx", 2000, F)
+_buf("ti", 4200, I)
+_buf("tb", 3000, B)
+_buf("tu", 1800, U16)
+_buf("FL FR BL BR", 16 * NS, B)
+_buf("NG NR", 128 * NS, F)
 _buf("CO CR", 256 * NS, B)
-for _n in ("D1", "D2", "PA", "X1", "MK", "M1", "M2", "M3"):
+for _n in ("X1", "X2", "D", "S", "MK", "M1", "M2", "V"):
     SCRATCH["ps" + _n] = ("psum", [128, 512], F)
 LOADS = ["dcs", "dho", "dwk", "dsn", "dx"]
-SEMAPHORES = ["sv", "ss", "st", "sg", "lsem", "oc_", "oh_", "ol_", "oy_"] + LOADS + [k + str(t) for k in "fnc" for t in range(NS)]
-CY = 0.00083 * 1.15
+SEMAPHORES = ["sv", "ss", "st", "sg", "lsem", "oc_", "oh_", "ol_", "oy_", "yt_"] + LOADS + [k + str(t) for k in "fbnc" for t in range(NS)]
+CY, PE = 0.00083 * 1.15, 0.00042 * 1.15
+WAKE = 0.12
+JENG = ("svsv", "svsv", "svsv", "svsv", "svsv")
 
 
 def rank_program(g, core, T, topo):
@@ -66,13 +74,13 @@ def rank_program(g, core, T, topo):
                 SCRATCH[name][2] in (B, U16), "ps" if name[:2] == "ps" else "sb")
 
     def IND(w, off):
-        wn, a, b = w
+        wn, a, b = w[1][0]
         on, c, d = off[1][0]
         return T[wn][:, a:b].indirect(off[0]), ((wn, a, b), (on, c, d)), 16 * (d - c), SCRATCH[wn][2] == B, "ind"
 
-    def part(o, a, b):
+    def part(o, a, b, step=1):
         name, s, _e = o[1][0]
-        return A(name, s + a, s + b)
+        return A(name, s + a, s + b, step)
 
     def op(e, call, outs, ins, cost, sem=None, inc=1, arr=None):
         rd = [x for o in ins for x in o[1]]
@@ -91,88 +99,90 @@ def rank_program(g, core, T, topo):
 
     def tt(o, a, b, f):
         op("v", lambda: g.vector.tensor_tensor(o[0], a[0], b[0], f), [o], [a, b], vcost(o, [a, b], b[2], True))
+        return o
 
     def ts(o, a, s1, f1, s2=None, f2=None):
-        col = [s1] if isinstance(s1, tuple) else []
-        x1 = s1[0] if col else s1
+        col = [s for s in (s1, s2) if isinstance(s, tuple)]
+        x1, x2 = [s[0] if isinstance(s, tuple) else s for s in (s1, s2)]
         if f2 is None:
             op("v", lambda: g.vector.tensor_scalar(o[0], a[0], x1, None, f1), [o], [a] + col, vcost(o, [a], a[2]))
         else:
-            op("v", lambda: g.vector.tensor_scalar(o[0], a[0], x1, s2, f1, f2), [o], [a] + col, vcost(o, [a], a[2]))
+            op("v", lambda: g.vector.tensor_scalar(o[0], a[0], x1, x2, f1, f2), [o], [a] + col, vcost(o, [a], a[2]))
+        return o
 
     def cp(o, a):
         op("v", lambda: g.vector.tensor_copy(o[0], a[0]), [o], [a], vcost(o, [a], a[2]))
+        return o
+
+    def scan(o, a, b, init, f0, f1):
+        op("v", lambda: g.vector.tensor_tensor_scan(o[0], a[0], b[0], init, f0, f1), [o], [a, b], max(64, a[2]) * CY)
+        return o
 
     def ms(o, v):
         op("v", lambda: g.vector.memset(o[0], v), [o], [], max(64, o[2] * (0.5 if o[3] else 1)) * CY)
+        return o
 
     def act(o, a, func=AF.Copy, bias=0.0, scale=1.0):
         c = 0.065 + a[2] * (3.0 if o[4] == "ind" else 1.5) * CY if "ind" in (o[4], a[4]) else max(64, a[2]) * CY
-        col = [scale] if isinstance(scale, tuple) else []
-        x = scale[0] if col else scale
-        if not col and bias == 0.0 and scale == 1.0:
+        if bias == 0.0 and scale == 1.0:
             op("s", lambda: g.scalar.activation(o[0], a[0], func), [o], [a], c)
         else:
-            op("s", lambda: g.scalar.activation(o[0], a[0], func, bias=bias, scale=x), [o], [a] + col, c)
+            op("s", lambda: g.scalar.activation(o[0], a[0], func, bias=bias, scale=scale), [o], [a], c)
+        return o
 
-    def mm(lst, first=True, last=True):
-        c = sum(max(64, x[2][2]) * (1 if x[1][3] else 4) for x in lst) * 0.00042 * 1.15
-        op("t", None, [x[0] for x in lst], [y for x in lst for y in x[1:]], c)
+    def mm(lst, first=True, last=True, whole=None):
+        c = sum(max(64, x[2][2]) * (1 if x[1][3] else 4) for x in lst) * PE
+        op("t", None, [whole] if whole else [x[0] for x in lst], [y for x in lst for y in x[1:]], c)
         ops[-1]["mm"] = (lst, first, last)
 
     def win(z, i):
         return A(z, 15 - i, 143 - i)
 
-    def to_w(o, src, sel="SEL"):
-        n = 2 if sel == "SELF" else 16
-        for j in range(0, 16, n):
-            mm([(o, A(sel, 128 * i, 128 * i + 128), A(src, i, 256, 16)) for i in range(j, j + n)], j == 0, j + n == 16)
+    def to_w(o, src, z):
+        mm([(o, win(z, i), part(src, i, src[2], 16)) for i in range(16)])
 
-    def to_r(on, a, srcs):
-        lst = []
-        for i in range(16):
-            lst.append([(A(on, a + i, a + 256, 16), A("WR", 128 * i, 128 * i + 128), s) for s in srcs])
-        op("t", None, [A(on, a, a + 256)], [A("WR")] + srcs, 16 * len(srcs) * 64 * 0.00042 * 1.15)
-        ops[-1]["mm"] = (lst, True, True)
+    def to_r(on, srcs):
+        n = 16 * srcs[0][2]
+        mm([(A(on, i, n, 16), A("WR", 128 * i, 128 * i + 128), s) for i in range(16) for s in srcs], whole=A(on, 0, n))
 
-    def rep(on, a, src):
-        op("t", None, [A(on, a, a + 128)], [A("ID"), src], 8 * 64 * 0.00042 * 1.15)
-        ops[-1]["mm"] = ([[(A(on, a + 16 * k, a + 16 * k + 16), A("ID"), src)] for k in range(8)], True, True)
+    def rep(on, a, m, src, times):
+        n = times * src[2]
+        mm([(A(on, a + k, a + n, times), A(m), src) for k in range(times)], whole=A(on, a, a + n))
 
     def load(e, sem, o, tin):
-        op(e, lambda: eng[e].dma_start(o[0], tin), [o], [], 0.1, sem, 16, 2.5 + o[2] * (2 if o[3] else 4) * 128 / 200e3)
+        op(e, lambda: eng[e].dma_start(o[0], tin), [o], [], 0.1, sem, 16, 2.5 + o[2] * (2 if o[3] else 4) * 128 / 170e3)
         ops[-1]["load"] = True
 
     twins = [T.cores[rank ^ (1 + t % 3)] for t in range(NS)]
-    narr = [len(topo.engines(d, core)[:8]) for d in twins]
     nsent = [0]
 
-    def send(t, sb, rb, w, key):
+    def send(t, s, rb, key):
         dst = twins[t]
         rid, pid, _se = topo.addr(dst)
-        es = topo.engines(core, dst)[:8]
-        s, r = A(sb, w * t, w * t + w), A(rb, w * t, w * t + w)
+        es = topo.engines(core, dst)
+        w = s[2]
+        r = A(rb, w * t, w * t + w)
         op("g", lambda: g.remote_dma(out_ap=r[0], in_ap=s[0], remote_sem=T.sem[key + str(t)], local_sem=T.sem.lsem, pid=pid, routing_id=rid,
                                      dma_engine_mask=sum(1 << x for x in es)), [], [s], 0.8, "lsem", len(es))
-        op("a", None, [(None, ((rb, w * t, w * t + w),))], [s], 0.0, key + str(t), narr[t], 2.0 + w / 256.0)
+        op("a", None, [(None, ((rb, w * t, w * t + w),))], [s], 0.0, key + str(t), len(topo.engines(dst, core)), 2.4 + w / 400.0)
         ops[-1]["send"] = len(ops) - 2
         nsent[0] += len(es)
+        return r
 
-    tops = {"tw": 0, "tx": 0, "ti": 0, "tb": 0, "tu": 0}
+    tops = {"tw": 0, "tx": 0, "ti": 0, "tb": 0, "tu": 0, "psV": 0}
 
-    def new(k, n):
+    def new(k, n=16):
         a = tops[k]
         if a + n > SCRATCH[k][1][1]:
             a = 0
         tops[k] = a + (n + 15) // 16 * 16
         return A(k, a, a + n)
 
-    cI, cU = new("ti", 128), new("tu", 128)
-    load("s", "dcs", cI, T.cs[:])
-    load("s", "dho", A("hI"), T.hold[:])
-    load("y", "dsn", A("VW", E0, E0 + 2048), T.snap[:])
-    load("y", "dx", A("VW", VB, VB + 8192), T.x[:])
+    load("s", "dcs", A("cI"), T.cs[:])
     load("s", "dwk", A("wI"), T.wake[:])
+    load("y", "dho", A("hI"), T.hold[:])
+    load("y", "dsn", A("EW", EB, EB + 2048), T.snap[:])
+    load("y", "dx", A("VW", 0, 8192), T.x[:])
 
     def iota(o, pattern, base, cm, flag=True):
         c = 0.13 + 2 * o[2] * CY
@@ -183,320 +193,291 @@ def rank_program(g, core, T, topo):
     iota(A("pI"), [[1, 1]], 0, 1, False)
     iota(A("uF"), [[1, 256]], 0, 0)
     iota(A("mI"), [[1, 128]], 0, 0, False)
-    iota(A("JE"), [[16, 128]], 0, 0)
-    iota(A("sG"), [[16, 2], [0, 8], [1, 16]], 936, 0)
-    iota(A("WH"), [[0, 8], [1, 256]], 33, 0)
-    ms(A("TT", 0, 4096), 0.0)
-    ts(A("rI"), A("pI"), 15, OP.bitwise_and)
-    ts(A("gI"), A("pI"), 112, OP.bitwise_and)
-    ts(A("mG"), A("mI"), 112, OP.bitwise_and)
+    iota(A("iA"), [[16, 16], [256, 8]], 0, 0)
+    iota(A("iB"), [[0, 8], [16, 16]], 8192, 0)
+    iota(A("M01"), [[0, 16], [1, 8]], 0, 0)
+    iota(A("u16F"), [[0, 16], [1, 16]], 0, 0)
+    iota(A("u2F"), [[0, 16], [16, 8], [0, 2]], 0, 0)
+    iota(A("P01"), [[0, 16], [1, 2]], 0, 0)
+    iota(A("TT", 6144, 8448), [[0, 2304]], 0, 0)
+    ms(A("TT", 0, 2048), 0.0)
+    for q in (1, 2):
+        act(A("TT", 2048 * q, 2048 * q + 2048), A("TT", 0, 2048))
+    for a, m in (("r", 15), ("g", 112), ("k", 7), ("s", 8), ("b", 1)):
+        ts(A(a + "I"), A("pI"), m, OP.bitwise_and)
+        cp(A(a + "F"), A(a + "I"))
     cp(A("pF"), A("pI"))
-    cp(A("rF"), A("rI"))
-    cp(A("gF"), A("gI"))
+    ts(A("mG"), A("mI"), 112, OP.bitwise_and)
     ts(A("g15"), A("gF"), 15.0, OP.add)
+    ts(A("g7"), A("gF"), 7.0, OP.add)
+    ts(A("gx"), A("gF"), 1.0 / 16, OP.mult)
     ts(A("lo8"), A("rF"), 8.0, OP.is_lt)
+    ts(A("hi8"), A("rF"), 8.0, OP.is_ge)
     ts(A("r1"), A("rF"), 1.0, OP.add)
-    ts(A("JE"), A("JE"), A("rF"), OP.add)
-    cp(A("OW"), A("JE", 0, 16))
-    ts(A("OWb"), A("OW"), 1.0, OP.add)
-    ts(A("J16"), A("JE", 0, 16), 8192.0, OP.add)
-    ts(A("JE8"), A("JE"), 8192.0, OP.add)
-    ts(A("JE9"), A("JE"), 8448.0, OP.add)
-    for q in range(4):
-        act(A("TT", 4096 + 1024 * q, 5120 + 1024 * q), A("TT", 1024 * q, 1024 * q + 1024))
-    x1, x2, x3, tl = new("tx", 128), new("tx", 128), new("tx", 128), new("tu", 128)
-    tt(x1, cI, A("JE8"), OP.subtract)
-    tt(x2, x1, A("hI"), OP.mult)
-    tt(x3, x2, A("JE8"), OP.add)
-    cp(tl, x3)
-    act(IND(("TT", 0, 10240), tl), A("WH"), AF.Silu)
-    cp(cU, cI)
-    Uh = new("tb", 128)
-    ts(Uh, A("hI"), -1.0, OP.mult, 1.0, OP.add)
+    ts(A("JO"), A("iB"), A("rF"), OP.add)
+    ts(A("J16"), A("JO", 0, 16), 0.0, OP.add)
+    ts(A("OW"), A("JO", 0, 16), -8192.0, OP.add)
+    ts(A("o8"), A("OW"), 8.0, OP.mult, 8.0, OP.add)
+    ts(A("o64"), A("OW"), 64.0, OP.mult, 64.0, OP.add)
+    ts(A("K1"), A("iB", 0, 16), 256.0 - 8192.0, OP.add)
+    ts(A("Kr"), A("uF", 0, 16), 0.0, OP.mult, A("rF"), OP.add)
+    SP = ts(new("tu", 128), A("iA"), A("rF"), OP.add)
+    ts(A("POS"), A("uF", 0, 128), 16.0, OP.mult, A("rF"), OP.add)
+    ts(A("POS"), A("POS"), 1.0 / 2048, OP.mult)
+    ts(A("c1"), A("kF"), 16.0, OP.mult, A("hi8"), OP.add)
+    ts(A("PI"), A("uF", 0, 8), 2.0, OP.mult, A("c1"), OP.add)
+    ts(A("c2"), A("rF"), 8.0, OP.mult)
+    ts(A("PO"), A("uF", 0, 8), A("c2"), OP.add)
+    c3 = ts(new("tw", 1), A("bF"), 16.0, OP.mult)
+    ts(A("X1"), A("uF", 0, 16), c3, OP.add)
+    ts(A("X2"), A("uF", 0, 16), 2.0, OP.mult, 1.0, OP.add)
+    ts(A("M01"), A("M01"), 0.0, OP.is_gt)
+    ts(A("RS"), A("M01"), -16384.0 - 8388608.0, OP.mult, 8388608.0, OP.add)
+    ts(A("HS"), A("M01"), 8388608.0, OP.mult, BASE, OP.add)
     ts(A("ZB"), A("uF", 0, 144), A("g15"), OP.is_equal)
     ts(A("ZA"), A("ZB"), A("lo8"), OP.mult)
-    tt(A("ZH"), A("ZB"), A("ZA"), OP.subtract)
+    ts(A("ZH"), A("ZB"), A("hi8"), OP.mult)
+    ts(A("ZW"), A("ZB"), A("r1"), OP.mult)
+    zc = ts(new("tb", 144), A("uF", 0, 144), A("g7"), OP.is_equal)
+    tt(A("ZC"), zc, A("ZB"), OP.add)
     ts(A("BO"), A("mG"), A("gF"), OP.is_equal)
     op("g", lambda: g.affine_select(T.LL[:], T.BO[:], [[-1, 128]], OP.is_ge, 0.0, 0, 1), [A("LL")], [A("BO")], 0.4)
     ts(A("ID"), A("uF", 0, 128), A("pF"), OP.is_equal)
-    ts(A("I8"), A("ID"), 8.0, OP.mult)
     ts(A("IN"), A("ID"), -1.0, OP.mult)
-    ts(A("NI"), A("ID"), -4096.0, OP.mult)
+    ts(A("HI"), A("ID"), HELD, OP.mult)
+    ts(A("DL"), A("ID"), A("lo8"), OP.mult)
+    ts(A("DH"), A("ID"), A("hi8"), OP.mult)
+    dr = ts(new("tb", 128), A("IN"), A("rF"), OP.mult)
+    tt(A("TRI"), dr, A("LL"), OP.subtract)
     ts(A("RM"), A("uF", 0, 16), A("rF"), OP.is_equal)
     ts(A("WY"), A("BO"), A("r1"), OP.mult)
     for i in range(16):
         ts(A("WR", 128 * i, 128 * i + 128), A("BO"), A("RM", i, i + 1), OP.mult)
-        ts(A("SEL", 128 * i, 128 * i + 128), A("ID"), A("RM", i, i + 1), OP.mult)
-        act(A("SELF", 128 * i, 128 * i + 128), A("ID"), AF.Copy, 0.0, A("RM", i, i + 1))
-    ts(A("I64"), A("ID"), -64.0, OP.mult)
-    tt(A("TRI"), A("I64"), A("LL"), OP.subtract)
-    tt(A("LT"), A("BO"), A("LL"), OP.subtract)
-    for h in range(2):
-        tt(A("sH", 128 * h, 128 * h + 128), A("sG", 128 * h, 128 * h + 128), A("BO"), OP.mult)
-    ts(A("IG"), A("sH"), -1000.0, OP.add)
-    ts(A("JG"), A("OW"), 256.0, OP.add)
-    ms(A("thR"), 1000000.0)
-    thW = new("tb", 16)
-    ms(thW, 0.0)
-    ts(A("thR", 1, 257), A("uF"), 33.0 - 1.0 / 128, OP.add)
+        ts(A("Z2", 144 * i, 144 * i + 136), A("ZC", 0, 136), A("RM", i, i + 1), OP.mult)
+    c4 = ts(new("tw", 1), A("rF"), 112.0, OP.add)
+    ts(A("DW"), A("uF", 0, 240), c4, OP.is_equal, -2.0, OP.mult)
+    ts(A("GI"), A("uF", 0, 8), A("gx"), OP.is_equal)
+    ts(A("MX"), A("u2F"), A("gF"), OP.is_equal)
+    ts(A("NM"), A("u16F"), A("rF"), OP.not_equal, -9e29, OP.mult)
+    ts(A("A16"), A("u16F"), 16.0, OP.mult)
+    ig = ts(new("tx", 128), A("u16F", 0, 128), 1.0, OP.add)
+    ig2 = tt(new("tx", 128), ig, A("BO"), OP.mult)
+    ts(A("IG"), ig2, -1.0, OP.add)
+    c5 = ts(new("tw", 1), A("kF"), 32.0, OP.mult, 8192.0 + 64.0, OP.add)
+    ts(A("SLd"), A("uF", 0, 32), c5, OP.add)
     ms(A("z32"), 0.0)
-    ms(A("z256"), 0.0)
-    ms(A("VW", VB + 8192, VB + 8448), 0.0)
-    ms(A("GG"), 0.0)
+    ms(A("thR"), -0.5)
+    ms(A("thR", 0, 1), 1000.0)
+    ms(A("VW", 8192, 8448), 0.0)
+    c6, c7 = ms(new("tx", 128), 0.4), ms(new("tx", 128), 0.0)
+    scan(A("wr"), c6, c7, 2.0 ** 85, OP.mult, OP.add)
+    mm([(A("psM2", 0, 8), win("ZA", i), A("wr", i, 128, 16)) for i in range(16)])
+    for h in range(2):
+        cp(A("wT", 8 * h, 8 * h + 8), A("psM2", 0, 8))
     for t in range(NS):
-        ms(A("ST", 256 * t, 256 * t + 256), float(t + 1))
-        ts(A("awI", 16 * t, 16 * t + 16), A("wI"), t, OP.arith_shift_right, 1, OP.bitwise_and)
-        if t < NS - 1:
-            ts(A("WHT", 256 * t, 256 * t + 256), A("WH", 0, 256), (t + 1) / 64.0, OP.add)
-    cp(A("aw"), A("awI"))
-    cur, curU, cur1 = A("OW"), new("tu", 16), A("cur1")
-    cp(curU, A("OW"))
-    ts(cur1, A("OW"), 1.0, OP.add)
+        s = (16 * t, 16 * t + 16)
+        ts(A("awI", *s), A("wI"), t, OP.arith_shift_right, 1, OP.bitwise_and)
+        c8 = ts(new("tw", 1), A("hi8"), t - 1.0, OP.mult, 33.0, OP.add)
+        ts(A("WHT", 256 * t, 256 * t + 256), A("uF"), A("lo8"), OP.mult, c8, OP.add)
+    ts(A("aw8"), A("awI"), 0.125, OP.mult)
+    ts(A("naw"), A("awI"), -1.0, OP.mult, 1.0, OP.add)
+    o1 = ts(new("tw"), A("OW"), 1.0, OP.add)
+    for t in range(NS):
+        s = (16 * t, 16 * t + 16)
+        tt(A("ct", *s), A("naw", *s), o1, OP.subtract)
+        tt(A("wa", *s), A("awI", *s), A("wT"), OP.mult)
 
-    def sums(src, a, n, c, last=False):
-        for z, p in (("ZA", 0), ("ZH", 128)):
-            mm([(A("psPA", p + c, p + c + n // 16), win(z, i), A(src, a + i, a + n, 16)) for i in range(16)], False, last and p > 0)
+    x = ts(new("tx", 128), IND(A("hI"), A("PI")), HELD, OP.mult, BASE, OP.add)
+    KH = tt(new("ti", 128), IND(A("cI"), A("PI")), x, OP.add)
+    cU = cp(new("tu", 128), ts(new("ti", 128), KH, 8191, OP.bitwise_and))
+    un = ts(new("tx", 128), KH, HELD, OP.is_lt)
+    n = cp(new("tw"), part(scan(new("tx", 128), A("M01"), un, 0.0, OP.mult, OP.add), 7, 128, 8))
+    FT = send(0, ts(A("FL", 0, 16), n, 0.0, OP.is_equal), "FR", "f")
+    x = tt(new("tx", 128), A("cI"), A("JO"), OP.subtract)
+    x = tt(new("tx", 128), x, A("hI"), OP.mult)
+    tl = cp(new("tu", 128), tt(new("tx", 128), x, A("JO"), OP.add))
+    for k in range(8):
+        act(IND(A("TT"), part(tl, 16 * k, 16 * k + 16)), A("WHT", 0, 256), AF.Silu)
+    for p in range(4):
+        act(A("EW", EA + 512 * p, EA + 512 * p + 512), IND(A("EW", EB, EB + 2048), part(SP, 32 * p, 32 * p + 32)))
+    chi = cp(new("tb", 128), A("cI"))
+    clo = tt(new("tb", 128), A("cI"), chi, OP.subtract)
+    for i in range(16):
+        mm([(A("psM1", i, 256, 16), A("Z2", 144 * i + 7 - k, 144 * i + 135 - k), part(c, 16 * k, 16 * k + 16)) for k in range(8) for c in (chi, clo)],
+           i == 0, i == 15, A("psM1", 0, 256))
+    act(A("CK"), A("psM1", 0, 256), AF.Copy, 64.0)
+    tW = ms(new("tb"), 0.0)
+    cur = cp(new("ti"), A("OW"))
+    curU = cp(new("tu"), A("OW"))
 
-    def zero():
-        mm([(A("psPA", 0, 256), A("ID"), A("z256"))], True, False)
+    def hashes(src, o):
+        for h in range(2):
+            for z, p in (("ZA", 0), ("ZH", 128)):
+                mm([(A("psS", p + 64 * h, p + 64 * h + 64), win(z, i), A("EW", src + 1024 * h + i, src + 1024 * h + 1024, 16)) for i in range(16)])
+        act(A("AGs"), A("psS", 0, 128))
+        pr = tt(new("ti", 128), A("psS", 128, 256), A("AGs"), OP.mult)
+        h1 = ts(new("ti", 128), pr, 3, OP.arith_shift_right, 1023, OP.bitwise_and)
+        h2 = ts(new("ti", 128), h1, 1.0, OP.add)
+        ts(part(h2, 0, 128, 8), part(pr, 0, 128, 8), 3, OP.arith_shift_right, 8191, OP.bitwise_and)
+        return scan(o, A("HS"), h2, BASE, OP.min, OP.add)
 
-    def hashes(o):
-        act(A("AGs"), A("psPA", 0, 128))
-        pr, hh = new("ti", 128), new("ti", 128)
-        tt(pr, A("psPA", 128, 256), A("AGs"), OP.mult)
-        ts(part(hh, 0, 16), part(pr, 0, 16), 3, OP.arith_shift_right, 8191, OP.bitwise_and)
-        ts(part(hh, 16, 128), part(pr, 16, 128), 3, OP.arith_shift_right, 1023, OP.bitwise_and)
-        ts(part(hh, 16, 128), part(hh, 16, 128), 1.0, OP.add)
-        for k in range(1, 8):
-            tt(part(hh, 16 * k, 16 * k + 16), part(hh, 16 * k, 16 * k + 16), part(hh, 16 * k - 16, 16 * k), OP.add)
-        ts(o, hh, 8191, OP.bitwise_and)
-
-    def split_cells():
-        lo, x = new("ti", 128), new("tx", 128)
-        ts(lo, cI, 63, OP.bitwise_and)
-        tt(x, cI, lo, OP.subtract)
-        cp(A("CT", 128, 256), lo)
-        act(A("CT", 0, 128), x, AF.Copy, -16384.0)
-
-    def claimed(t):
-        x = new("tx", 128)
-        o = new("tb", 128)
-        ts(st["cl"], A("psM2", 80, 96), float(t + 1), OP.is_equal)
-        rep("psM3", 256, st["cl"])
-        tt(x, A("psM3", 256, 384), st["fm"], OP.mult)
-        tt(o, st["U1"], x, OP.subtract)
-        return o
-
-    def lock(t):
-        x, y, z, l = new("tw", 16), new("tw", 16), new("tw", 16), new("tu", 16)
-        tt(x, st["cf"], A("J16"), OP.subtract)
-        tt(y, x, st["cl"], OP.mult)
-        tt(z, y, A("J16"), OP.add)
-        cp(l, z)
-        act(IND(("TT", 0, 10240), l), A("WHT", 256 * t, 256 * t + 256), AF.Silu)
-
-    st = {}
-    zero()
-    sums("VW", E0, 2048, 0, True)
-    NE = new("ti", 128)
-    hashes(NE)
-    split_cells()
-    dec = None
+    NE = hashes(EA, new("tx", 128))
+    NR = {}
+    thB = ms(new("tw"), 200.0)
 
     for t in range(NS):
-        eb = (E0, E0, E1, E0, E1)[t]
+        eb = (EA, EA, EB, EA, EB)[t]
         lastt = t == NS - 1
-        zero()
-        sums("VW", eb, 1024, 0)
-        if t > 0:
-            Uh = claimed(t - 1)
-        for p in range(2):
-            j = 512 * p
-            tt(A("df", j, j + 512), IND(("VW", VB, VB + 8192), part(cU, 32 * p, 32 * p + 32)), A("VW", eb + j, eb + j + 512), OP.subtract)
-            act(A("gt", j, j + 512), IND(("VW", VB, VB + 8192), part(cU, 64 + 32 * p, 96 + 32 * p)))
-            x = ("psX1", "psD2")[p]
-            mm([(A(x), A("IN"), A("VW", eb + 1024 + j, eb + 1536 + j))], True, False)
-            mm([(A(x), A("ID"), A("gt", j, j + 512))], False, True)
-        for p in range(2):
-            act(A("ad", 512 * p, 512 * p + 512), A("df", 512 * p, 512 * p + 512), AF.Abs)
-        mm([(A("psD1", 0, 64), win("ZB", i), A("ad", i, 1024, 16)) for i in range(16)], True, t == 0)
-        if t > 0:
-            mm([(A("psD1", 16 * k, 16 * k + 16), A("NI"), dec) for k in range(4)], False, True)
-        b1 = new("tx", 64)
-        act(b1, A("psD1", 0, 64))
-        for p in range(2):
-            act(A("ad", 1024 + 512 * p, 1536 + 512 * p), A(("psX1", "psD2")[p]), AF.Abs)
-        mm([(A("psM2", 128, 192), win("ZB", i), A("ad", 1024 + i, 2048, 16)) for i in range(16)], True, t == 0)
-        if t > 0:
-            mm([(A("psM2", 128 + 16 * k, 144 + 16 * k), A("NI"), dec) for k in range(4)], False, True)
-        mm([(A("psM3", 16 * s, 128), A("ID" if s == 0 else "I8"), part(Uh, 0, 128 - 16 * s)) for s in range(8)])
-        mm([(A("psM3", 128, 144), A("ID"), part(Uh, 16 * k, 16 * k + 16)) for k in range(8)])
-        Ft, nf, fm = new("tw", 16), new("tw", 16), new("tb", 128)
-        act(Ft, A("psM3", 128, 144), AF.Copy, 200.5, -30000.0)
-        act(nf, A("psM3", 128, 144), AF.Sign)
-        ts(fm, A("psM3", 0, 128), 1.0, OP.is_equal)
-        m1, m2, m3 = new("tx", 64), new("tx", 32), new("tw", 16)
-        tt(m1, A("psM2", 128, 192), b1, OP.max)
-        tt(m2, part(m1, 0, 32), part(m1, 32, 64), OP.max)
-        tt(m3, part(m2, 0, 16), part(m2, 16, 32), OP.max)
-        f = 32 * t
-        tt(A("FL", f, f + 16), Ft, m3, OP.is_gt)
-        ts(A("FL", f + 16, f + 32), m3, 200.0, OP.is_gt)
-        send(t, "FL", "FR", 32, "f")
-        sums("df", 0, 1024, 0)
-        sums("gt", 0, 1024, 64, True)
-        NG = A("NG", 128 * t, 128 * t + 128)
-        hashes(NG)
-        send(t, "NG", "NR", 128, "n")
-        if lastt:
-            for q in range(16):
-                b = ("psX1", "psPA")[q & 1]
-                mm([(A(b), A("WY"), A("VW", VB + 512 * q, VB + 512 * q + 512))])
-                (act if q % 8 < 5 else cp)(A("YY", 512 * q, 512 * q + 512), A(b))
-        if t > 0:
-            lock(t - 1)
-        cf, cfU, who = new("tw", 16), new("tu", 16), new("tu", 16)
-        fc = A("fc")
-        tt(fc, fm, cI, OP.mult)
-        tt(part(fc, 0, 64), part(fc, 0, 64), part(fc, 64, 128), OP.add)
-        tt(part(fc, 0, 32), part(fc, 0, 32), part(fc, 32, 64), OP.add)
-        tt(cf, part(fc, 0, 16), part(fc, 16, 32), OP.add)
-        cp(cfU, cf)
-        act(A("tau"), IND(("TT", 0, 8192), cfU))
-        act(A("taub"), IND(("tau", 0, 256), curU), AF.Copy, -32.0)
-        act(A("tauL"), IND(("tau", 0, 256), curU))
-        to_w(A("psM2", 96, 112), "taub")
-        cp(who, A("psM2", 96, 112))
-        tt(A("vR"), IND(("thR", 0, 264), who), A("tauL"), OP.is_le)
-        to_w(A("psM2", 112, 128), "vR")
-        cf1, k1, k2, kb = new("tw", 16), new("ti", 16), new("ti", 16), new("tb", 32)
-        act(cf1, cf, AF.Copy, 1.0)
-        tt(k1, cf1, nf, OP.mult)
-        ts(k2, k1, 127, OP.bitwise_and)
-        cp(part(kb, 16, 32), k2)
-        tt(part(kb, 0, 16), k1, k2, OP.subtract)
-        to_r("psM1", 256, [part(kb, 0, 16), part(kb, 16, 32)])
-        act(A("cdR"), A("psM1", 256, 512))
-        act(A("clR"), IND(("cdR", 0, 256), curU))
-        to_w(A("psM3", 160, 176), "clR", "SELF")
-        ts(A("clU"), A("clR"), 0.0, OP.add)
-        if t > 0:
-            x1, x2, o = new("tx", 128), new("tx", 128), new("ti", 128)
-            tt(x1, A("psMK", 384, 512), NG, OP.mult)
-            tt(x2, A("psMK", 256, 384), NE, OP.mult)
-            tt(o, x1, x2, OP.add)
-            NE = o
-            if not lastt:
-                x3, x4, x5, EL = new("tx", 128), new("tx", 128), new("tx", 128), new("tu", 128)
-                ts(x3, cI, 2048.0 if eb == E0 else -16384.0, OP.add)
-                tt(x4, A("psMK", 384, 512), x3, OP.mult)
-                if eb == E0:
-                    tt(x5, x4, A("JE"), OP.max)
-                else:
-                    ts(x3, x4, 16384.0, OP.add)
-                    tt(x5, x3, A("JE9"), OP.min)
-                cp(EL, x5)
-                for p in range(4):
-                    o, w0, w1 = (E1, E0, VB + 8192) if eb == E0 else (E0, VB, E1 + 2048)
-                    act(A("VW", o + 512 * p, o + 512 * p + 512), IND(("VW", w0, w1), part(EL, 32 * p, 32 * p + 32)))
-        aw = A("aw", 16 * t, 16 * t + 16)
-        lc = A("psM3", 160, 176)
-        w = [new("tw", 16) for _ in range(10)]
-        want, stay, home, back = w[2], w[7], w[8], w[9]
-        tt(w[0], A("psM2", 112, 128), aw, OP.mult)
-        tt(w[1], aw, w[0], OP.subtract)
-        tt(want, lc, w[1], OP.mult)
-        act(w[3], lc, AF.Sign)
-        tt(w[4], w[0], w[3], OP.mult)
-        cp(w[5], who)
-        tt(w[6], w[5], cur1, OP.subtract)
-        tt(w[6], w[6], w[4], OP.mult)
-        tt(stay, w[6], cur, OP.add)
-        tt(home, A("OW"), stay, OP.subtract)
-        tt(back, cur, A("JG"), OP.subtract)
-        rdy, cum, ab, cm, dec, keep = [new("tb", 16) for _ in range(6)]
-        tt(rdy, A("FL", f, f + 16), A("FR", f, f + 16), OP.mult)
-        (lambda c, r: op("v", lambda: g.vector.tensor_tensor_scan(c[0], r[0], T.z32[:, 0:16], 0.0, OP.add, OP.add), [c], [r, A("z32")], 64 * CY))(cum, rdy)
-        tt(ab, A("FL", f + 16, f + 32), A("FR", f + 16, f + 32), OP.max)
-        mm([(A("psD2", 64, 80), A("TRI"), rdy), (A("psD2", 64, 80), A("BO"), cum)])
-        ts(cm, A("psD2", 64, 80), -32.0, OP.is_lt)
-        tt(dec, ab, cm, OP.max)
-        mm([(A("psD1", 128, 160), A("ID"), A("z32"))], True, False)
-        for c in range(16):
-            ts(A("XO", 256 * c, 256 * c + 256), A("IG"), A("psD2", 64 + c, 65 + c), OP.is_equal)
-            mm([(A("psD1", 128 + h, 160, 2), A("XO", 256 * c + 128 * h, 256 * c + 128 * h + 128), A("CT", c, 256, 16)) for h in range(2)], False, c == 15)
-        z1, z2, z3, zU = new("tw", 16), new("tw", 16), new("tw", 16), new("tu", 16)
-        act(z1, A("psD1", 144, 160), AF.Copy, 16384.0)
-        tt(z2, A("psD1", 128, 144), z1, OP.add)
-        tt(z3, z2, A("J16"), OP.min)
-        cp(zU, z3)
-        cp(A("CO", 256 * t, 256 * t + 256), IND(("VW", VB, VB + 8448), zU))
-        send(t, "CO", "CR", 256, "c")
-        act(keep, dec, AF.Copy, 1.0, -1.0)
-        for q, s in enumerate((ab, cm, keep, dec)):
-            rep("psMK", 128 * q, s)
-        x1, x2, x3, x4, o, ou, u1 = [new("tx", 128) for _ in range(4)] + [new("ti", 128), new("tu", 128), new("tb", 128)]
-        tt(x1, A("psMK", 0, 128), NE, OP.mult)
-        tt(x2, A("psMK", 128, 256), A("NR", 128 * t, 128 * t + 128), OP.mult)
-        tt(x3, x1, x2, OP.max)
-        tt(x4, A("psMK", 256, 384), cI, OP.mult)
-        tt(o, x3, x4, OP.max)
-        cI = o
+        s16 = (16 * t, 16 * t + 16)
+        run = scan(new("ti", 128), A("RS"), KH, 0.0, OP.add, OP.min)
+        cfI = ts(new("ti"), part(run, 7, 128, 8), 8191, OP.bitwise_and)
+        kb = new("tb", 32)
+        cp(part(kb, 0, 16), cfI)
+        tt(part(kb, 16, 32), cfI, part(kb, 0, 16), OP.subtract)
+        cfF, cfU = cp(new("tw"), cfI), cp(new("tu"), cfI)
+        to_r("psM1", [part(kb, 0, 16), part(kb, 16, 32)])
+        cp(A("cfR"), A("psM1", 0, 256))
+        for q in range(16):
+            ts(A("EQ", 256 * q, 256 * q + 256), A("cfR"), part(cfF, q, q + 1), OP.is_equal)
+        fm = tt(new("tb", 128), KH, run, OP.is_le)
+        act(A("tau"), IND(A("TT"), cfU), AF.Copy, -32.0)
+        who8, held8 = A("psM2", 0, 16), A("psM2", 16, 32)
+        to_w(who8, A("tau"), "ZA")
+        whoU = ts(new("tu"), who8, 0.125, OP.mult)
+        d = tt(new("tw"), who8, A("o8"), OP.subtract)
+        tt(A("vR"), IND(A("thR"), whoU), A("tau"), OP.is_le)
+        to_w(held8, A("vR"), "ZH")
+        h1 = ts(new("tw"), held8, 0.125, OP.mult, 1.0, OP.add)
+        nx = tt(new("tw"), tt(new("tw"), held8, d, OP.mult), A("o64"), OP.add)
         if not lastt:
-            cU = ou
-            cp(cU, cI)
-            split_cells()
-        tt(u1, A("psMK", 384, 512), Uh, OP.max)
-        to_r("psM1", 0, [dec])
-        act(A("dR"), A("psM1", 0, 256))
-        act(A("gR"), IND(("dR", 0, 256), curU))
-        gone = A("psM2", 32, 48)
-        to_w(gone, "gR")
-        al, ca, wn, hm, nc, ncu = [new("tw", 16) for _ in range(5)] + [new("tu", 16)]
-        act(al, gone, AF.Copy, 1.0, -1.0)
-        tt(ca, want, al, OP.mult)
-        act(wn, ca, AF.Sign)
-        tt(hm, gone, home, OP.mult)
-        tt(nc, hm, stay, OP.add)
-        cur, curU, cur1 = nc, ncu, new("tw", 16)
-        cp(curU, cur)
-        act(cur1, cur, AF.Copy, 1.0)
-        for c in range(16):
-            ts(A("EQ", 272 * c, 256 * c + 256), A("clU", 16 * c, 256), part(ca, c, c + 1), OP.is_equal)
-        mm([(A("psM1", 0, 256), A("LT"), A("EQ", 0, 256)), (A("psM1", 16, 256), A("LL"), A("EQ", 16, 256))], True, False)
-        for c in range(1, 16):
-            l = [(A("psM1", 16 * c + 16, 256), A("BO"), A("EQ", 272 * c + 16, 256 * c + 256))] if c < 15 else []
-            mm(l + [(A("psM1", 16 * c, 16 * c + 16), A("LT"), A("EQ", 272 * c, 272 * c + 16))], False, c == 15)
-        act(A("cnR"), A("psM1", 0, 256))
-        to_w(A("psM2", 64, 80), "cnR")
-        w = [new("tw", 16) for _ in range(4)]
-        gU = new("tu", 16)
-        ts(w[0], A("psM2", 64, 80), 0.0, OP.is_equal)
-        tt(w[1], w[0], wn, OP.mult)
-        tt(w[2], w[1], back, OP.mult)
-        tt(w[3], w[2], A("JG"), OP.add)
-        cp(gU, w[3])
-        cp(IND(("GG", 0, 512), gU), A("ST", 256 * t, 256 * t + 256))
-        to_w(A("psM2", 80, 96), "GG")
-        st = {"cl": new("tb", 16), "cf": cf, "fm": fm, "U1": u1}
-        if lastt:
-            mm([(A("psD1", 0, 256), A("WY"), A("CR", 256 * t, 256 * t + 256))])
-            act(A("ys8"), A("psD1", 0, 256))
-            cp(A("oc"), cI)
-            ts(A("oh"), claimed(t), -1.0, OP.mult, 1.0, OP.add)
-            cp(IND(("YY", 0, 8448), zU), A("ys8"))
+            tn = tt(new("tw"), n, h1, OP.mult)
+            pre = tt(new("tw"), cfF, A("J16"), OP.subtract)
+        V = new("tb", 32)
+        if t == 0:
+            ms(V, 0.0)
+            cp(part(V, 0, 8), A("wa", 0, 8))
+            ts(part(V, 16, 24), A("wa", 0, 8), 0.0, OP.is_gt, BIG, OP.mult)
+            cp(part(V, 24, 32), A("wa", 8, 16))
         else:
-            cp(IND(("VW", VB, VB + 8448), zU), A("CR", 256 * t, 256 * t + 256))
-            x, y = new("tw", 16), new("tb", 16)
-            act(x, dec, AF.Copy, 0.0, (t + 2) / 64.0)
-            tt(y, thW, x, OP.max)
-            thW = y
-            to_r("psM1", 256, [A("OWb"), thW])
-            act(A("thR", 1, 257), A("psM1", 256, 512), AF.Copy, 32.0 - 1.0 / 128)
-    for sem, tout, o in (("oc_", T.yc[:], A("oc")), ("ol_", T.yl[:], cur), ("oh_", T.yh[:], A("oh"))):
-        (lambda sem, tout, o: op("y", lambda: g.sync.dma_start(tout, o[0]), [], [o], 0.1, sem, 16, 2.5))(sem, tout, o)
-    yo = (T.YY[0:128:16, 0:8192], (("YY", 0, 8192),), 8192, False, "sb")
-    op("y", lambda: g.sync.dma_start(T.ys[:], yo[0]), [], [yo], 0.1, "oy_", 16, 2.5)
+            bi = ts(new("ti"), cur, 15, OP.bitwise_and)
+            bf = cp(new("tw"), bi)
+            a16 = tt(new("tb"), cur, bi, OP.subtract)
+            rep("psM2", 256, "ID", a16, 16)
+            tt(A("RO"), A("psM2", 256, 512), A("A16"), OP.is_equal)
+            for h in range(2):
+                for q in range(8 * h, 8 * h + 8):
+                    ts(A("LO", 128 * q, 128 * q + 128), A("IG"), part(bf, q, q + 1), OP.is_equal, A("wa", 16 * t + q, 16 * t + q + 1), OP.mult)
+                mm([(A("psM2", 32 + 16 * h, 48 + 16 * h), A("LO", 128 * q, 128 * q + 128), A("RO", 16 * q, 16 * q + 16)) for q in range(8 * h, 8 * h + 8)])
+            cp(part(V, 0, 16), A("psM2", 32, 48))
+            tt(part(V, 16, 32), A("psM2", 48, 64), ts(new("tw"), A("psM2", 32, 48), 0.0, OP.is_gt, BIG, OP.mult), OP.max)
+        b0 = tt(new("tw"), tt(new("tw"), A("naw", *s16), cur, OP.mult), A("ct", *s16), OP.add)
+        for p in range(4):
+            j = 512 * p
+            gt, x = A("EW", GT + j, GT + j + 512), A(("psX1", "psX2")[p & 1])
+            (act if JENG[t][p] == "s" else cp)(gt, IND(A("VW", 0, 8192), part(cU, 32 * p, 32 * p + 32)))
+            mm([(x, A("IN"), A("EW", eb + j, eb + j + 512))], True, False)
+            mm([(x, A("ID"), gt)], False, True)
+            act(A("ad", j, j + 512), x, AF.Abs)
+            if p & 1:
+                mm([(A("psD", 32 * p - 32, 32 * p + 32), win("ZB", i), A("ad", j - 512 + i, j + 512, 16)) for i in range(16)])
+        md = scan(new("tx", 128), A("M01"), A("psD", 0, 128), 0.0, OP.mult, OP.max)
+        bad = tt(A("BL", *s16), part(md, 7, 128, 8), thB, OP.is_gt)
+        badT = send(t, bad, "BR", "b")
+        X = hashes(GT, A("NG", 128 * t, 128 * t + 128))
+        for u in ((0, 1), (2,), (3,), (4,), ())[t]:
+            NR[u] = send(u, X, "NR", "n")
+        if t > 0:
+            x = tt(new("psV", 128), A("psMK", 256, 384), NE, OP.mult)
+            y = tt(new("tx", 128), A("psMK", 384, 512), X, OP.mult)
+            NE = tt(new("tx", 128), x, y, OP.add)
+            if not lastt:
+                m = A("psMK", 384, 512) if eb == EA else A("psMK", 256, 384)
+                EL = ts(new("tu", 128), tt(new("psV", 128), m, A("POS"), OP.add), 2048.0, OP.mult)
+                for p in range(4):
+                    o, w = (EB, EA) if eb == EA else (EA, GT)
+                    act(A("EW", o + 512 * p, o + 512 * p + 512), IND(A("EW", w, w + 4096), part(EL, 32 * p, 32 * p + 32)))
+        if lastt:
+            for i in range(16):
+                mm([(A("psX1"), win("ZW", i), A("VW", 512 * i, 512 * i + 512))], i == 0, i == 15)
+            act(A("YT"), A("psX1"))
+            yo = (T.YY[0:128:16, 0:8192], (("YY", 0, 8192),), 8192, False, "sb")
+            op("y", lambda: g.sync.dma_start(yo[0], T.YT[:]), [yo], [A("YT")], 0.1, "yt_", 16, 3.5)
+        mk = new("tb", 64)
+        ab, cm, keep, dec = [part(mk, 16 * j, 16 * j + 16) for j in range(4)]
+        tt(ab, bad, badT, OP.max)
+        rdy = tt(new("tb"), A("FL", *s16), FT, OP.mult)
+        if t == 0:
+            rdy = tt(new("tb"), rdy, ab, OP.is_gt)
+        cum = scan(new("tb"), rdy, A("z32", 0, 16), 0.0, OP.add, OP.add)
+        rK = tt(new("tb"), rdy, A("K1"), OP.mult)
+        off = A("psD", 128, 144)
+        mm([(off, A(a), b) for a, b in (("ID", A("K1")), ("ID", A("Kr")), ("TRI", rdy), ("BO", cum), ("IN", rK))])
+        offU = cp(new("tu"), off)
+        ts(cm, off, 31.5, OP.is_lt)
+        act(A("SL", 0, 32), A("SLd"))
+        act(IND(A("SL"), offU), A("CK"), AF.Silu)
+        mm([(A("psD", 144, 160), A("DL"), A("SL", 0, 16)), (A("psD", 144, 160), A("DH"), A("SL", 16, 32))])
+        zU = ts(new("tu"), A("psD", 144, 160), -64.0, OP.add)
+        CR = send(t, act(A("CO", 256 * t, 256 * t + 256), IND(A("VW"), zU)), "CR", "c")
+        tt(dec, ab, cm, OP.max)
+        ts(keep, dec, -1.0, OP.mult, 1.0, OP.add)
+        vv = new("tb", 32)
+        for h in range(2):
+            tt(part(vv, 16 * h, 16 * h + 16), part(V, 16 * h, 16 * h + 16), keep, OP.mult)
+        tt(A("vX"), IND(vv, A("X1")), A("MX"), OP.mult)
+        for h in range(2):
+            o = A("psM2", 64 + 16 * h, 80 + 16 * h)
+            mm([(o, A("EQ", 256 * q + 128 * h, 256 * q + 128 * h + 128), A("vX", 16 * q, 16 * q + 16)) for q in range(16)]
+               + [(o, A("DW", 112 - 16 * q, 240 - 16 * q), A("vX", 128 * h + 16 * q, 128 * h + 16 * q + 16)) for q in range(8)])
+        mn = scan(new("tb", 32), A("P01"), A("psM2", 64, 96), 0.0, OP.mult, OP.min)
+        tt(A("Er"), IND(mn, A("X2")), A("NM"), OP.is_lt)
+        wT = A("psM2", 96, 112)
+        mm([(part(wT, 8 * h, 8 * h + 8), A("Er", 128 * h, 128 * h + 128), A("GI")) for h in range(2)])
+        if not lastt:
+            thr = tt(new("tw"), tn, act(new("tw"), dec, AF.Copy, -0.5, 8.0), OP.add)
+            FT = send(t + 1, tt(A("FL", 16 * t + 16, 16 * t + 32), wT, thr, OP.is_ge), "FR", "f")
+        wn = tt(new("tb"), wT, h1, OP.is_ge)
+        rep("psMK", 0, "ID", mk, 8)
+        x1 = tt(new("psV", 128), A("psMK", 0, 128), NE, OP.mult)
+        x2 = tt(new("tx", 128), A("psMK", 128, 256), NR[t], OP.mult)
+        y = tt(new("psV", 128), x1, x2, OP.add)
+        z = tt(new("tx", 128), A("psMK", 256, 384), KH, OP.mult)
+        KS = tt(new("ti", 128), y, z, OP.add)
+        cI = ts(new("ti", 128), KS, 8191, OP.bitwise_and)
+        rep("psM2", 128, "HI", wn, 8)
+        KH = tt(new("ti", 128), tt(new("psV", 128), A("psM2", 128, 256), fm, OP.mult), KS, OP.add)
+        ct = new("tb", 32)
+        tt(part(ct, 0, 16), nx, keep, OP.mult)
+        if lastt:
+            to_r("psM1", [part(ct, 0, 16)])
+        else:
+            tW = tt(part(ct, 16, 32), tW, act(new("tb"), dec, AF.Copy, 0.0, t + 1.0), OP.max)
+            to_r("psM1", [ct])
+        act(A("cdR"), A("psM1", 0, 256), AF.Copy, 0.0, 1.0 / 64)
+        act(A("yR"), IND(A("cdR"), curU))
+        y8 = A("psM2", 112, 128)
+        to_w(y8, A("yR"), "ZA")
+        a = tt(new("tw"), tt(new("tw"), y8, A("aw8", *s16), OP.mult), A("OW"), OP.add)
+        sb = tt(new("tw"), ts(new("tw"), y8, 0.0, OP.is_gt), b0, OP.mult)
+        if lastt:
+            tt(A("ol"), a, sb, OP.add)
+            cp(A("oc"), IND(cI, A("PO")))
+            ts(A("oh"), IND(KH, A("PO")), HELD, OP.is_ge)
+            mm([(A("psD", 256, 512), A("WY"), CR)])
+            act(A("ys8"), A("psD", 256, 512))
+            cp(IND(A("YY"), zU), A("ys8"))
+        else:
+            cur = tt(new("ti"), a, sb, OP.add)
+            curU = cp(new("tu"), cur)
+            cU = cp(new("tu", 128), cI)
+            act(A("thR", 1, 257), A("psM1", 256, 512), AF.Copy, -0.5)
+            thB = act(new("tw"), dec, AF.Copy, 200.0, 100000.0)
+            n = tt(new("tw"), tt(new("tw"), n, wn, OP.subtract), act(new("tw"), dec, AF.Copy, 0.0, 8.0), OP.max)
+            l = cp(new("tu"), tt(new("tw"), tt(new("tw"), pre, wn, OP.mult), A("J16"), OP.add))
+            act(IND(A("TT"), l), A("WHT", 256 * t + 256, 256 * t + 512), AF.Silu)
+            cp(IND(A("VW"), zU), CR)
+    for e, sem, tout, o in (("s", "oc_", T.yc[:], A("oc")), ("s", "ol_", T.yl[:], A("ol")), ("y", "oh_", T.yh[:], A("oh")), ("y", "oy_", T.ys[:], yo)):
+        (lambda e, sem, tout, o: op(e, lambda: eng[e].dma_start(tout, o[0]), [], [o], 0.1, sem, 16, 2.5))(e, sem, tout, o)
 
     n = len(ops)
     deps = [set() for _ in range(n)]
@@ -504,9 +485,8 @@ def rank_program(g, core, T, topo):
     for i, o in enumerate(ops):
         for w, acc in ((False, o["rd"]), (True, o["wr"])):
             for name, a, b in acc:
-                ps = name[:2] == "ps"
                 for a2, b2, w2, k in log.get(name, []):
-                    if k != i and ((ps and (ops[k]["e"] != o["e"] or o["e"] == "t")) or (a < b2 and a2 < b and (w or w2))):
+                    if k != i and a < b2 and a2 < b and (w or w2):
                         deps[i].add(k)
         for w, acc in ((False, o["rd"]), (True, o["wr"])):
             for name, a, b in acc:
@@ -516,14 +496,15 @@ def rank_program(g, core, T, topo):
                 log[name] = old + [(a, b, w, i)]
         if "send" in o:
             deps[i].add(o["send"])
+        o["banks"] = {x[0] for x in o["rd"] + o["wr"] if x[0][:2] == "ps"}
     succ = [[] for _ in range(n)]
     for i in range(n):
         for k in deps[i]:
             succ[k].append(i)
-    lat = [(o["arr"] if o["arr"] is not None else 0.13) for o in ops]
+    lat = [(o["arr"] if o["arr"] is not None else WAKE) for o in ops]
     prio = [0.0] * n
     for i in range(n - 1, -1, -1):
-        prio[i] = ops[i]["cost"] + max([lat[i] + prio[k] if ops[k]["e"] != ops[i]["e"] or ops[i]["e"] != "t" else prio[k] for k in succ[i]] + [0.0])
+        prio[i] = ops[i]["cost"] + max([lat[i] + prio[k] if ops[k]["e"] != ops[i]["e"] or ops[i]["e"] != "t" else prio[k] for k in succ[i]] + [lat[i]])
     for i in range(n):
         if "load" in ops[i]:
             prio[i] = 1e6 - i
@@ -534,24 +515,38 @@ def rank_program(g, core, T, topo):
         if not left[i]:
             ready.setdefault(ops[i]["e"], []).append(i)
     free = {e: 0.0 for e in "vstgya"}
+    bank = {}
+    shut = set()
+
+    def start(i):
+        o = ops[i]
+        if o["banks"] & shut and not (o["mm"] and not o["mm"][1]):
+            return 1e9
+        return max([rt[i]] + [bank[b][1] + WAKE for b in o["banks"] if b in bank and bank[b][0] != o["e"]])
+
     order = []
     while len(order) < n:
         best = None
         for e, l in ready.items():
-            if not l:
-                continue
-            t0 = max(free[e], min(rt[i] for i in l))
-            if best is None or t0 < best[0]:
-                best = (t0, e)
-        t0, e = best
-        i = max([i for i in ready[e] if rt[i] <= t0 + 1e-9], key=lambda i: (prio[i], -i))
+            if l:
+                st = [start(i) for i in l]
+                t0 = max(free[e], min(st))
+                if best is None or t0 < best[0]:
+                    best = (t0, e, st)
+        t0, e, st = best
+        i = max([i for i, s in zip(ready[e], st) if s <= t0 + 1e-9], key=lambda i: (prio[i], -i))
+        o = ops[i]
         ready[e].remove(i)
         order.append(i)
         if e != "a":
-            free[e] = t0 + ops[i]["cost"]
+            free[e] = t0 + o["cost"]
+        for b in o["banks"]:
+            bank[b] = (e, t0 + o["cost"])
+        if o["mm"] and o["mm"][1] != o["mm"][2]:
+            (shut.update if o["mm"][1] else shut.difference_update)(o["banks"])
         for k in succ[i]:
-            d = 0.0 if ops[i]["e"] == ops[k]["e"] == "t" else 0.0 if ops[i]["e"] == "g" and ops[k]["e"] == "a" else lat[i]
-            rt[k] = max(rt[k], t0 + ops[i]["cost"] + d)
+            d = 0.0 if o["e"] == ops[k]["e"] == "t" else 0.0 if o["e"] == "g" and ops[k]["e"] == "a" else lat[i]
+            rt[k] = max(rt[k], t0 + o["cost"] + d)
             left[k] -= 1
             if not left[k]:
                 ready.setdefault(ops[k]["e"], []).append(k)
@@ -595,12 +590,10 @@ def rank_program(g, core, T, topo):
                 x.then_inc(T.sem[sem], o["inc"])
         else:
             lst, first, last = o["mm"]
-            runs = lst if isinstance(lst[0], list) else [lst]
-            for run in runs:
-                for q, (po, pl, pr) in enumerate(run):
-                    waits(e, pl[1] + pr[1], False)
-                    waits(e, po[1], True)
-                    x = g.tensor.matmul(po[0], pl[0], pr[0], first and q == 0, last and q == len(run) - 1)
+            for q, (po, pl, pr) in enumerate(lst):
+                waits(e, pl[1] + pr[1], False)
+                waits(e, po[1], True)
+                x = g.tensor.matmul(po[0], pl[0], pr[0], first and q == 0, last and q == len(lst) - 1)
             x.then_inc(T.sem.st, 1)
         if sem == "lsem":
             continue

@@ -1,7 +1,7 @@
 from concourse.mybir import AluOpType as OP, ActivationFunctionType as AF
 
 NS = 5
-EA, GT, EB = 0, 2048, 4096
+EA, EB = 0, 4096
 F, B, I, U16 = "float32", "bfloat16", "int32", "uint16"
 BASE, HELD = 131072.0, 262144.0
 BIG = 2.0 ** 95
@@ -14,28 +14,30 @@ def _buf(names, n, d):
 
 
 _buf("VW", 8448, B)
-_buf("EW", 6144, B)
+_buf("EW", 8192, B)
 _buf("TT YY", 8448, F)
-_buf("ad WR LO", 2048, B)
+_buf("ad WR", 2048, B)
 _buf("Z2", 16 * 144, B)
 _buf("EQ", 4096, B)
-_buf("pI rI gI kI sI bI", 1, I)
-_buf("pF rF gF g15 g7 lo8 hi8 r1 kF sF bF gx c1 c2", 1, F)
-_buf("uF CK ys8 u16F u2F", 256, F)
+_buf("pI rI gI kI bI", 1, I)
+_buf("pF rF gF g15 g7 lo8 hi8 r1 kF bF gx", 1, F)
+_buf("uF CK PK ys8 u16F u2F", 256, F)
 _buf("mI mG cI hI", 128, I)
 _buf("ZB ZA ZH ZW ZC", 144, B)
-_buf("BO ID IN LL TRI WY HI IG wr", 128, B)
+_buf("BO ID IN LL TRI WY HI wr", 128, B)
 _buf("DL DH JO POS M01 RS HS AGs oc oh iA iB", 128, F)
 _buf("DW", 240, B)
 _buf("GI", 8, B)
 _buf("RM OW J16 o8 o64 wT ol", 16, F)
 _buf("K1 Kr", 16, B)
-_buf("MX NM A16 RO vX Er tau vR cdR yR", 256, B)
-_buf("SL", 768, F)
+_buf("MX NM OHa OHb G1 G2 T1 T2 WO vX Er tau vR cdR yR u3F", 256, B)
+_buf("waR", 1024, B)
+_buf("X3", 2, U16)
+_buf("SL SM", 768, F)
 _buf("SLd P01", 32, F)
 _buf("WHT", 256 * NS, F)
 _buf("thR", 272, B)
-_buf("aw8 naw ct wa", 16 * NS, F)
+_buf("aw8 naw ct", 16 * NS, F)
 _buf("awI", 16 * NS, I)
 _buf("z32", 32, B)
 _buf("wI", 16, I)
@@ -48,16 +50,74 @@ _buf("tx", 2000, F)
 _buf("ti", 4200, I)
 _buf("tb", 3000, B)
 _buf("tu", 1800, U16)
-_buf("FL FR BL BR", 16 * NS, B)
+_buf("FL FR BL BR wa", 16 * NS, B)
 _buf("NG NR", 128 * NS, F)
-_buf("CO CR", 256 * NS, B)
-for _n in ("X1", "X2", "D", "S", "MK", "M1", "M2", "V"):
+_buf("CR", 256, B)
+_buf("GR", 2048 * NS, B)
+for _n in ("X1", "X2", "X3", "D", "MK", "M1", "M2", "V"):
     SCRATCH["ps" + _n] = ("psum", [128, 512], F)
 LOADS = ["dcs", "dho", "dwk", "dsn", "dx"]
-SEMAPHORES = ["sv", "ss", "st", "sg", "lsem", "oc_", "oh_", "ol_", "oy_", "yt_"] + LOADS + [k + str(t) for k in "fbnc" for t in range(NS)]
+SEMAPHORES = ["sv", "ss", "st", "sg", "lsem", "oc_", "oh_", "ol_", "oy_", "yt_"] + LOADS + [k + str(t) for k in "fbncl" for t in range(NS)]
 CY, PE = 0.00083 * 1.15, 0.00042 * 1.15
-WAKE = 0.12
+WAKE, SAME, FAR, PASSES, SHAKE = 0.25, 0.15, 2.5, 150, 1.0
+YS = 0
 JENG = ("svsv", "svsv", "svsv", "svsv", "svsv")
+
+
+PLAN = []
+
+
+def plan(ops, deps):
+    n = len(ops)
+    cost = [o["cost"] for o in ops]
+    pred, succ = [[] for _ in range(n)], [[] for _ in range(n)]
+    for i in range(n):
+        for k in deps[i]:
+            a, b = ops[k], ops[i]
+            d = a["arr"] if a["arr"] is not None else 0.0 if a["e"] == b["e"] == "t" or b["e"] == "a" else SAME if a["e"] == b["e"] else WAKE
+            pred[i].append((k, d))
+            succ[k].append((i, d))
+    tail = [(o["arr"] or 0.0) for o in ops]
+
+    lanes = [([(o["e"], 0.0)] if o["e"] != "a" else []) + [(b, WAKE) for b in sorted(o["banks"])] for o in ops]
+
+    def place(before, key, head, text):
+        for i in text:
+            key[i] = max([key[i]] + [key[k] + 1e-6 for k, _d in before[i]])
+        busy, at = {}, [0.0] * n
+        for i in sorted(text, key=lambda i: key[i]):
+            e, c = ops[i]["e"], cost[i]
+            s = max([head[i]] + [at[k] + cost[k] + d for k, d in before[i]])
+            moved = True
+            while moved:
+                moved = False
+                for r, w in lanes[i]:
+                    for u in range(int(s - w), int(s + c + w) + 1):
+                        for a, b, e2 in busy.get((r, u), ()):
+                            if (not w or e2 != e) and a - w < s + c - 1e-9 and s + 1e-9 < b + w:
+                                s, moved = b + w, True
+            at[i] = s
+            for r, _w in lanes[i]:
+                for u in range(int(s), int(s + c) + 1):
+                    busy.setdefault((r, u), []).append((s, s + c, e))
+        return at
+
+    prio = [0.0] * n
+    for i in range(n - 1, -1, -1):
+        prio[i] = cost[i] + max([d + prio[k] for k, d in succ[i]] + [tail[i]])
+    best, seed = None, 1
+    for p in range(PASSES):
+        if p % 3 == 0 and best:
+            for i in range(n):
+                seed = (seed * 1103515245 + 12345) % 2147483648
+                prio[i] = SHAKE * seed / 2147483648 - best[1][i]
+        at = place(pred, [(-1e6 + i if "load" in ops[i] else -prio[i]) for i in range(n)], [0.0] * n, range(n))
+        end = max(at[i] + cost[i] + tail[i] for i in range(n))
+        if best is None or end < best[0]:
+            best = (end, at)
+        back = place(succ, [-at[i] - cost[i] for i in range(n)], [0.0 if succ[i] else tail[i] for i in range(n)], range(n - 1, -1, -1))
+        prio = [back[i] + cost[i] for i in range(n)]
+    return sorted(range(n), key=lambda i: (best[1][i], i))
 
 
 def rank_program(g, core, T, topo):
@@ -154,7 +214,7 @@ def rank_program(g, core, T, topo):
         ops[-1]["load"] = True
 
     twins = [T.cores[rank ^ (1 + t % 3)] for t in range(NS)]
-    nsent = [0]
+    nsent, sent = [0], [0]
 
     def send(t, s, rb, key):
         dst = twins[t]
@@ -162,11 +222,21 @@ def rank_program(g, core, T, topo):
         es = topo.engines(core, dst)
         w = s[2]
         r = A(rb, w * t, w * t + w)
-        op("g", lambda: g.remote_dma(out_ap=r[0], in_ap=s[0], remote_sem=T.sem[key + str(t)], local_sem=T.sem.lsem, pid=pid, routing_id=rid,
+        ls = "l" + str(t) if key == "c" else "lsem"
+        op("g", lambda: g.remote_dma(out_ap=r[0], in_ap=s[0], remote_sem=T.sem[key + str(t)], local_sem=T.sem[ls], pid=pid, routing_id=rid,
                                      dma_engine_mask=sum(1 << x for x in es)), [], [s], 0.8, "lsem", len(es))
-        op("a", None, [(None, ((rb, w * t, w * t + w),))], [s], 0.0, key + str(t), len(topo.engines(dst, core)), 2.4 + w / 400.0)
-        ops[-1]["send"] = len(ops) - 2
-        nsent[0] += len(es)
+        i = len(ops) - 1
+        if key != "f":
+            ops[i]["send"] = sent[0]
+            sent[0] = i
+        way = FAR + 128 / len(es) * (0.05 + w * (2 if s[3] else 4) / 14e3)
+        op("a", None, [(None, ((rb, w * t, w * t + w),))], [], 0.0, key + str(t), len(topo.engines(dst, core)), way)
+        ops[-1]["send"] = i
+        if key == "c":
+            op("a", None, [], [s], 0.0, ls, len(es), way)
+            ops[-1]["send"] = i
+        else:
+            nsent[0] += len(es)
         return r
 
     tops = {"tw": 0, "tx": 0, "ti": 0, "tb": 0, "tu": 0, "psV": 0}
@@ -198,12 +268,13 @@ def rank_program(g, core, T, topo):
     iota(A("M01"), [[0, 16], [1, 8]], 0, 0)
     iota(A("u16F"), [[0, 16], [1, 16]], 0, 0)
     iota(A("u2F"), [[0, 16], [16, 8], [0, 2]], 0, 0)
+    iota(A("u3F"), [[1, 16], [0, 16]], 0, 0)
     iota(A("P01"), [[0, 16], [1, 2]], 0, 0)
     iota(A("TT", 6144, 8448), [[0, 2304]], 0, 0)
     ms(A("TT", 0, 2048), 0.0)
     for q in (1, 2):
         act(A("TT", 2048 * q, 2048 * q + 2048), A("TT", 0, 2048))
-    for a, m in (("r", 15), ("g", 112), ("k", 7), ("s", 8), ("b", 1)):
+    for a, m in (("r", 15), ("g", 112), ("k", 7), ("b", 1)):
         ts(A(a + "I"), A("pI"), m, OP.bitwise_and)
         cp(A(a + "F"), A(a + "I"))
     cp(A("pF"), A("pI"))
@@ -224,10 +295,8 @@ def rank_program(g, core, T, topo):
     SP = ts(new("tu", 128), A("iA"), A("rF"), OP.add)
     ts(A("POS"), A("uF", 0, 128), 16.0, OP.mult, A("rF"), OP.add)
     ts(A("POS"), A("POS"), 1.0 / 2048, OP.mult)
-    ts(A("c1"), A("kF"), 16.0, OP.mult, A("hi8"), OP.add)
-    ts(A("PI"), A("uF", 0, 8), 2.0, OP.mult, A("c1"), OP.add)
-    ts(A("c2"), A("rF"), 8.0, OP.mult)
-    ts(A("PO"), A("uF", 0, 8), A("c2"), OP.add)
+    ts(A("PI"), A("uF", 0, 8), 2.0, OP.mult, ts(new("tw", 1), A("kF"), 16.0, OP.mult, A("hi8"), OP.add), OP.add)
+    ts(A("PO"), A("uF", 0, 8), ts(new("tw", 1), A("rF"), 8.0, OP.mult), OP.add)
     c3 = ts(new("tw", 1), A("bF"), 16.0, OP.mult)
     ts(A("X1"), A("uF", 0, 16), c3, OP.add)
     ts(A("X2"), A("uF", 0, 16), 2.0, OP.mult, 1.0, OP.add)
@@ -259,12 +328,14 @@ def rank_program(g, core, T, topo):
     ts(A("GI"), A("uF", 0, 8), A("gx"), OP.is_equal)
     ts(A("MX"), A("u2F"), A("gF"), OP.is_equal)
     ts(A("NM"), A("u16F"), A("rF"), OP.not_equal, -9e29, OP.mult)
-    ts(A("A16"), A("u16F"), 16.0, OP.mult)
-    ig = ts(new("tx", 128), A("u16F", 0, 128), 1.0, OP.add)
-    ig2 = tt(new("tx", 128), ig, A("BO"), OP.mult)
-    ts(A("IG"), ig2, -1.0, OP.add)
+    ts(A("OHb"), A("u16F"), A("rF"), OP.is_equal)
+    ts(A("OHa"), A("u3F"), A("rF"), OP.is_equal)
+    ts(A("X3"), A("uF", 0, 2), 128.0, OP.mult, A("pF"), OP.add)
     c5 = ts(new("tw", 1), A("kF"), 32.0, OP.mult, 8192.0 + 64.0, OP.add)
     ts(A("SLd"), A("uF", 0, 32), c5, OP.add)
+    iota(A("PK"), [[128, 16], [1, 16]], 64, 0)
+    ts(A("PK"), A("PK"), ts(new("tw", 1), A("kF"), 16.0, OP.mult), OP.add)
+    ms(A("SM", 0, 32), 64.0)
     ms(A("z32"), 0.0)
     ms(A("thR"), -0.5)
     ms(A("thR", 0, 1), 1000.0)
@@ -286,6 +357,9 @@ def rank_program(g, core, T, topo):
         s = (16 * t, 16 * t + 16)
         tt(A("ct", *s), A("naw", *s), o1, OP.subtract)
         tt(A("wa", *s), A("awI", *s), A("wT"), OP.mult)
+    for h in range(2):
+        to_r("psMK", [A("wa", 16 + 32 * h, 48 + 32 * h)])
+        act(A("waR", 512 * h, 512 * h + 512), A("psMK"))
 
     x = ts(new("tx", 128), IND(A("hI"), A("PI")), HELD, OP.mult, BASE, OP.add)
     KH = tt(new("ti", 128), IND(A("cI"), A("PI")), x, OP.add)
@@ -303,8 +377,7 @@ def rank_program(g, core, T, topo):
     chi = cp(new("tb", 128), A("cI"))
     clo = tt(new("tb", 128), A("cI"), chi, OP.subtract)
     for i in range(16):
-        mm([(A("psM1", i, 256, 16), A("Z2", 144 * i + 7 - k, 144 * i + 135 - k), part(c, 16 * k, 16 * k + 16)) for k in range(8) for c in (chi, clo)],
-           i == 0, i == 15, A("psM1", 0, 256))
+        mm([(A("psM1", i, 256, 16), A("Z2", 144 * i + 7 - k, 144 * i + 135 - k), part(c, 16 * k, 16 * k + 16)) for k in range(8) for c in (chi, clo)])
     act(A("CK"), A("psM1", 0, 256), AF.Copy, 64.0)
     tW = ms(new("tb"), 0.0)
     cur = cp(new("ti"), A("OW"))
@@ -312,21 +385,21 @@ def rank_program(g, core, T, topo):
 
     def hashes(src, o):
         for h in range(2):
-            for z, p in (("ZA", 0), ("ZH", 128)):
-                mm([(A("psS", p + 64 * h, p + 64 * h + 64), win(z, i), A("EW", src + 1024 * h + i, src + 1024 * h + 1024, 16)) for i in range(16)])
-        act(A("AGs"), A("psS", 0, 128))
-        pr = tt(new("ti", 128), A("psS", 128, 256), A("AGs"), OP.mult)
+            for z, p in (("ZA", 256), ("ZH", 384)):
+                mm([(A("psD", p + 64 * h, p + 64 * h + 64), win(z, i), A("EW", src + 1024 * h + i, src + 1024 * h + 1024, 16)) for i in range(16)])
+        act(A("AGs"), A("psD", 256, 384))
+        pr = tt(new("ti", 128), A("psD", 384, 512), A("AGs"), OP.mult)
         h1 = ts(new("ti", 128), pr, 3, OP.arith_shift_right, 1023, OP.bitwise_and)
         h2 = ts(new("ti", 128), h1, 1.0, OP.add)
         ts(part(h2, 0, 128, 8), part(pr, 0, 128, 8), 3, OP.arith_shift_right, 8191, OP.bitwise_and)
         return scan(o, A("HS"), h2, BASE, OP.min, OP.add)
 
     NE = hashes(EA, new("tx", 128))
-    NR = {}
+    NR, GR = {}, {}
     thB = ms(new("tw"), 200.0)
 
     for t in range(NS):
-        eb = (EA, EA, EB, EA, EB)[t]
+        eb, GT = (EA, EA, EB, EA, EB)[t], (EB, EA)[t & 1] + 2048
         lastt = t == NS - 1
         s16 = (16 * t, 16 * t + 16)
         run = scan(new("ti", 128), A("RS"), KH, 0.0, OP.add, OP.min)
@@ -359,21 +432,19 @@ def rank_program(g, core, T, topo):
             ts(part(V, 16, 24), A("wa", 0, 8), 0.0, OP.is_gt, BIG, OP.mult)
             cp(part(V, 24, 32), A("wa", 8, 16))
         else:
-            bi = ts(new("ti"), cur, 15, OP.bitwise_and)
-            bf = cp(new("tw"), bi)
-            a16 = tt(new("tb"), cur, bi, OP.subtract)
-            rep("psM2", 256, "ID", a16, 16)
-            tt(A("RO"), A("psM2", 256, 512), A("A16"), OP.is_equal)
-            for h in range(2):
-                for q in range(8 * h, 8 * h + 8):
-                    ts(A("LO", 128 * q, 128 * q + 128), A("IG"), part(bf, q, q + 1), OP.is_equal, A("wa", 16 * t + q, 16 * t + q + 1), OP.mult)
-                mm([(A("psM2", 32 + 16 * h, 48 + 16 * h), A("LO", 128 * q, 128 * q + 128), A("RO", 16 * q, 16 * q + 16)) for q in range(8 * h, 8 * h + 8)])
-            cp(part(V, 0, 16), A("psM2", 32, 48))
-            tt(part(V, 16, 32), A("psM2", 48, 64), ts(new("tw"), A("psM2", 32, 48), 0.0, OP.is_gt, BIG, OP.mult), OP.max)
+            tt(A("G1"), IND(A("OHb"), curU), A("waR", 256 * t - 256, 256 * t), OP.mult)
+            act(A("G2"), IND(A("OHa"), curU))
+            for a, b, j, c in (("G1", "psM2", 256, "T1"), ("G2", "psMK", 0, "T2")):
+                mm([(A(b, j + 128 * h, j + 128 + 128 * h), A(a, 128 * h, 128 * h + 128), A("ID")) for h in range(2)])
+                act(A(c), A(b, j, j + 256))
+            mm([(A("psM2", 256 + 128 * h, 384 + 128 * h), A("T1", 128 * h, 128 * h + 128), A("T2", 128 * h, 128 * h + 128)) for h in range(2)])
+            act(A("WO"), A("psM2", 256, 512))
+            cp(V, IND(A("WO"), A("X3")))
+            tt(part(V, 16, 32), part(V, 16, 32), ts(new("tw"), part(V, 0, 16), 0.0, OP.is_gt, BIG, OP.mult), OP.max)
         b0 = tt(new("tw"), tt(new("tw"), A("naw", *s16), cur, OP.mult), A("ct", *s16), OP.add)
         for p in range(4):
             j = 512 * p
-            gt, x = A("EW", GT + j, GT + j + 512), A(("psX1", "psX2")[p & 1])
+            gt, x = A("EW", GT + j, GT + j + 512), A(("psX1", "psX2", "psX3", "psX1")[p])
             (act if JENG[t][p] == "s" else cp)(gt, IND(A("VW", 0, 8192), part(cU, 32 * p, 32 * p + 32)))
             mm([(x, A("IN"), A("EW", eb + j, eb + j + 512))], True, False)
             mm([(x, A("ID"), gt)], False, True)
@@ -385,20 +456,20 @@ def rank_program(g, core, T, topo):
         badT = send(t, bad, "BR", "b")
         X = hashes(GT, A("NG", 128 * t, 128 * t + 128))
         for u in ((0, 1), (2,), (3,), (4,), ())[t]:
+            GR[u] = send(u, A("EW", GT, GT + 2048), "GR", "c")
             NR[u] = send(u, X, "NR", "n")
         if t > 0:
             x = tt(new("psV", 128), A("psMK", 256, 384), NE, OP.mult)
             y = tt(new("tx", 128), A("psMK", 384, 512), X, OP.mult)
             NE = tt(new("tx", 128), x, y, OP.add)
             if not lastt:
-                m = A("psMK", 384, 512) if eb == EA else A("psMK", 256, 384)
-                EL = ts(new("tu", 128), tt(new("psV", 128), m, A("POS"), OP.add), 2048.0, OP.mult)
+                EL = ts(new("tu", 128), tt(new("psV", 128), A("psMK", 384, 512), A("POS"), OP.add), 2048.0, OP.mult)
                 for p in range(4):
-                    o, w = (EB, EA) if eb == EA else (EA, GT)
-                    act(A("EW", o + 512 * p, o + 512 * p + 512), IND(A("EW", w, w + 4096), part(EL, 32 * p, 32 * p + 32)))
-        if lastt:
-            for i in range(16):
-                mm([(A("psX1"), win("ZW", i), A("VW", 512 * i, 512 * i + 512))], i == 0, i == 15)
+                    o = EA + EB - eb + 512 * p
+                    act(A("EW", o, o + 512), IND(A("EW", eb, eb + 4096), part(EL, 32 * p, 32 * p + 32)))
+        if t == YS:
+            for j in range(0, 512, 64):
+                mm([(A("psX1", j, j + 64), win("ZW", i), A("VW", 512 * i + j, 512 * i + j + 64)) for i in range(16)])
             act(A("YT"), A("psX1"))
             yo = (T.YY[0:128:16, 0:8192], (("YY", 0, 8192),), 8192, False, "sb")
             op("y", lambda: g.sync.dma_start(yo[0], T.YT[:]), [yo], [A("YT")], 0.1, "yt_", 16, 3.5)
@@ -415,12 +486,13 @@ def rank_program(g, core, T, topo):
         offU = cp(new("tu"), off)
         ts(cm, off, 31.5, OP.is_lt)
         act(A("SL", 0, 32), A("SLd"))
-        act(IND(A("SL"), offU), A("CK"), AF.Silu)
-        mm([(A("psD", 144, 160), A("DL"), A("SL", 0, 16)), (A("psD", 144, 160), A("DH"), A("SL", 16, 32))])
-        zU = ts(new("tu"), A("psD", 144, 160), -64.0, OP.add)
-        CR = send(t, act(A("CO", 256 * t, 256 * t + 256), IND(A("VW"), zU)), "CR", "c")
+        for a, b, c in (("SM", "PK", 160), ("SL", "CK", 144)):
+            act(IND(A(a), offU), A(b), AF.Silu)
+            mm([(A("psD", c, c + 16), A("DL"), A(a, 0, 16)), (A("psD", c, c + 16), A("DH"), A(a, 16, 32))])
+        pU, zU = [ts(new("tu"), A("psD", c, c + 16), -64.0, OP.add) for c in (160, 144)]
+        CR = act(A("CR"), IND(GR[t], pU))
+        tt(keep, ab, cm, OP.is_equal)
         tt(dec, ab, cm, OP.max)
-        ts(keep, dec, -1.0, OP.mult, 1.0, OP.add)
         vv = new("tb", 32)
         for h in range(2):
             tt(part(vv, 16 * h, 16 * h + 16), part(V, 16 * h, 16 * h + 16), keep, OP.mult)
@@ -437,12 +509,14 @@ def rank_program(g, core, T, topo):
             thr = tt(new("tw"), tn, act(new("tw"), dec, AF.Copy, -0.5, 8.0), OP.add)
             FT = send(t + 1, tt(A("FL", 16 * t + 16, 16 * t + 32), wT, thr, OP.is_ge), "FR", "f")
         wn = tt(new("tb"), wT, h1, OP.is_ge)
-        rep("psMK", 0, "ID", mk, 8)
-        x1 = tt(new("psV", 128), A("psMK", 0, 128), NE, OP.mult)
-        x2 = tt(new("tx", 128), A("psMK", 128, 256), NR[t], OP.mult)
-        y = tt(new("psV", 128), x1, x2, OP.add)
-        z = tt(new("tx", 128), A("psMK", 256, 384), KH, OP.mult)
-        KS = tt(new("ti", 128), y, z, OP.add)
+        rep("psMK", 128, "ID", cm, 8)
+        x = tt(new("tx", 128), A("psMK", 128, 256), tt(new("tx", 128), NR[t], KH, OP.subtract), OP.mult)
+        y = tt(new("psV", 128), x, KH, OP.add)
+        z = tt(new("tx", 128), NE, y, OP.subtract)
+        rep("psMK", 0, "ID", ab, 8)
+        KS = tt(new("ti", 128), tt(new("tx", 128), A("psMK", 0, 128), z, OP.mult), y, OP.add)
+        if not lastt:
+            rep("psMK", 256, "ID", part(mk, 32, 64), 8)
         cI = ts(new("ti", 128), KS, 8191, OP.bitwise_and)
         rep("psM2", 128, "HI", wn, 8)
         KH = tt(new("ti", 128), tt(new("psV", 128), A("psM2", 128, 256), fm, OP.mult), KS, OP.add)
@@ -451,7 +525,7 @@ def rank_program(g, core, T, topo):
         if lastt:
             to_r("psM1", [part(ct, 0, 16)])
         else:
-            tW = tt(part(ct, 16, 32), tW, act(new("tb"), dec, AF.Copy, 0.0, t + 1.0), OP.max)
+            tW = tt(part(ct, 16, 32), act(new("tb"), tW, AF.Copy, 1.0), keep, OP.mult)
             to_r("psM1", [ct])
         act(A("cdR"), A("psM1", 0, 256), AF.Copy, 0.0, 1.0 / 64)
         act(A("yR"), IND(A("cdR"), curU))
@@ -459,18 +533,19 @@ def rank_program(g, core, T, topo):
         to_w(y8, A("yR"), "ZA")
         a = tt(new("tw"), tt(new("tw"), y8, A("aw8", *s16), OP.mult), A("OW"), OP.add)
         sb = tt(new("tw"), ts(new("tw"), y8, 0.0, OP.is_gt), b0, OP.mult)
+        if t >= YS:
+            mm([(A("psM2", 256, 512), A("WY"), CR)])
+            act(A("ys8"), A("psM2", 256, 512))
+            cp(IND(A("YY"), zU), A("ys8"))
         if lastt:
             tt(A("ol"), a, sb, OP.add)
             cp(A("oc"), IND(cI, A("PO")))
             ts(A("oh"), IND(KH, A("PO")), HELD, OP.is_ge)
-            mm([(A("psD", 256, 512), A("WY"), CR)])
-            act(A("ys8"), A("psD", 256, 512))
-            cp(IND(A("YY"), zU), A("ys8"))
         else:
             cur = tt(new("ti"), a, sb, OP.add)
             curU = cp(new("tu"), cur)
             cU = cp(new("tu", 128), cI)
-            act(A("thR", 1, 257), A("psM1", 256, 512), AF.Copy, -0.5)
+            act(A("thR", 1, 257), A("psM1", 256, 512), AF.Copy, t + 0.5, -1.0)
             thB = act(new("tw"), dec, AF.Copy, 200.0, 100000.0)
             n = tt(new("tw"), tt(new("tw"), n, wn, OP.subtract), act(new("tw"), dec, AF.Copy, 0.0, 8.0), OP.max)
             l = cp(new("tu"), tt(new("tw"), tt(new("tw"), pre, wn, OP.mult), A("J16"), OP.add))
@@ -497,59 +572,9 @@ def rank_program(g, core, T, topo):
         if "send" in o:
             deps[i].add(o["send"])
         o["banks"] = {x[0] for x in o["rd"] + o["wr"] if x[0][:2] == "ps"}
-    succ = [[] for _ in range(n)]
-    for i in range(n):
-        for k in deps[i]:
-            succ[k].append(i)
-    lat = [(o["arr"] if o["arr"] is not None else WAKE) for o in ops]
-    prio = [0.0] * n
-    for i in range(n - 1, -1, -1):
-        prio[i] = ops[i]["cost"] + max([lat[i] + prio[k] if ops[k]["e"] != ops[i]["e"] or ops[i]["e"] != "t" else prio[k] for k in succ[i]] + [lat[i]])
-    for i in range(n):
-        if "load" in ops[i]:
-            prio[i] = 1e6 - i
-    left = [len(d) for d in deps]
-    ready = {}
-    rt = [0.0] * n
-    for i in range(n):
-        if not left[i]:
-            ready.setdefault(ops[i]["e"], []).append(i)
-    free = {e: 0.0 for e in "vstgya"}
-    bank = {}
-    shut = set()
-
-    def start(i):
-        o = ops[i]
-        if o["banks"] & shut and not (o["mm"] and not o["mm"][1]):
-            return 1e9
-        return max([rt[i]] + [bank[b][1] + WAKE for b in o["banks"] if b in bank and bank[b][0] != o["e"]])
-
-    order = []
-    while len(order) < n:
-        best = None
-        for e, l in ready.items():
-            if l:
-                st = [start(i) for i in l]
-                t0 = max(free[e], min(st))
-                if best is None or t0 < best[0]:
-                    best = (t0, e, st)
-        t0, e, st = best
-        i = max([i for i, s in zip(ready[e], st) if s <= t0 + 1e-9], key=lambda i: (prio[i], -i))
-        o = ops[i]
-        ready[e].remove(i)
-        order.append(i)
-        if e != "a":
-            free[e] = t0 + o["cost"]
-        for b in o["banks"]:
-            bank[b] = (e, t0 + o["cost"])
-        if o["mm"] and o["mm"][1] != o["mm"][2]:
-            (shut.update if o["mm"][1] else shut.difference_update)(o["banks"])
-        for k in succ[i]:
-            d = 0.0 if o["e"] == ops[k]["e"] == "t" else 0.0 if o["e"] == "g" and ops[k]["e"] == "a" else lat[i]
-            rt[k] = max(rt[k], t0 + o["cost"] + d)
-            left[k] -= 1
-            if not left[k]:
-                ready.setdefault(ops[k]["e"], []).append(k)
+    if not PLAN:
+        PLAN.append(plan(ops, deps))
+    order = PLAN[0]
 
     cnt = {}
     known = {e: {} for e in "vstgya"}
@@ -562,7 +587,7 @@ def rank_program(g, core, T, topo):
             ps = name[:2] == "ps"
             for a2, b2, w2, sem, m in log.get(name, []):
                 ov = a < b2 and a2 < b
-                if (ov and w2 and (e != "t" or not w)) if sem == own else (ps or (ov and (w or w2))):
+                if (ov and (w or w2) and e != "t") if sem == own else (ps or (ov and (w or w2))):
                     if known[e].get(sem, 0) < m:
                         eng[e].wait_ge(T.sem[sem], m)
                         for q, v in list(clocks[(sem, m)].items()):
@@ -581,6 +606,7 @@ def rank_program(g, core, T, topo):
         if e == "a":
             clocks[(sem, m)] = {sem: m}
             note(sem, m, o["wr"], True)
+            note(sem, m, o["rd"], False)
             continue
         if o["mm"] is None:
             waits(e, o["rd"], False)
@@ -604,5 +630,5 @@ def rank_program(g, core, T, topo):
     for s in ("oc_", "ol_", "oh_", "oy_"):
         g.sync.wait_ge(T.sem[s], 16)
     g.wait_ge(T.sem.lsem, nsent[0])
-    for s in ("sv", "ss", "st", "sg"):
+    for s in ("sv", "ss", "st", "sg", "l%d" % (NS - 1)):
         g.wait_ge(T.sem[s], cnt[s])

@@ -1,3 +1,4 @@
+import math
 from concourse.mybir import AluOpType as OP, ActivationFunctionType as AF
 
 NS = 5
@@ -23,16 +24,16 @@ _buf("pI rI gI kI bI", 1, I)
 _buf("pF rF gF g15 g7 lo8 hi8 r1 kF bF gx", 1, F)
 _buf("uF CK PK ys8 u16F u2F", 256, F)
 _buf("mI mG cI hI", 128, I)
-_buf("ZB ZA ZH ZW ZC", 144, B)
+_buf("ZB ZA ZH ZC", 144, B)
 _buf("BO ID IN LL TRI WY HI wr", 128, B)
 _buf("DL DH JO POS M01 RS HS AGs oc oh iA iB", 128, F)
 _buf("DW", 240, B)
-_buf("GI", 8, B)
+_buf("GI WG", 8, B)
 _buf("RM OW J16 o8 o64 wT ol", 16, F)
 _buf("K1 Kr", 16, B)
 _buf("MX NM OHa OHb G1 G2 T1 T2 WO vX Er tau vR cdR yR u3F", 256, B)
 _buf("waR", 1024, B)
-_buf("X3", 2, U16)
+_buf("X3", 4, U16)
 _buf("SL SM", 768, F)
 _buf("SLd P01", 32, F)
 _buf("WHT", 256 * NS, F)
@@ -50,18 +51,22 @@ _buf("tx", 2000, F)
 _buf("ti", 4200, I)
 _buf("tb", 3000, B)
 _buf("tu", 1800, U16)
-_buf("FL FR BL BR wa", 16 * NS, B)
+_buf("FL FR wa", 16 * NS, B)
+_buf("BL BR", 32 * NS, B)
 _buf("NG NR", 128 * NS, F)
 _buf("CR", 256, B)
 _buf("GR", 2048 * NS, B)
-for _n in ("X1", "X2", "X3", "D", "MK", "M1", "M2", "V"):
+for _n in ("X1", "X2", "X3", "X4", "D", "MK", "M1", "M2"):
     SCRATCH["ps" + _n] = ("psum", [128, 512], F)
 LOADS = ["dcs", "dho", "dwk", "dsn", "dx"]
 SEMAPHORES = ["sv", "ss", "st", "sg", "lsem", "oc_", "oh_", "ol_", "oy_", "yt_"] + LOADS + [k + str(t) for k in "fbncl" for t in range(NS)]
-CY, PE = 0.00083 * 1.15, 0.00042 * 1.15
-WAKE, SAME, FAR, PASSES, SHAKE = 0.25, 0.15, 2.5, 150, 1.0
-YS = 0
-JENG = ("svsv", "svsv", "svsv", "svsv", "svsv")
+CY, PE = 0.00083, 0.00042
+CASES = ((1.0, 1.04, 1.0, 0.3, 0.2, 2.7, 0.8), (1.1, 1.04, 1.0, 0.25, 0.15, 3.0, 0.8), (1.5, 1.33, 1.58, 0.2, 0.2, 3.0, 0.8))
+MID = (1.05, 1.04, 1.0, 0.3, 0.2, 2.8, 0.8)
+MOVES, SEED = 1500, 3
+PASSES, SHAKE = 150, 1.0
+YS = 3
+JENG = ("vsvs",) * NS
 
 
 PLAN = []
@@ -69,19 +74,22 @@ PLAN = []
 
 def plan(ops, deps):
     n = len(ops)
-    cost = [o["cost"] for o in ops]
-    pred, succ = [[] for _ in range(n)], [[] for _ in range(n)]
-    for i in range(n):
-        for k in deps[i]:
-            a, b = ops[k], ops[i]
-            d = a["arr"] if a["arr"] is not None else 0.0 if a["e"] == b["e"] == "t" or b["e"] == "a" else SAME if a["e"] == b["e"] else WAKE
-            pred[i].append((k, d))
-            succ[k].append((i, d))
-    tail = [(o["arr"] or 0.0) for o in ops]
 
-    lanes = [([(o["e"], 0.0)] if o["e"] != "a" else []) + [(b, WAKE) for b in sorted(o["banks"])] for o in ops]
+    def times(f, ga, sc, wake, same, far, slow):
+        cost = [o["cost"] * (slow if o["e"] == "a" else 1.0 if o["sem"] == "lsem" or o["arr"] else f) * {"ga": ga, "sc": sc}.get(o["kind"], 1.0) for o in ops]
+        tail = [(o["arr"] or 0.0) * slow for o in ops]
+        pred, succ = [[] for _ in range(n)], [[] for _ in range(n)]
+        for i in range(n):
+            for k in deps[i]:
+                a, b = ops[k], ops[i]
+                d = (0.0 if a["e"] == b["e"] and a["e"] in "tga" else far - 0.8 if b["e"] == "a" else tail[k] if a["arr"]
+                     else same if a["e"] == b["e"] else wake)
+                pred[i].append((k, d))
+                succ[k].append((i, d))
+        return cost, pred, succ, tail, wake
 
-    def place(before, key, head, text):
+    def place(before, key, head, text, cost, wake):
+        lanes = [[(o["e"], 0.0)] + [(b, wake) for b in sorted(o["banks"])] for o in ops]
         for i in text:
             key[i] = max([key[i]] + [key[k] + 1e-6 for k, _d in before[i]])
         busy, at = {}, [0.0] * n
@@ -102,22 +110,86 @@ def plan(ops, deps):
                     busy.setdefault((r, u), []).append((s, s + c, e))
         return at
 
+    def replay(order, case):
+        cost, pred, _succ, tail, wake = case
+        free, bank, at = {}, {}, [0.0] * n
+        for i in order:
+            e = ops[i]["e"]
+            s = max([free.get(e, 0.0)] + [at[k] + cost[k] + d for k, d in pred[i]]
+                    + [bank[b][1] + wake for b in ops[i]["banks"] if b in bank and bank[b][0] != e])
+            at[i] = s
+            free[e] = s + cost[i]
+            for b in ops[i]["banks"]:
+                bank[b] = (e, s + cost[i])
+        return at, max(at[i] + cost[i] + tail[i] for i in range(n))
+
+    cases = [times(*c) for c in CASES]
+    cost, pred, succ, tail, wake = times(*MID)
     prio = [0.0] * n
     for i in range(n - 1, -1, -1):
         prio[i] = cost[i] + max([d + prio[k] for k, d in succ[i]] + [tail[i]])
-    best, seed = None, 1
+    best, short, seed = None, None, SEED
     for p in range(PASSES):
-        if p % 3 == 0 and best:
+        if p % 3 == 0 and short:
             for i in range(n):
                 seed = (seed * 1103515245 + 12345) % 2147483648
-                prio[i] = SHAKE * seed / 2147483648 - best[1][i]
-        at = place(pred, [(-1e6 + i if "load" in ops[i] else -prio[i]) for i in range(n)], [0.0] * n, range(n))
+                prio[i] = SHAKE * seed / 2147483648 - short[1][i]
+        at = place(pred, [(-1e6 + i if "load" in ops[i] else -prio[i]) for i in range(n)], [0.0] * n, range(n), cost, wake)
         end = max(at[i] + cost[i] + tail[i] for i in range(n))
-        if best is None or end < best[0]:
-            best = (end, at)
-        back = place(succ, [-at[i] - cost[i] for i in range(n)], [0.0 if succ[i] else tail[i] for i in range(n)], range(n - 1, -1, -1))
+        if short is None or end < short[0]:
+            short = (end, at)
+        order = sorted(range(n), key=lambda i: (at[i], i))
+        score = sum(math.log(replay(order, c)[1]) for c in cases)
+        if best is None or score < best[0]:
+            best = (score, order)
+        back = place(succ, [-at[i] - cost[i] for i in range(n)], [0.0 if succ[i] else tail[i] for i in range(n)], range(n - 1, -1, -1), cost, wake)
         prio = [back[i] + cost[i] for i in range(n)]
-    return sorted(range(n), key=lambda i: (best[1][i], i))
+    order, score = best[1], best[0]
+    for p in range(MOVES):
+        cost, pred, succ, tail, wake = cases[p % len(cases)]
+        at = replay(order, cases[p % len(cases)])[0]
+        pos, last, arcs = {}, {}, []
+        for j, i in enumerate(order):
+            pos[i] = (j, [last[r] for r in [ops[i]["e"]] + sorted(ops[i]["banks"]) if r in last])
+            for r in [ops[i]["e"]] + sorted(ops[i]["banks"]):
+                last[r] = i
+        i = max(range(n), key=lambda i: at[i] + cost[i] + tail[i])
+        while at[i] > 0:
+            k = max(pred[i], key=lambda x: at[x[0]] + cost[x[0]] + x[1], default=None)
+            if k is None or at[k[0]] + cost[k[0]] + k[1] < at[i] - 1e-9:
+                k = (max(pos[i][1], key=lambda x: at[x] + cost[x] + (wake if ops[x]["e"] != ops[i]["e"] else 0.0)),)
+                arcs.append((k[0], i))
+            i = k[0]
+        for _ in range(8):
+            seed = (seed * 1103515245 + 12345) % 2147483648
+            a, b = arcs[seed // 64 % len(arcs)]
+            if "load" in ops[a]:
+                continue
+            mid = order[pos[a][0]:pos[b][0] + 1]
+            if seed & 32:
+                need = {b}
+                for i in reversed(mid):
+                    if i in need:
+                        need.update(k for k, _d in pred[i])
+                if a in need:
+                    continue
+                mid = [i for i in mid if i in need] + [i for i in mid if i not in need]
+            else:
+                need = {a}
+                for i in mid:
+                    if any(k in need for k, _d in pred[i]):
+                        need.add(i)
+                if b in need:
+                    continue
+                mid = [i for i in mid if i not in need] + [i for i in mid if i in need]
+            new = order[:pos[a][0]] + mid + order[pos[b][0] + 1:]
+            s = sum(math.log(replay(new, c)[1]) for c in cases)
+            if s <= score + 0.0005:
+                order, score = new, s
+                if s < best[0]:
+                    best = (s, new)
+                break
+    return best[1]
 
 
 def rank_program(g, core, T, topo):
@@ -148,11 +220,12 @@ def rank_program(g, core, T, topo):
         for o in outs:
             wr.append(o[1][0])
             rd += list(o[1][1:])
-        ops.append({"e": e, "call": call, "rd": rd, "wr": wr, "cost": cost, "sem": sem or esem.get(e), "inc": inc, "arr": arr, "mm": None})
+        ops.append({"e": e, "call": call, "rd": rd, "wr": wr, "cost": cost, "sem": sem or esem.get(e), "inc": inc, "arr": arr, "mm": None,
+                    "kind": "sc" if any(len(o) > 4 and o[4] == "ind" for o in outs) else "ga" if any(o[4] == "ind" for o in ins) else ""})
 
     def vcost(o, ins, n, two=False):
         if o[4] == "ind":
-            return 0.05 + n * 3.0 * CY
+            return 0.05 + n * 3.8 * CY
         if any(x[4] == "ind" for x in ins):
             return 0.05 + n * 1.5 * CY
         return max(64, n * (2 if two and all(x[4] == "sb" for x in ins) else 0.5 if not two and o[3] and ins[0][3] else 1)) * CY
@@ -183,7 +256,7 @@ def rank_program(g, core, T, topo):
         return o
 
     def act(o, a, func=AF.Copy, bias=0.0, scale=1.0):
-        c = 0.065 + a[2] * (3.0 if o[4] == "ind" else 1.5) * CY if "ind" in (o[4], a[4]) else max(64, a[2]) * CY
+        c = 0.065 + a[2] * (3.8 if o[4] == "ind" else 1.5) * CY if "ind" in (o[4], a[4]) else max(64, a[2]) * CY
         if bias == 0.0 and scale == 1.0:
             op("s", lambda: g.scalar.activation(o[0], a[0], func), [o], [a], c)
         else:
@@ -210,7 +283,7 @@ def rank_program(g, core, T, topo):
         mm([(A(on, a + k, a + n, times), A(m), src) for k in range(times)], whole=A(on, a, a + n))
 
     def load(e, sem, o, tin):
-        op(e, lambda: eng[e].dma_start(o[0], tin), [o], [], 0.1, sem, 16, 2.5 + o[2] * (2 if o[3] else 4) * 128 / 170e3)
+        op(e, lambda: eng[e].dma_start(o[0], tin), [o], [], 0.1, sem, 16, 2.5 + o[2] * (2 if o[3] else 4) * 128 / 120e3)
         ops[-1]["load"] = True
 
     twins = [T.cores[rank ^ (1 + t % 3)] for t in range(NS)]
@@ -226,20 +299,19 @@ def rank_program(g, core, T, topo):
         op("g", lambda: g.remote_dma(out_ap=r[0], in_ap=s[0], remote_sem=T.sem[key + str(t)], local_sem=T.sem[ls], pid=pid, routing_id=rid,
                                      dma_engine_mask=sum(1 << x for x in es)), [], [s], 0.8, "lsem", len(es))
         i = len(ops) - 1
-        if key != "f":
-            ops[i]["send"] = sent[0]
-            sent[0] = i
-        way = FAR + 128 / len(es) * (0.05 + w * (2 if s[3] else 4) / 14e3)
-        op("a", None, [(None, ((rb, w * t, w * t + w),))], [], 0.0, key + str(t), len(topo.engines(dst, core)), way)
+        ops[i]["send"] = sent[0]
+        sent[0] = i
+        way = 128 / len(es) * (0.05 + w * (2 if s[3] else 4) / 9e3)
+        op("a", None, [(None, ((rb, w * t, w * t + w),))], [], way, key + str(t), len(es), 0.8)
         ops[-1]["send"] = i
         if key == "c":
-            op("a", None, [], [s], 0.0, ls, len(es), way)
-            ops[-1]["send"] = i
+            op("a", None, [], [s], 0.01, ls, len(es), 0.8)
+            ops[-1]["send"] = i + 1
         else:
             nsent[0] += len(es)
         return r
 
-    tops = {"tw": 0, "tx": 0, "ti": 0, "tb": 0, "tu": 0, "psV": 0}
+    tops = {"tw": 0, "tx": 0, "ti": 0, "tb": 0, "tu": 0}
 
     def new(k, n=16):
         a = tops[k]
@@ -271,9 +343,9 @@ def rank_program(g, core, T, topo):
     iota(A("u3F"), [[1, 16], [0, 16]], 0, 0)
     iota(A("P01"), [[0, 16], [1, 2]], 0, 0)
     iota(A("TT", 6144, 8448), [[0, 2304]], 0, 0)
-    ms(A("TT", 0, 2048), 0.0)
-    for q in (1, 2):
-        act(A("TT", 2048 * q, 2048 * q + 2048), A("TT", 0, 2048))
+    ms(A("TT", 0, 768), 0.0)
+    for a, b in ((768, 768), (1536, 1536), (3072, 1536), (4608, 1536)):
+        act(A("TT", a, a + b), A("TT", 0, b))
     for a, m in (("r", 15), ("g", 112), ("k", 7), ("b", 1)):
         ts(A(a + "I"), A("pI"), m, OP.bitwise_and)
         cp(A(a + "F"), A(a + "I"))
@@ -306,7 +378,6 @@ def rank_program(g, core, T, topo):
     ts(A("ZB"), A("uF", 0, 144), A("g15"), OP.is_equal)
     ts(A("ZA"), A("ZB"), A("lo8"), OP.mult)
     ts(A("ZH"), A("ZB"), A("hi8"), OP.mult)
-    ts(A("ZW"), A("ZB"), A("r1"), OP.mult)
     zc = ts(new("tb", 144), A("uF", 0, 144), A("g7"), OP.is_equal)
     tt(A("ZC"), zc, A("ZB"), OP.add)
     ts(A("BO"), A("mG"), A("gF"), OP.is_equal)
@@ -326,11 +397,12 @@ def rank_program(g, core, T, topo):
     c4 = ts(new("tw", 1), A("rF"), 112.0, OP.add)
     ts(A("DW"), A("uF", 0, 240), c4, OP.is_equal, -2.0, OP.mult)
     ts(A("GI"), A("uF", 0, 8), A("gx"), OP.is_equal)
+    ts(A("WG"), A("GI"), A("r1"), OP.mult)
     ts(A("MX"), A("u2F"), A("gF"), OP.is_equal)
     ts(A("NM"), A("u16F"), A("rF"), OP.not_equal, -9e29, OP.mult)
     ts(A("OHb"), A("u16F"), A("rF"), OP.is_equal)
     ts(A("OHa"), A("u3F"), A("rF"), OP.is_equal)
-    ts(A("X3"), A("uF", 0, 2), 128.0, OP.mult, A("pF"), OP.add)
+    ts(A("X3"), A("uF", 0, 4), 64.0, OP.mult, A("pF"), OP.add)
     c5 = ts(new("tw", 1), A("kF"), 32.0, OP.mult, 8192.0 + 64.0, OP.add)
     ts(A("SLd"), A("uF", 0, 32), c5, OP.add)
     iota(A("PK"), [[128, 16], [1, 16]], 64, 0)
@@ -377,8 +449,8 @@ def rank_program(g, core, T, topo):
     chi = cp(new("tb", 128), A("cI"))
     clo = tt(new("tb", 128), A("cI"), chi, OP.subtract)
     for i in range(16):
-        mm([(A("psM1", i, 256, 16), A("Z2", 144 * i + 7 - k, 144 * i + 135 - k), part(c, 16 * k, 16 * k + 16)) for k in range(8) for c in (chi, clo)])
-    act(A("CK"), A("psM1", 0, 256), AF.Copy, 64.0)
+        mm([(A("psD", 256 + i, 512, 16), A("Z2", 144 * i + 7 - k, 144 * i + 135 - k), part(c, 16 * k, 16 * k + 16)) for k in range(8) for c in (chi, clo)])
+    act(A("CK"), A("psD", 256, 512), AF.Copy, 64.0)
     tW = ms(new("tb"), 0.0)
     cur = cp(new("ti"), A("OW"))
     curU = cp(new("tu"), A("OW"))
@@ -386,9 +458,9 @@ def rank_program(g, core, T, topo):
     def hashes(src, o):
         for h in range(2):
             for z, p in (("ZA", 256), ("ZH", 384)):
-                mm([(A("psD", p + 64 * h, p + 64 * h + 64), win(z, i), A("EW", src + 1024 * h + i, src + 1024 * h + 1024, 16)) for i in range(16)])
-        act(A("AGs"), A("psD", 256, 384))
-        pr = tt(new("ti", 128), A("psD", 384, 512), A("AGs"), OP.mult)
+                mm([(A("psM1", p + 64 * h, p + 64 * h + 64), win(z, i), A("EW", src + 1024 * h + i, src + 1024 * h + 1024, 16)) for i in range(16)])
+        act(A("AGs"), A("psM1", 256, 384))
+        pr = tt(new("ti", 128), A("psM1", 384, 512), A("AGs"), OP.mult)
         h1 = ts(new("ti", 128), pr, 3, OP.arith_shift_right, 1023, OP.bitwise_and)
         h2 = ts(new("ti", 128), h1, 1.0, OP.add)
         ts(part(h2, 0, 128, 8), part(pr, 0, 128, 8), 3, OP.arith_shift_right, 8191, OP.bitwise_and)
@@ -439,12 +511,13 @@ def rank_program(g, core, T, topo):
                 act(A(c), A(b, j, j + 256))
             mm([(A("psM2", 256 + 128 * h, 384 + 128 * h), A("T1", 128 * h, 128 * h + 128), A("T2", 128 * h, 128 * h + 128)) for h in range(2)])
             act(A("WO"), A("psM2", 256, 512))
-            cp(V, IND(A("WO"), A("X3")))
-            tt(part(V, 16, 32), part(V, 16, 32), ts(new("tw"), part(V, 0, 16), 0.0, OP.is_gt, BIG, OP.mult), OP.max)
+            x = ts(new("tw"), IND(A("WO"), A("X3", 0, 1)), 0.0, OP.is_gt, BIG, OP.mult)
+            cp(part(V, 0, 16), IND(A("WO"), A("X3", 0, 1)))
+            tt(part(V, 16, 32), IND(A("WO"), A("X3", 2, 3)), x, OP.max)
         b0 = tt(new("tw"), tt(new("tw"), A("naw", *s16), cur, OP.mult), A("ct", *s16), OP.add)
         for p in range(4):
             j = 512 * p
-            gt, x = A("EW", GT + j, GT + j + 512), A(("psX1", "psX2", "psX3", "psX1")[p])
+            gt, x = A("EW", GT + j, GT + j + 512), A("psX%d" % (p + 1))
             (act if JENG[t][p] == "s" else cp)(gt, IND(A("VW", 0, 8192), part(cU, 32 * p, 32 * p + 32)))
             mm([(x, A("IN"), A("EW", eb + j, eb + j + 512))], True, False)
             mm([(x, A("ID"), gt)], False, True)
@@ -452,50 +525,60 @@ def rank_program(g, core, T, topo):
             if p & 1:
                 mm([(A("psD", 32 * p - 32, 32 * p + 32), win("ZB", i), A("ad", j - 512 + i, j + 512, 16)) for i in range(16)])
         md = scan(new("tx", 128), A("M01"), A("psD", 0, 128), 0.0, OP.mult, OP.max)
-        bad = tt(A("BL", *s16), part(md, 7, 128, 8), thB, OP.is_gt)
-        badT = send(t, bad, "BR", "b")
+        ok = A("BL", 32 * t, 32 * t + 32)
+        for h in range(2):
+            tt(part(ok, 16 * h, 16 * h + 16), part(md, 7, 128, 8), thB, OP.is_le)
+        if t == 0:
+            GR[0] = send(0, A("EW", GT, GT + 2048), "GR", "c")
+        okT = send(t, ok, "BR", "b")
         X = hashes(GT, A("NG", 128 * t, 128 * t + 128))
-        for u in ((0, 1), (2,), (3,), (4,), ())[t]:
-            GR[u] = send(u, A("EW", GT, GT + 2048), "GR", "c")
-            NR[u] = send(u, X, "NR", "n")
+        if t == 0:
+            NR[0] = send(0, X, "NR", "n")
+        if not lastt:
+            GR[t + 1] = send(t + 1, A("EW", GT, GT + 2048), "GR", "c")
+            NR[t + 1] = send(t + 1, X, "NR", "n")
         if t > 0:
-            x = tt(new("psV", 128), A("psMK", 256, 384), NE, OP.mult)
+            x = tt(A("psMK", 256, 384), A("psMK", 256, 384), NE, OP.mult)
             y = tt(new("tx", 128), A("psMK", 384, 512), X, OP.mult)
             NE = tt(new("tx", 128), x, y, OP.add)
             if not lastt:
-                EL = ts(new("tu", 128), tt(new("psV", 128), A("psMK", 384, 512), A("POS"), OP.add), 2048.0, OP.mult)
+                EL = ts(new("tu", 128), tt(new("tx", 128), A("psMK", 384, 512), A("POS"), OP.add), 2048.0, OP.mult)
                 for p in range(4):
                     o = EA + EB - eb + 512 * p
                     act(A("EW", o, o + 512), IND(A("EW", eb, eb + 4096), part(EL, 32 * p, 32 * p + 32)))
         if t == YS:
-            for j in range(0, 512, 64):
-                mm([(A("psX1", j, j + 64), win("ZW", i), A("VW", 512 * i + j, 512 * i + j + 64)) for i in range(16)])
+            for j in range(0, 64, 16):
+                mm([(A("psX1", b, 512, 64), A("VW", b, 8192, 64), A("WG")) for b in range(j, j + 16)])
             act(A("YT"), A("psX1"))
             yo = (T.YY[0:128:16, 0:8192], (("YY", 0, 8192),), 8192, False, "sb")
-            op("y", lambda: g.sync.dma_start(yo[0], T.YT[:]), [yo], [A("YT")], 0.1, "yt_", 16, 3.5)
-        mk = new("tb", 64)
-        ab, cm, keep, dec = [part(mk, 16 * j, 16 * j + 16) for j in range(4)]
-        tt(ab, bad, badT, OP.max)
+
+            def spread():
+                for b in range(8):
+                    g.sync.dma_start(T.YY[16 * b:16 * b + 1, 0:8192], T.YT[:, 64 * b:64 * b + 64]).then_inc(T.sem.yt_, 16)
+            op("y", spread, [yo], [A("YT")], 0.5, "yt_", 128, 9.0)
+        mk, ncm = new("tb", 32), new("tb", 32)
+        keep, dec = part(mk, 0, 16), part(mk, 16, 32)
+        nab = tt(new("tb"), part(ok, 0, 16), part(okT, 0, 16), OP.mult)
         rdy = tt(new("tb"), A("FL", *s16), FT, OP.mult)
         if t == 0:
-            rdy = tt(new("tb"), rdy, ab, OP.is_gt)
+            rdy = tt(new("tb"), tt(new("tb"), rdy, part(ok, 0, 16), OP.mult), part(okT, 0, 16), OP.mult)
         cum = scan(new("tb"), rdy, A("z32", 0, 16), 0.0, OP.add, OP.add)
         rK = tt(new("tb"), rdy, A("K1"), OP.mult)
         off = A("psD", 128, 144)
         mm([(off, A(a), b) for a, b in (("ID", A("K1")), ("ID", A("Kr")), ("TRI", rdy), ("BO", cum), ("IN", rK))])
         offU = cp(new("tu"), off)
-        ts(cm, off, 31.5, OP.is_lt)
+        for h in range(2):
+            ts(part(ncm, 16 * h, 16 * h + 16), off, 31.5, OP.is_gt)
         act(A("SL", 0, 32), A("SLd"))
         for a, b, c in (("SM", "PK", 160), ("SL", "CK", 144)):
             act(IND(A(a), offU), A(b), AF.Silu)
             mm([(A("psD", c, c + 16), A("DL"), A(a, 0, 16)), (A("psD", c, c + 16), A("DH"), A(a, 16, 32))])
         pU, zU = [ts(new("tu"), A("psD", c, c + 16), -64.0, OP.add) for c in (160, 144)]
         CR = act(A("CR"), IND(GR[t], pU))
-        tt(keep, ab, cm, OP.is_equal)
-        tt(dec, ab, cm, OP.max)
-        vv = new("tb", 32)
-        for h in range(2):
-            tt(part(vv, 16 * h, 16 * h + 16), part(V, 16 * h, 16 * h + 16), keep, OP.mult)
+        tt(keep, nab, part(ncm, 0, 16), OP.mult)
+        act(dec, keep, AF.Copy, 1.0, -1.0)
+        m1, m2 = (okT, ncm) if t == 0 else (ncm, okT)
+        vv = tt(new("tb", 32), tt(new("tb", 32), V, tt(new("tb", 32), ok, m1, OP.mult), OP.mult), m2, OP.mult)
         tt(A("vX"), IND(vv, A("X1")), A("MX"), OP.mult)
         for h in range(2):
             o = A("psM2", 64 + 16 * h, 80 + 16 * h)
@@ -506,20 +589,27 @@ def rank_program(g, core, T, topo):
         wT = A("psM2", 96, 112)
         mm([(part(wT, 8 * h, 8 * h + 8), A("Er", 128 * h, 128 * h + 128), A("GI")) for h in range(2)])
         if not lastt:
-            thr = tt(new("tw"), tn, act(new("tw"), dec, AF.Copy, -0.5, 8.0), OP.add)
+            thr = tt(new("tw"), tn, act(new("tw"), keep, AF.Copy, 7.5, -8.0), OP.add)
             FT = send(t + 1, tt(A("FL", 16 * t + 16, 16 * t + 32), wT, thr, OP.is_ge), "FR", "f")
         wn = tt(new("tb"), wT, h1, OP.is_ge)
-        rep("psMK", 128, "ID", cm, 8)
-        x = tt(new("tx", 128), A("psMK", 128, 256), tt(new("tx", 128), NR[t], KH, OP.subtract), OP.mult)
-        y = tt(new("psV", 128), x, KH, OP.add)
-        z = tt(new("tx", 128), NE, y, OP.subtract)
-        rep("psMK", 0, "ID", ab, 8)
-        KS = tt(new("ti", 128), tt(new("tx", 128), A("psMK", 0, 128), z, OP.mult), y, OP.add)
+        KS = KH
+        picks = ((A("psMK", 128, 256), part(ncm, 0, 16), NR[t]), (A("psMK", 0, 128), nab, NE))
+        for j, (p, m, c) in enumerate(picks[::-1] if t == 0 else picks):
+            rep(p[1][0][0], p[1][0][1], "ID", m, 8)
+            tt(p, p, tt(new("tx", 128), c, KS, OP.subtract), OP.mult)
+            KS = tt(new("ti", 128) if j else p, c, p, OP.subtract)
         if not lastt:
-            rep("psMK", 256, "ID", part(mk, 32, 64), 8)
+            rep("psMK", 256, "ID", mk, 8)
         cI = ts(new("ti", 128), KS, 8191, OP.bitwise_and)
-        rep("psM2", 128, "HI", wn, 8)
-        KH = tt(new("ti", 128), tt(new("psV", 128), A("psM2", 128, 256), fm, OP.mult), KS, OP.add)
+        if lastt:
+            x = ts(A("psMK", 256, 384), KS, HELD, OP.is_ge, -3.0, OP.mult)
+            y = tt(new("tx", 128), x, ts(new("tb", 128), fm, -1.5, OP.mult, 2.0, OP.add), OP.add)
+            z = cp(new("tx", 128), IND(y, A("PO")))
+            mm([(A("psM2", 128 + 16 * k, 144 + 16 * k), A("ID"), wn) for k in range(8)], whole=A("psM2", 128, 256))
+            tt(A("oh"), A("psM2", 128, 256), z, OP.is_gt)
+        else:
+            rep("psM2", 128, "HI", wn, 8)
+            KH = tt(new("ti", 128), tt(A("psM2", 128, 256), A("psM2", 128, 256), fm, OP.mult), KS, OP.add)
         ct = new("tb", 32)
         tt(part(ct, 0, 16), nx, keep, OP.mult)
         if lastt:
@@ -540,14 +630,13 @@ def rank_program(g, core, T, topo):
         if lastt:
             tt(A("ol"), a, sb, OP.add)
             cp(A("oc"), IND(cI, A("PO")))
-            ts(A("oh"), IND(KH, A("PO")), HELD, OP.is_ge)
         else:
             cur = tt(new("ti"), a, sb, OP.add)
             curU = cp(new("tu"), cur)
             cU = cp(new("tu", 128), cI)
             act(A("thR", 1, 257), A("psM1", 256, 512), AF.Copy, t + 0.5, -1.0)
-            thB = act(new("tw"), dec, AF.Copy, 200.0, 100000.0)
-            n = tt(new("tw"), tt(new("tw"), n, wn, OP.subtract), act(new("tw"), dec, AF.Copy, 0.0, 8.0), OP.max)
+            thB = act(new("tw"), keep, AF.Copy, 100200.0, -100000.0)
+            n = tt(new("tw"), tt(new("tw"), n, wn, OP.subtract), act(new("tw"), keep, AF.Copy, 8.0, -8.0), OP.max)
             l = cp(new("tu"), tt(new("tw"), tt(new("tw"), pre, wn, OP.mult), A("J16"), OP.add))
             act(IND(A("TT"), l), A("WHT", 256 * t + 256, 256 * t + 512), AF.Silu)
             cp(IND(A("VW"), zU), CR)
@@ -612,7 +701,7 @@ def rank_program(g, core, T, topo):
             waits(e, o["rd"], False)
             waits(e, o["wr"], True)
             x = o["call"]()
-            if sem != "lsem":
+            if sem not in ("lsem", "yt_"):
                 x.then_inc(T.sem[sem], o["inc"])
         else:
             lst, first, last = o["mm"]

@@ -22,23 +22,25 @@ _buf("Z2", 16 * 144, B)
 _buf("EQ", 4096, B)
 _buf("pI rI gI kI bI", 1, I)
 _buf("pF rF gF g15 g7 lo8 hi8 r1 kF bF gx", 1, F)
-_buf("uF CK PK ys8 u16F u2F", 256, F)
+_buf("uF PK ys8 u16F u2F", 256, F)
+_buf("CK", 288, F)
 _buf("mI mG cI hI", 128, I)
-_buf("ZB ZA ZH ZC", 144, B)
+_buf("ZB ZA ZH ZX ZC", 144, B)
 _buf("BO ID IN LL TRI WY HI wr", 128, B)
-_buf("DL DH JO POS M01 RS HS AGs oc oh iA iB", 128, F)
+_buf("DL DH JO POS M01 RS HS oc oh iA iB", 128, F)
 _buf("DW", 240, B)
 _buf("GI WG", 8, B)
 _buf("RM OW J16 o8 o64 wT ol", 16, F)
 _buf("K1 Kr", 16, B)
-_buf("MX NM OHa OHb G1 G2 T1 T2 WO vX Er tau vR cdR yR u3F", 256, B)
-_buf("waR", 1024, B)
+_buf("MX NM OHb G1 G2 T1 T2 WO vX Er tau vR cdR yR u3F", 256, B)
+_buf("OHa", 512, B)
+_buf("wc", 1, F)
 _buf("X3", 4, U16)
 _buf("SL SM", 768, F)
-_buf("SLd P01", 32, F)
+_buf("P01", 32, F)
 _buf("WHT", 256 * NS, F)
 _buf("thR", 272, B)
-_buf("aw8 naw ct", 16 * NS, F)
+_buf("naw ct", 16 * NS, F)
 _buf("awI", 16 * NS, I)
 _buf("z32", 32, B)
 _buf("wI", 16, I)
@@ -46,10 +48,10 @@ _buf("cfR", 256, U16)
 _buf("PI PO", 8, U16)
 _buf("X1 X2", 16, U16)
 _buf("YT", 512, F)
-_buf("tw", 3600, F)
+_buf("tw", 3900, F)
 _buf("tx", 2000, F)
 _buf("ti", 4200, I)
-_buf("tb", 3000, B)
+_buf("tb", 3600, B)
 _buf("tu", 1800, U16)
 _buf("FL FR wa", 16 * NS, B)
 _buf("BL BR", 32 * NS, B)
@@ -61,10 +63,12 @@ for _n in ("X1", "X2", "X3", "X4", "D", "MK", "M1", "M2"):
 LOADS = ["dcs", "dho", "dwk", "dsn", "dx"]
 SEMAPHORES = ["sv", "ss", "st", "sg", "lsem", "oc_", "oh_", "ol_", "oy_", "yt_"] + LOADS + [k + str(t) for k in "fbncl" for t in range(NS)]
 CY, PE = 0.00083, 0.00042
-CASES = ((1.0, 1.04, 1.0, 0.3, 0.2, 2.7, 0.8), (1.1, 1.04, 1.0, 0.25, 0.15, 3.0, 0.8), (1.5, 1.33, 1.58, 0.2, 0.2, 3.0, 0.8))
-MID = (1.05, 1.04, 1.0, 0.3, 0.2, 2.8, 0.8)
-MOVES, SEED = 1500, 3
-PASSES, SHAKE = 150, 1.0
+CASES = ((1.0, 1.04, 1.0, 0.25, 0.25, 2.45, 0.8), (1.2, 1.04, 1.0, 0.3, 0.2, 2.7, 0.8), (1.0, 1.04, 1.0, 0.15, 0.1, 3.9, 1.0), (1.5, 1.33, 1.58, 0.2, 0.2, 3.0, 0.8))
+MID = (1.05, 1.04, 1.0, 0.3, 0.2, 2.8, 0.8, 4.0)
+OUTS = ("oc_", "oh_", "ol_", "oy_")
+NEAR, RUN, KEPT = 15, 45, 4
+MOVES, SEED = 1000, 8
+PASSES, SHAKE = 360, 1.0
 YS = 3
 JENG = ("vsvs",) * NS
 
@@ -75,15 +79,17 @@ PLAN = []
 def plan(ops, deps):
     n = len(ops)
 
-    def times(f, ga, sc, wake, same, far, slow):
+    def times(f, ga, sc, wake, same, far, slow, early=0.0):
         cost = [o["cost"] * (slow if o["e"] == "a" else 1.0 if o["sem"] == "lsem" or o["arr"] else f) * {"ga": ga, "sc": sc}.get(o["kind"], 1.0) for o in ops]
-        tail = [(o["arr"] or 0.0) * slow for o in ops]
+        tail = [(o["arr"] or 0.0) * (0.8 if "load" in o else slow) for o in ops]
         pred, succ = [[] for _ in range(n)], [[] for _ in range(n)]
         for i in range(n):
             for k in deps[i]:
                 a, b = ops[k], ops[i]
                 d = (0.0 if a["e"] == b["e"] and a["e"] in "tga" else far - 0.8 if b["e"] == "a" else tail[k] if a["arr"]
                      else same if a["e"] == b["e"] else wake)
+                if b["e"] == "t" and a["wr"] and a["wr"][0][0] == "EQ":
+                    d += early
                 pred[i].append((k, d))
                 succ[k].append((i, d))
         return cost, pred, succ, tail, wake
@@ -111,26 +117,46 @@ def plan(ops, deps):
         return at
 
     def replay(order, case):
-        cost, pred, _succ, tail, wake = case
-        free, bank, at = {}, {}, [0.0] * n
+        cost, pred, succ, tail, wake = case
+        free, bank, at, done = dict.fromkeys("vstgya", 0.0), {}, [0.0] * n, [0.0] * n
         for i in order:
-            e = ops[i]["e"]
-            s = max([free.get(e, 0.0)] + [at[k] + cost[k] + d for k, d in pred[i]]
-                    + [bank[b][1] + wake for b in ops[i]["banks"] if b in bank and bank[b][0] != e])
+            e = who[i]
+            s = free[e]
+            for k, d in pred[i]:
+                if done[k] + d > s:
+                    s = done[k] + d
+            for b in banks[i]:
+                x = bank.get(b)
+                if x and x[0] != e and x[1] > s:
+                    s = x[1]
             at[i] = s
-            free[e] = s + cost[i]
-            for b in ops[i]["banks"]:
-                bank[b] = (e, s + cost[i])
-        return at, max(at[i] + cost[i] + tail[i] for i in range(n))
+            free[e] = done[i] = s = s + cost[i]
+            for b in banks[i]:
+                bank[b] = (e, s + wake)
+        return at, max(done[i] + tail[i] for i in ends), sum(at[i] for i in marks) / len(marks)
+
+    who, banks = [o["e"] for o in ops], [sorted(o["banks"]) for o in ops]
+    ends = set(range(n)).difference(*deps)
+    marks = [i for i in range(n) if ops[i]["sem"] in OUTS or (ops[i]["e"] == "a" and ops[i]["sem"][0] in "fb")]
 
     cases = [times(*c) for c in CASES]
     cost, pred, succ, tail, wake = times(*MID)
     prio = [0.0] * n
     for i in range(n - 1, -1, -1):
         prio[i] = cost[i] + max([d + prio[k] for k, d in succ[i]] + [tail[i]])
-    best, short, seed = None, None, SEED
+    est = [0.0] * n
+    for i in range(n):
+        est[i] = max([0.0] + [est[k] + cost[k] + d for k, d in pred[i]])
+    first = [0.5 * (prio[i] - est[i]) for i in range(n)]
+    pool, seed = [], SEED
     for p in range(PASSES):
-        if p % 3 == 0 and short:
+        if p % RUN == 0:
+            best, short = None, None
+            pool.append(None)
+            for i in range(n):
+                seed = (seed * 1103515245 + 12345) % 2147483648
+                prio[i] = first[i] + SHAKE * seed / 2147483648
+        elif p % 3 == 0:
             for i in range(n):
                 seed = (seed * 1103515245 + 12345) % 2147483648
                 prio[i] = SHAKE * seed / 2147483648 - short[1][i]
@@ -141,28 +167,67 @@ def plan(ops, deps):
         order = sorted(range(n), key=lambda i: (at[i], i))
         score = sum(math.log(replay(order, c)[1]) for c in cases)
         if best is None or score < best[0]:
-            best = (score, order)
+            best = pool[-1] = (score, order)
         back = place(succ, [-at[i] - cost[i] for i in range(n)], [0.0 if succ[i] else tail[i] for i in range(n)], range(n - 1, -1, -1), cost, wake)
         prio = [back[i] + cost[i] for i in range(n)]
-    order, score = best[1], best[0]
-    for p in range(MOVES):
+
+    def cross(pool):
+        best = min(pool)
+        for _s, other in pool + pool:
+            for cut in range(100, n - 50, 25):
+                for a, b in ((best[1], other), (other, best[1])):
+                    head = set(a[:cut])
+                    order = a[:cut] + [i for i in b if i not in head]
+                    best = min(best, (rate(order)[1], order))
+        return best
+
+    def rate(order):
+        r = [replay(order, c) for c in cases]
+        return sum(math.log(x[1] + x[2]) for x in r), sum(math.log(x[1]) for x in r)
+    pool = [cross(pool)] + sorted(pool)[:KEPT - 1]
+    for p in range((KEPT + 2) * MOVES):
+        if p % MOVES == 0 and p <= KEPT * MOVES:
+            if p:
+                pool[p // MOVES - 1] = best
+            best = pool[p // MOVES] if p < KEPT * MOVES else cross(pool)
+            order, score = best[1], rate(best[1])[0]
         cost, pred, succ, tail, wake = cases[p % len(cases)]
-        at = replay(order, cases[p % len(cases)])[0]
+        at, now, x = replay(order, cases[p % len(cases)])
+        now += x
+        if p % 50 == 49:
+            for q in range(2):
+                at = place(pred, [(-1e6 + i if "load" in ops[i] else at[i]) for i in range(n)], [0.0] * n, range(n), cost, wake)
+                new = sorted(range(n), key=lambda i: (at[i], i))
+                s, hard = rate(new)
+                if s <= score:
+                    order, score = new, s
+                    if hard < best[0]:
+                        best = (hard, new)
+                at = place(succ, [-at[i] - cost[i] for i in range(n)], [0.0 if succ[i] else tail[i] for i in range(n)], range(n - 1, -1, -1), cost, wake)
+                at = [-at[i] - cost[i] for i in range(n)]
+            continue
         pos, last, arcs = {}, {}, []
         for j, i in enumerate(order):
             pos[i] = (j, [last[r] for r in [ops[i]["e"]] + sorted(ops[i]["banks"]) if r in last])
             for r in [ops[i]["e"]] + sorted(ops[i]["banks"]):
                 last[r] = i
-        i = max(range(n), key=lambda i: at[i] + cost[i] + tail[i])
+        seed = (seed * 1103515245 + 12345) % 2147483648
+        i = marks[seed // 1024 % len(marks)]
         while at[i] > 0:
             k = max(pred[i], key=lambda x: at[x[0]] + cost[x[0]] + x[1], default=None)
             if k is None or at[k[0]] + cost[k[0]] + k[1] < at[i] - 1e-9:
                 k = (max(pos[i][1], key=lambda x: at[x] + cost[x] + (wake if ops[x]["e"] != ops[i]["e"] else 0.0)),)
                 arcs.append((k[0], i))
             i = k[0]
-        for _ in range(8):
+        for _ in range(min(8, len(arcs))):
             seed = (seed * 1103515245 + 12345) % 2147483648
-            a, b = arcs[seed // 64 % len(arcs)]
+            a, b = arcs[seed // 64 % min(len(arcs), NEAR)]
+            if seed & 48 == 48:
+                r = max([0.0] + [at[k] + cost[k] + d for k, d in pred[b]])
+                j = pos[a][0]
+                while j > 0 and (who[order[j]] != who[b] or at[order[j]] + (cost[order[j]] if seed & 2048 else 0.0) > r):
+                    a = order[j] if who[order[j]] == who[b] else a
+                    j -= 1
             if "load" in ops[a]:
                 continue
             mid = order[pos[a][0]:pos[b][0] + 1]
@@ -183,11 +248,14 @@ def plan(ops, deps):
                     continue
                 mid = [i for i in mid if i not in need] + [i for i in mid if i in need]
             new = order[:pos[a][0]] + mid + order[pos[b][0] + 1:]
-            s = sum(math.log(replay(new, c)[1]) for c in cases)
-            if s <= score + 0.0005:
+            x = replay(new, cases[p % len(cases)])
+            if x[1] + x[2] > now + 0.02:
+                continue
+            s, hard = rate(new)
+            if s <= score + 0.0001:
                 order, score = new, s
-                if s < best[0]:
-                    best = (s, new)
+                if hard < best[0]:
+                    best = (hard, new)
                 break
     return best[1]
 
@@ -248,7 +316,7 @@ def rank_program(g, core, T, topo):
         return o
 
     def scan(o, a, b, init, f0, f1):
-        op("v", lambda: g.vector.tensor_tensor_scan(o[0], a[0], b[0], init, f0, f1), [o], [a, b], max(64, a[2]) * CY)
+        op("v", lambda: g.vector.tensor_tensor_scan(o[0], a[0], b[0], init, f0, f1), [o], [a, b], max(64, a[2] / (2 if o[3] and a[3] and b[3] else 1)) * CY)
         return o
 
     def ms(o, v):
@@ -257,7 +325,9 @@ def rank_program(g, core, T, topo):
 
     def act(o, a, func=AF.Copy, bias=0.0, scale=1.0):
         c = 0.065 + a[2] * (3.8 if o[4] == "ind" else 1.5) * CY if "ind" in (o[4], a[4]) else max(64, a[2]) * CY
-        if bias == 0.0 and scale == 1.0:
+        if isinstance(scale, tuple):
+            op("s", lambda: g.scalar.activation(o[0], a[0], func, scale=scale[0]), [o], [a, scale], c)
+        elif bias == 0.0 and scale == 1.0:
             op("s", lambda: g.scalar.activation(o[0], a[0], func), [o], [a], c)
         else:
             op("s", lambda: g.scalar.activation(o[0], a[0], func, bias=bias, scale=scale), [o], [a], c)
@@ -378,6 +448,7 @@ def rank_program(g, core, T, topo):
     ts(A("ZB"), A("uF", 0, 144), A("g15"), OP.is_equal)
     ts(A("ZA"), A("ZB"), A("lo8"), OP.mult)
     ts(A("ZH"), A("ZB"), A("hi8"), OP.mult)
+    ts(A("ZX"), A("ZB"), ts(new("tw", 1), A("hi8"), 2047.0, OP.mult, 1.0, OP.add), OP.mult)
     zc = ts(new("tb", 144), A("uF", 0, 144), A("g7"), OP.is_equal)
     tt(A("ZC"), zc, A("ZB"), OP.add)
     ts(A("BO"), A("mG"), A("gF"), OP.is_equal)
@@ -401,10 +472,12 @@ def rank_program(g, core, T, topo):
     ts(A("MX"), A("u2F"), A("gF"), OP.is_equal)
     ts(A("NM"), A("u16F"), A("rF"), OP.not_equal, -9e29, OP.mult)
     ts(A("OHb"), A("u16F"), A("rF"), OP.is_equal)
-    ts(A("OHa"), A("u3F"), A("rF"), OP.is_equal)
+    ts(A("OHa", 0, 256), A("u3F"), A("rF"), OP.is_equal)
+    ms(A("OHa", 256, 512), 0.0)
+    ts(A("u3F"), A("u16F"), 0.0, OP.is_gt)
     ts(A("X3"), A("uF", 0, 4), 64.0, OP.mult, A("pF"), OP.add)
     c5 = ts(new("tw", 1), A("kF"), 32.0, OP.mult, 8192.0 + 64.0, OP.add)
-    ts(A("SLd"), A("uF", 0, 32), c5, OP.add)
+    ts(A("CK", 256, 288), A("uF", 0, 32), c5, OP.add)
     iota(A("PK"), [[128, 16], [1, 16]], 64, 0)
     ts(A("PK"), A("PK"), ts(new("tw", 1), A("kF"), 16.0, OP.mult), OP.add)
     ms(A("SM", 0, 32), 64.0)
@@ -422,16 +495,15 @@ def rank_program(g, core, T, topo):
         ts(A("awI", *s), A("wI"), t, OP.arith_shift_right, 1, OP.bitwise_and)
         c8 = ts(new("tw", 1), A("hi8"), t - 1.0, OP.mult, 33.0, OP.add)
         ts(A("WHT", 256 * t, 256 * t + 256), A("uF"), A("lo8"), OP.mult, c8, OP.add)
-    ts(A("aw8"), A("awI"), 0.125, OP.mult)
     ts(A("naw"), A("awI"), -1.0, OP.mult, 1.0, OP.add)
     o1 = ts(new("tw"), A("OW"), 1.0, OP.add)
     for t in range(NS):
         s = (16 * t, 16 * t + 16)
         tt(A("ct", *s), A("naw", *s), o1, OP.subtract)
-        tt(A("wa", *s), A("awI", *s), A("wT"), OP.mult)
-    for h in range(2):
-        to_r("psMK", [A("wa", 16 + 32 * h, 48 + 32 * h)])
-        act(A("waR", 512 * h, 512 * h + 512), A("psMK"))
+    tt(A("wa", 0, 16), A("awI", 0, 16), A("wT"), OP.mult)
+    ts(A("wa", 16, 16 * NS), A("naw", 16, 16 * NS), 256.0, OP.mult)
+    mm([(A("psM2", 8, 9), A("wr"), A("ID", 0, 1))])
+    cp(A("wc"), A("psM2", 8, 9))
 
     x = ts(new("tx", 128), IND(A("hI"), A("PI")), HELD, OP.mult, BASE, OP.add)
     KH = tt(new("ti", 128), IND(A("cI"), A("PI")), x, OP.add)
@@ -450,17 +522,16 @@ def rank_program(g, core, T, topo):
     clo = tt(new("tb", 128), A("cI"), chi, OP.subtract)
     for i in range(16):
         mm([(A("psD", 256 + i, 512, 16), A("Z2", 144 * i + 7 - k, 144 * i + 135 - k), part(c, 16 * k, 16 * k + 16)) for k in range(8) for c in (chi, clo)])
-    act(A("CK"), A("psD", 256, 512), AF.Copy, 64.0)
+    act(A("CK", 0, 256), A("psD", 256, 512), AF.Copy, 64.0)
     tW = ms(new("tb"), 0.0)
     cur = cp(new("ti"), A("OW"))
     curU = cp(new("tu"), A("OW"))
 
     def hashes(src, o):
         for h in range(2):
-            for z, p in (("ZA", 256), ("ZH", 384)):
-                mm([(A("psM1", p + 64 * h, p + 64 * h + 64), win(z, i), A("EW", src + 1024 * h + i, src + 1024 * h + 1024, 16)) for i in range(16)])
-        act(A("AGs"), A("psM1", 256, 384))
-        pr = tt(new("ti", 128), A("psM1", 384, 512), A("AGs"), OP.mult)
+            mm([(A("psM1", 256 + 64 * h, 320 + 64 * h), win("ZX", i), A("EW", src + 1024 * h + i, src + 1024 * h + 1024, 16)) for i in range(16)])
+        xi = cp(new("ti", 128), A("psM1", 256, 384))
+        pr = tt(new("ti", 128), ts(new("ti", 128), xi, 11, OP.arith_shift_right), ts(new("ti", 128), xi, 2047, OP.bitwise_and), OP.mult)
         h1 = ts(new("ti", 128), pr, 3, OP.arith_shift_right, 1023, OP.bitwise_and)
         h2 = ts(new("ti", 128), h1, 1.0, OP.add)
         ts(part(h2, 0, 128, 8), part(pr, 0, 128, 8), 3, OP.arith_shift_right, 8191, OP.bitwise_and)
@@ -504,11 +575,11 @@ def rank_program(g, core, T, topo):
             ts(part(V, 16, 24), A("wa", 0, 8), 0.0, OP.is_gt, BIG, OP.mult)
             cp(part(V, 24, 32), A("wa", 8, 16))
         else:
-            tt(A("G1"), IND(A("OHb"), curU), A("waR", 256 * t - 256, 256 * t), OP.mult)
-            act(A("G2"), IND(A("OHa"), curU))
+            act(A("G1"), IND(A("OHb"), curU))
+            act(A("G2"), IND(A("OHa"), cp(new("tu"), tt(new("tw"), cur, A("wa", *s16), OP.add))))
             for a, b, j, c in (("G1", "psM2", 256, "T1"), ("G2", "psMK", 0, "T2")):
                 mm([(A(b, j + 128 * h, j + 128 + 128 * h), A(a, 128 * h, 128 * h + 128), A("ID")) for h in range(2)])
-                act(A(c), A(b, j, j + 256))
+                act(A(c), A(b, j, j + 256), AF.Copy, 0.0, A("wc") if c == "T1" else 1.0)
             mm([(A("psM2", 256 + 128 * h, 384 + 128 * h), A("T1", 128 * h, 128 * h + 128), A("T2", 128 * h, 128 * h + 128)) for h in range(2)])
             act(A("WO"), A("psM2", 256, 512))
             x = ts(new("tw"), IND(A("WO"), A("X3", 0, 1)), 0.0, OP.is_gt, BIG, OP.mult)
@@ -569,17 +640,24 @@ def rank_program(g, core, T, topo):
         offU = cp(new("tu"), off)
         for h in range(2):
             ts(part(ncm, 16 * h, 16 * h + 16), off, 31.5, OP.is_gt)
-        act(A("SL", 0, 32), A("SLd"))
-        for a, b, c in (("SM", "PK", 160), ("SL", "CK", 144)):
-            act(IND(A(a), offU), A(b), AF.Silu)
+        act(A("SL", 0, 32), A("CK", 256, 288))
+        act(IND(A("SM"), offU), A("PK"), AF.Silu)
+        if t == 0:
+            cp(IND(A("SL"), offU), A("CK", 0, 256))
+        else:
+            act(IND(A("SL"), offU), A("CK", 0, 256), AF.Silu)
+        for a, c in (("SM", 160), ("SL", 144)):
             mm([(A("psD", c, c + 16), A("DL"), A(a, 0, 16)), (A("psD", c, c + 16), A("DH"), A(a, 16, 32))])
         pU, zU = [ts(new("tu"), A("psD", c, c + 16), -64.0, OP.add) for c in (160, 144)]
         CR = act(A("CR"), IND(GR[t], pU))
         tt(keep, nab, part(ncm, 0, 16), OP.mult)
         act(dec, keep, AF.Copy, 1.0, -1.0)
         m1, m2 = (okT, ncm) if t == 0 else (ncm, okT)
-        vv = tt(new("tb", 32), tt(new("tb", 32), V, tt(new("tb", 32), ok, m1, OP.mult), OP.mult), m2, OP.mult)
-        tt(A("vX"), IND(vv, A("X1")), A("MX"), OP.mult)
+        vv = tt(new("tb", 32), V, tt(new("tb", 32), ok, m1, OP.mult), OP.mult)
+        if lastt:
+            tt(A("vX"), IND(m2, A("X1")), tt(A("G1"), IND(vv, A("X1")), A("MX"), OP.mult), OP.mult)
+        else:
+            tt(A("vX"), IND(tt(new("tb", 32), vv, m2, OP.mult), A("X1")), A("MX"), OP.mult)
         for h in range(2):
             o = A("psM2", 64 + 16 * h, 80 + 16 * h)
             mm([(o, A("EQ", 256 * q + 128 * h, 256 * q + 128 * h + 128), A("vX", 16 * q, 16 * q + 16)) for q in range(16)]
@@ -587,11 +665,11 @@ def rank_program(g, core, T, topo):
         mn = scan(new("tb", 32), A("P01"), A("psM2", 64, 96), 0.0, OP.mult, OP.min)
         tt(A("Er"), IND(mn, A("X2")), A("NM"), OP.is_lt)
         wT = A("psM2", 96, 112)
-        mm([(part(wT, 8 * h, 8 * h + 8), A("Er", 128 * h, 128 * h + 128), A("GI")) for h in range(2)])
         if not lastt:
+            mm([(part(wT, 8 * h, 8 * h + 8), A("Er", 128 * h, 128 * h + 128), A("GI")) for h in range(2)])
             thr = tt(new("tw"), tn, act(new("tw"), keep, AF.Copy, 7.5, -8.0), OP.add)
             FT = send(t + 1, tt(A("FL", 16 * t + 16, 16 * t + 32), wT, thr, OP.is_ge), "FR", "f")
-        wn = tt(new("tb"), wT, h1, OP.is_ge)
+            wn = tt(new("tb"), wT, h1, OP.is_ge)
         KS = KH
         picks = ((A("psMK", 128, 256), part(ncm, 0, 16), NR[t]), (A("psMK", 0, 128), nab, NE))
         for j, (p, m, c) in enumerate(picks[::-1] if t == 0 else picks):
@@ -602,14 +680,17 @@ def rank_program(g, core, T, topo):
             rep("psMK", 256, "ID", mk, 8)
         cI = ts(new("ti", 128), KS, 8191, OP.bitwise_and)
         if lastt:
-            x = ts(A("psMK", 256, 384), KS, HELD, OP.is_ge, -3.0, OP.mult)
-            y = tt(new("tx", 128), x, ts(new("tb", 128), fm, -1.5, OP.mult, 2.0, OP.add), OP.add)
-            z = cp(new("tx", 128), IND(y, A("PO")))
-            mm([(A("psM2", 128 + 16 * k, 144 + 16 * k), A("ID"), wn) for k in range(8)], whole=A("psM2", 128, 256))
+            x = ts(A("psMK", 256, 384), KS, HELD, OP.is_ge, -5.0, OP.mult)
+            rep("psD", 256, "ID", ts(new("tb"), h1, 2.0, OP.mult), 8)
+            y = tt(new("tx", 128), A("psD", 256, 384), ts(new("tb", 128), fm, -1.5, OP.mult), OP.add)
+            z = cp(new("tx", 128), IND(tt(new("tx", 128), x, y, OP.add), A("PO")))
+            mm([(A("psM2", 128 + 16 * k + 8 * h, 136 + 16 * k + 8 * h), A("Er", 128 * h, 128 * h + 128), A("GI")) for h in range(2) for k in range(8)],
+               whole=A("psM2", 128, 256))
             tt(A("oh"), A("psM2", 128, 256), z, OP.is_gt)
         else:
-            rep("psM2", 128, "HI", wn, 8)
-            KH = tt(new("ti", 128), tt(A("psM2", 128, 256), A("psM2", 128, 256), fm, OP.mult), KS, OP.add)
+            rep("psD", 256, "HI", wn, 8)
+            KH = A("psD", 256, 384)
+            tt(KH, tt(KH, KH, fm, OP.mult), KS, OP.add)
         ct = new("tb", 32)
         tt(part(ct, 0, 16), nx, keep, OP.mult)
         if lastt:
@@ -618,14 +699,14 @@ def rank_program(g, core, T, topo):
             tW = tt(part(ct, 16, 32), act(new("tb"), tW, AF.Copy, 1.0), keep, OP.mult)
             to_r("psM1", [ct])
         act(A("cdR"), A("psM1", 0, 256), AF.Copy, 0.0, 1.0 / 64)
-        act(A("yR"), IND(A("cdR"), curU))
-        y8 = A("psM2", 112, 128)
-        to_w(y8, A("yR"), "ZA")
-        a = tt(new("tw"), tt(new("tw"), y8, A("aw8", *s16), OP.mult), A("OW"), OP.add)
+        tt(A("yR"), IND(A("cdR"), curU), A("OHb"), OP.mult)
+        y8 = part(scan(new("tb", 256), A("u3F"), A("yR"), 0.0, OP.mult, OP.add), 15, 256, 16)
+        a = tt(new("tw"), tt(new("tw"), y8, A("awI", *s16), OP.mult), A("OW"), OP.add)
         sb = tt(new("tw"), ts(new("tw"), y8, 0.0, OP.is_gt), b0, OP.mult)
         if t >= YS:
-            mm([(A("psM2", 256, 512), A("WY"), CR)])
-            act(A("ys8"), A("psM2", 256, 512))
+            x = A("psX2" if lastt else "psM2", 256, 512)
+            mm([(x, A("WY"), CR)])
+            act(A("ys8"), x)
             cp(IND(A("YY"), zU), A("ys8"))
         if lastt:
             tt(A("ol"), a, sb, OP.add)
@@ -641,7 +722,7 @@ def rank_program(g, core, T, topo):
             act(IND(A("TT"), l), A("WHT", 256 * t + 256, 256 * t + 512), AF.Silu)
             cp(IND(A("VW"), zU), CR)
     for e, sem, tout, o in (("s", "oc_", T.yc[:], A("oc")), ("s", "ol_", T.yl[:], A("ol")), ("y", "oh_", T.yh[:], A("oh")), ("y", "oy_", T.ys[:], yo)):
-        (lambda e, sem, tout, o: op(e, lambda: eng[e].dma_start(tout, o[0]), [], [o], 0.1, sem, 16, 2.5))(e, sem, tout, o)
+        (lambda e, sem, tout, o: op(e, lambda: eng[e].dma_start(tout, o[0]), [], [o], 0.1, sem, 16, 5.5 if sem == "oy_" else 3.0))(e, sem, tout, o)
 
     n = len(ops)
     deps = [set() for _ in range(n)]

import math
from concourse.mybir import AluOpType as OP, ActivationFunctionType as AF

NS = 5
EA, EB = 0, 4096
F, B, I, U16 = "float32", "bfloat16", "int32", "uint16"
BASE, HELD = 131072.0, 262144.0
BIG = 2.0 ** 95
SCRATCH = {}


def _buf(names, n, d):
    for x in names.split():
        SCRATCH[x] = ("sbuf", [128, n], d)


_buf("VW", 8448, B)
_buf("EW", 8192, B)
_buf("TT YY", 8448, F)
_buf("ad WR", 2048, B)
_buf("Z2", 16 * 144, B)
_buf("EQ", 4096, B)
_buf("pI rI gI kI bI", 1, I)
_buf("pF rF gF g15 g7 lo8 hi8 r1 kF bF gx", 1, F)
_buf("uF PK ys8 u16F u2F", 256, F)
_buf("CK", 288, F)
_buf("mI mG cI hI", 128, I)
_buf("ZB ZA ZH ZX ZC", 144, B)
_buf("BO ID IN LL TRI WY HI wr", 128, B)
_buf("DL DH JO POS M01 RS HS oc oh iA iB", 128, F)
_buf("DW", 240, B)
_buf("GI WG", 8, B)
_buf("RM OW J16 o8 o64 wT ol", 16, F)
_buf("K1 Kr", 16, B)
_buf("MX NM OHb G1 G2 T1 T2 WO vX Er tau vR cdR yR u3F", 256, B)
_buf("OHa", 512, B)
_buf("wc", 1, F)
_buf("X3", 4, U16)
_buf("SL SM", 768, F)
_buf("P01", 32, F)
_buf("WHT", 256 * NS, F)
_buf("thR", 272, B)
_buf("naw ct", 16 * NS, F)
_buf("awI", 16 * NS, I)
_buf("z32", 32, B)
_buf("wI", 16, I)
_buf("cfR", 256, U16)
_buf("PI PO", 8, U16)
_buf("X1 X2", 16, U16)
_buf("YT", 512, F)
_buf("tw", 3900, F)
_buf("tx", 2000, F)
_buf("ti", 4200, I)
_buf("tb", 3600, B)
_buf("tu", 1800, U16)
_buf("FL FR wa", 16 * NS, B)
_buf("BL BR", 32 * NS, B)
_buf("NG NR", 128 * NS, F)
_buf("CR", 256, B)
_buf("GR", 2048 * NS, B)
for _n in ("X1", "X2", "X3", "X4", "D", "MK", "M1", "M2"):
    SCRATCH["ps" + _n] = ("psum", [128, 512], F)
LOADS = ["dcs", "dho", "dwk", "dsn", "dx"]
SEMAPHORES = ["sv", "ss", "st", "sg", "lsem", "oc_", "oh_", "ol_", "oy_", "yt_"] + LOADS + [k + str(t) for k in "fbncl" for t in range(NS)]
CY, PE = 0.00083, 0.00042
CASES = ((1.0, 1.04, 1.0, 0.25, 0.25, 2.45, 0.8), (1.2, 1.04, 1.0, 0.3, 0.2, 2.7, 0.8), (1.0, 1.04, 1.0, 0.15, 0.1, 3.9, 1.0), (1.5, 1.33, 1.58, 0.2, 0.2, 3.0, 0.8))
MID = (1.05, 1.04, 1.0, 0.3, 0.2, 2.8, 0.8, 4.0)
OUTS = ("oc_", "oh_", "ol_", "oy_")
NEAR, RUN, KEPT = 15, 45, 4
MOVES, SEED = 1000, 8
PASSES, SHAKE = 360, 1.0
YS = 3
JENG = ("vsvs",) * NS


PLAN = []


def plan(ops, deps):
    n = len(ops)

    def times(f, ga, sc, wake, same, far, slow, early=0.0):
        cost = [o["cost"] * (slow if o["e"] == "a" else 1.0 if o["sem"] == "lsem" or o["arr"] else f) * {"ga": ga, "sc": sc}.get(o["kind"], 1.0) for o in ops]
        tail = [(o["arr"] or 0.0) * (0.8 if "load" in o else slow) for o in ops]
        pred, succ = [[] for _ in range(n)], [[] for _ in range(n)]
        for i in range(n):
            for k in deps[i]:
                a, b = ops[k], ops[i]
                d = (0.0 if a["e"] == b["e"] and a["e"] in "tga" else far - 0.8 if b["e"] == "a" else tail[k] if a["arr"]
                     else same if a["e"] == b["e"] else wake)
                if b["e"] == "t" and a["wr"] and a["wr"][0][0] == "EQ":
                    d += early
                pred[i].append((k, d))
                succ[k].append((i, d))
        return cost, pred, succ, tail, wake

    def place(before, key, head, text, cost, wake):
        lanes = [[(o["e"], 0.0)] + [(b, wake) for b in sorted(o["banks"])] for o in ops]
        for i in text:
            key[i] = max([key[i]] + [key[k] + 1e-6 for k, _d in before[i]])
        busy, at = {}, [0.0] * n
        for i in sorted(text, key=lambda i: key[i]):
            e, c = ops[i]["e"], cost[i]
            s = max([head[i]] + [at[k] + cost[k] + d for k, d in before[i]])
            moved = True
            while moved:
                moved = False
                for r, w in lanes[i]:
                    for u in range(int(s - w), int(s + c + w) + 1):
                        for a, b, e2 in busy.get((r, u), ()):
                            if (not w or e2 != e) and a - w < s + c - 1e-9 and s + 1e-9 < b + w:
                                s, moved = b + w, True
            at[i] = s
            for r, _w in lanes[i]:
                for u in range(int(s), int(s + c) + 1):
                    busy.setdefault((r, u), []).append((s, s + c, e))
        return at

    def replay(order, case):
        cost, pred, succ, tail, wake = case
        free, bank, at, done = dict.fromkeys("vstgya", 0.0), {}, [0.0] * n, [0.0] * n
        for i in order:
            e = who[i]
            s = free[e]
            for k, d in pred[i]:
                if done[k] + d > s:
                    s = done[k] + d
            for b in banks[i]:
                x = bank.get(b)
                if x and x[0] != e and x[1] > s:
                    s = x[1]
            at[i] = s
            free[e] = done[i] = s = s + cost[i]
            for b in banks[i]:
                bank[b] = (e, s + wake)
        return at, max(done[i] + tail[i] for i in ends), sum(at[i] for i in marks) / len(marks)

    who, banks = [o["e"] for o in ops], [sorted(o["banks"]) for o in ops]
    ends = set(range(n)).difference(*deps)
    marks = [i for i in range(n) if ops[i]["sem"] in OUTS or (ops[i]["e"] == "a" and ops[i]["sem"][0] in "fb")]

    cases = [times(*c) for c in CASES]
    cost, pred, succ, tail, wake = times(*MID)
    prio = [0.0] * n
    for i in range(n - 1, -1, -1):
        prio[i] = cost[i] + max([d + prio[k] for k, d in succ[i]] + [tail[i]])
    est = [0.0] * n
    for i in range(n):
        est[i] = max([0.0] + [est[k] + cost[k] + d for k, d in pred[i]])
    first = [0.5 * (prio[i] - est[i]) for i in range(n)]
    pool, seed = [], SEED
    for p in range(PASSES):
        if p % RUN == 0:
            best, short = None, None
            pool.append(None)
            for i in range(n):
                seed = (seed * 1103515245 + 12345) % 2147483648
                prio[i] = first[i] + SHAKE * seed / 2147483648
        elif p % 3 == 0:
            for i in range(n):
                seed = (seed * 1103515245 + 12345) % 2147483648
                prio[i] = SHAKE * seed / 2147483648 - short[1][i]
        at = place(pred, [(-1e6 + i if "load" in ops[i] else -prio[i]) for i in range(n)], [0.0] * n, range(n), cost, wake)
        end = max(at[i] + cost[i] + tail[i] for i in range(n))
        if short is None or end < short[0]:
            short = (end, at)
        order = sorted(range(n), key=lambda i: (at[i], i))
        score = sum(math.log(replay(order, c)[1]) for c in cases)
        if best is None or score < best[0]:
            best = pool[-1] = (score, order)
        back = place(succ, [-at[i] - cost[i] for i in range(n)], [0.0 if succ[i] else tail[i] for i in range(n)], range(n - 1, -1, -1), cost, wake)
        prio = [back[i] + cost[i] for i in range(n)]

    def cross(pool):
        best = min(pool)
        for _s, other in pool + pool:
            for cut in range(100, n - 50, 25):
                for a, b in ((best[1], other), (other, best[1])):
                    head = set(a[:cut])
                    order = a[:cut] + [i for i in b if i not in head]
                    best = min(best, (rate(order)[1], order))
        return best

    def rate(order):
        r = [replay(order, c) for c in cases]
        return sum(math.log(x[1] + x[2]) for x in r), sum(math.log(x[1]) for x in r)
    pool = [cross(pool)] + sorted(pool)[:KEPT - 1]
    for p in range((KEPT + 2) * MOVES):
        if p % MOVES == 0 and p <= KEPT * MOVES:
            if p:
                pool[p // MOVES - 1] = best
            best = pool[p // MOVES] if p < KEPT * MOVES else cross(pool)
            order, score = best[1], rate(best[1])[0]
        cost, pred, succ, tail, wake = cases[p % len(cases)]
        at, now, x = replay(order, cases[p % len(cases)])
        now += x
        if p % 50 == 49:
            for q in range(2):
                at = place(pred, [(-1e6 + i if "load" in ops[i] else at[i]) for i in range(n)], [0.0] * n, range(n), cost, wake)
                new = sorted(range(n), key=lambda i: (at[i], i))
                s, hard = rate(new)
                if s <= score:
                    order, score = new, s
                    if hard < best[0]:
                        best = (hard, new)
                at = place(succ, [-at[i] - cost[i] for i in range(n)], [0.0 if succ[i] else tail[i] for i in range(n)], range(n - 1, -1, -1), cost, wake)
                at = [-at[i] - cost[i] for i in range(n)]
            continue
        pos, last, arcs = {}, {}, []
        for j, i in enumerate(order):
            pos[i] = (j, [last[r] for r in [ops[i]["e"]] + sorted(ops[i]["banks"]) if r in last])
            for r in [ops[i]["e"]] + sorted(ops[i]["banks"]):
                last[r] = i
        seed = (seed * 1103515245 + 12345) % 2147483648
        i = marks[seed // 1024 % len(marks)]
        while at[i] > 0:
            k = max(pred[i], key=lambda x: at[x[0]] + cost[x[0]] + x[1], default=None)
            if k is None or at[k[0]] + cost[k[0]] + k[1] < at[i] - 1e-9:
                k = (max(pos[i][1], key=lambda x: at[x] + cost[x] + (wake if ops[x]["e"] != ops[i]["e"] else 0.0)),)
                arcs.append((k[0], i))
            i = k[0]
        for _ in range(min(8, len(arcs))):
            seed = (seed * 1103515245 + 12345) % 2147483648
            a, b = arcs[seed // 64 % min(len(arcs), NEAR)]
            if seed & 48 == 48:
                r = max([0.0] + [at[k] + cost[k] + d for k, d in pred[b]])
                j = pos[a][0]
                while j > 0 and (who[order[j]] != who[b] or at[order[j]] + (cost[order[j]] if seed & 2048 else 0.0) > r):
                    a = order[j] if who[order[j]] == who[b] else a
                    j -= 1
            if "load" in ops[a]:
                continue
            mid = order[pos[a][0]:pos[b][0] + 1]
            if seed & 32:
                need = {b}
                for i in reversed(mid):
                    if i in need:
                        need.update(k for k, _d in pred[i])
                if a in need:
                    continue
                mid = [i for i in mid if i in need] + [i for i in mid if i not in need]
            else:
                need = {a}
                for i in mid:
                    if any(k in need for k, _d in pred[i]):
                        need.add(i)
                if b in need:
                    continue
                mid = [i for i in mid if i not in need] + [i for i in mid if i in need]
            new = order[:pos[a][0]] + mid + order[pos[b][0] + 1:]
            x = replay(new, cases[p % len(cases)])
            if x[1] + x[2] > now + 0.02:
                continue
            s, hard = rate(new)
            if s <= score + 0.0001:
                order, score = new, s
                if hard < best[0]:
                    best = (hard, new)
                break
    return best[1]


def rank_program(g, core, T, topo):
    rank = T.rank_of(core)
    if rank is None:
        return
    eng = {"v": g.vector, "s": g.scalar, "t": g.tensor, "g": g, "y": g.sync}
    esem = {"v": "sv", "s": "ss", "t": "st", "g": "sg"}
    ops = []

    def A(name, a=0, b=None, step=1):
        b = SCRATCH[name][1][1] if b is None else b
        return ((T[name][:, a:b] if step == 1 else T[name][:, a:b:step]), ((name, a, b),), (b - a + step - 1) // step,
                SCRATCH[name][2] in (B, U16), "ps" if name[:2] == "ps" else "sb")

    def IND(w, off):
        wn, a, b = w[1][0]
        on, c, d = off[1][0]
        return T[wn][:, a:b].indirect(off[0]), ((wn, a, b), (on, c, d)), 16 * (d - c), SCRATCH[wn][2] == B, "ind"

    def part(o, a, b, step=1):
        name, s, _e = o[1][0]
        return A(name, s + a, s + b, step)

    def op(e, call, outs, ins, cost, sem=None, inc=1, arr=None):
        rd = [x for o in ins for x in o[1]]
        wr = []
        for o in outs:
            wr.append(o[1][0])
            rd += list(o[1][1:])
        ops.append({"e": e, "call": call, "rd": rd, "wr": wr, "cost": cost, "sem": sem or esem.get(e), "inc": inc, "arr": arr, "mm": None,
                    "kind": "sc" if any(len(o) > 4 and o[4] == "ind" for o in outs) else "ga" if any(o[4] == "ind" for o in ins) else ""})

    def vcost(o, ins, n, two=False):
        if o[4] == "ind":
            return 0.05 + n * 3.8 * CY
        if any(x[4] == "ind" for x in ins):
            return 0.05 + n * 1.5 * CY
        return max(64, n * (2 if two and all(x[4] == "sb" for x in ins) else 0.5 if not two and o[3] and ins[0][3] else 1)) * CY

    def tt(o, a, b, f):
        op("v", lambda: g.vector.tensor_tensor(o[0], a[0], b[0], f), [o], [a, b], vcost(o, [a, b], b[2], True))
        return o

    def ts(o, a, s1, f1, s2=None, f2=None):
        col = [s for s in (s1, s2) if isinstance(s, tuple)]
        x1, x2 = [s[0] if isinstance(s, tuple) else s for s in (s1, s2)]
        if f2 is None:
            op("v", lambda: g.vector.tensor_scalar(o[0], a[0], x1, None, f1), [o], [a] + col, vcost(o, [a], a[2]))
        else:
            op("v", lambda: g.vector.tensor_scalar(o[0], a[0], x1, x2, f1, f2), [o], [a] + col, vcost(o, [a], a[2]))
        return o

    def cp(o, a):
        op("v", lambda: g.vector.tensor_copy(o[0], a[0]), [o], [a], vcost(o, [a], a[2]))
        return o

    def scan(o, a, b, init, f0, f1):
        op("v", lambda: g.vector.tensor_tensor_scan(o[0], a[0], b[0], init, f0, f1), [o], [a, b], max(64, a[2] / (2 if o[3] and a[3] and b[3] else 1)) * CY)
        return o

    def ms(o, v):
        op("v", lambda: g.vector.memset(o[0], v), [o], [], max(64, o[2] * (0.5 if o[3] else 1)) * CY)
        return o

    def act(o, a, func=AF.Copy, bias=0.0, scale=1.0):
        c = 0.065 + a[2] * (3.8 if o[4] == "ind" else 1.5) * CY if "ind" in (o[4], a[4]) else max(64, a[2]) * CY
        if isinstance(scale, tuple):
            op("s", lambda: g.scalar.activation(o[0], a[0], func, scale=scale[0]), [o], [a, scale], c)
        elif bias == 0.0 and scale == 1.0:
            op("s", lambda: g.scalar.activation(o[0], a[0], func), [o], [a], c)
        else:
            op("s", lambda: g.scalar.activation(o[0], a[0], func, bias=bias, scale=scale), [o], [a], c)
        return o

    def mm(lst, first=True, last=True, whole=None):
        c = sum(max(64, x[2][2]) * (1 if x[1][3] else 4) for x in lst) * PE
        op("t", None, [whole] if whole else [x[0] for x in lst], [y for x in lst for y in x[1:]], c)
        ops[-1]["mm"] = (lst, first, last)

    def win(z, i):
        return A(z, 15 - i, 143 - i)

    def to_w(o, src, z):
        mm([(o, win(z, i), part(src, i, src[2], 16)) for i in range(16)])

    def to_r(on, srcs):
        n = 16 * srcs[0][2]
        mm([(A(on, i, n, 16), A("WR", 128 * i, 128 * i + 128), s) for i in range(16) for s in srcs], whole=A(on, 0, n))

    def rep(on, a, m, src, times):
        n = times * src[2]
        mm([(A(on, a + k, a + n, times), A(m), src) for k in range(times)], whole=A(on, a, a + n))

    def load(e, sem, o, tin):
        op(e, lambda: eng[e].dma_start(o[0], tin), [o], [], 0.1, sem, 16, 2.5 + o[2] * (2 if o[3] else 4) * 128 / 120e3)
        ops[-1]["load"] = True

    twins = [T.cores[rank ^ (1 + t % 3)] for t in range(NS)]
    nsent, sent = [0], [0]

    def send(t, s, rb, key):
        dst = twins[t]
        rid, pid, _se = topo.addr(dst)
        es = topo.engines(core, dst)
        w = s[2]
        r = A(rb, w * t, w * t + w)
        ls = "l" + str(t) if key == "c" else "lsem"
        op("g", lambda: g.remote_dma(out_ap=r[0], in_ap=s[0], remote_sem=T.sem[key + str(t)], local_sem=T.sem[ls], pid=pid, routing_id=rid,
                                     dma_engine_mask=sum(1 << x for x in es)), [], [s], 0.8, "lsem", len(es))
        i = len(ops) - 1
        ops[i]["send"] = sent[0]
        sent[0] = i
        way = 128 / len(es) * (0.05 + w * (2 if s[3] else 4) / 9e3)
        op("a", None, [(None, ((rb, w * t, w * t + w),))], [], way, key + str(t), len(es), 0.8)
        ops[-1]["send"] = i
        if key == "c":
            op("a", None, [], [s], 0.01, ls, len(es), 0.8)
            ops[-1]["send"] = i + 1
        else:
            nsent[0] += len(es)
        return r

    tops = {"tw": 0, "tx": 0, "ti": 0, "tb": 0, "tu": 0}

    def new(k, n=16):
        a = tops[k]
        if a + n > SCRATCH[k][1][1]:
            a = 0
        tops[k] = a + (n + 15) // 16 * 16
        return A(k, a, a + n)

    load("s", "dcs", A("cI"), T.cs[:])
    load("s", "dwk", A("wI"), T.wake[:])
    load("y", "dho", A("hI"), T.hold[:])
    load("y", "dsn", A("EW", EB, EB + 2048), T.snap[:])
    load("y", "dx", A("VW", 0, 8192), T.x[:])

    def iota(o, pattern, base, cm, flag=True):
        c = 0.13 + 2 * o[2] * CY
        if flag:
            op("g", lambda: g.iota(o[0], pattern, base, cm, allow_small_or_imprecise_dtypes=True), [o], [], c)
        else:
            op("g", lambda: g.iota(o[0], pattern, base, cm), [o], [], c)
    iota(A("pI"), [[1, 1]], 0, 1, False)
    iota(A("uF"), [[1, 256]], 0, 0)
    iota(A("mI"), [[1, 128]], 0, 0, False)
    iota(A("iA"), [[16, 16], [256, 8]], 0, 0)
    iota(A("iB"), [[0, 8], [16, 16]], 8192, 0)
    iota(A("M01"), [[0, 16], [1, 8]], 0, 0)
    iota(A("u16F"), [[0, 16], [1, 16]], 0, 0)
    iota(A("u2F"), [[0, 16], [16, 8], [0, 2]], 0, 0)
    iota(A("u3F"), [[1, 16], [0, 16]], 0, 0)
    iota(A("P01"), [[0, 16], [1, 2]], 0, 0)
    iota(A("TT", 6144, 8448), [[0, 2304]], 0, 0)
    ms(A("TT", 0, 768), 0.0)
    for a, b in ((768, 768), (1536, 1536), (3072, 1536), (4608, 1536)):
        act(A("TT", a, a + b), A("TT", 0, b))
    for a, m in (("r", 15), ("g", 112), ("k", 7), ("b", 1)):
        ts(A(a + "I"), A("pI"), m, OP.bitwise_and)
        cp(A(a + "F"), A(a + "I"))
    cp(A("pF"), A("pI"))
    ts(A("mG"), A("mI"), 112, OP.bitwise_and)
    ts(A("g15"), A("gF"), 15.0, OP.add)
    ts(A("g7"), A("gF"), 7.0, OP.add)
    ts(A("gx"), A("gF"), 1.0 / 16, OP.mult)
    ts(A("lo8"), A("rF"), 8.0, OP.is_lt)
    ts(A("hi8"), A("rF"), 8.0, OP.is_ge)
    ts(A("r1"), A("rF"), 1.0, OP.add)
    ts(A("JO"), A("iB"), A("rF"), OP.add)
    ts(A("J16"), A("JO", 0, 16), 0.0, OP.add)
    ts(A("OW"), A("JO", 0, 16), -8192.0, OP.add)
    ts(A("o8"), A("OW"), 8.0, OP.mult, 8.0, OP.add)
    ts(A("o64"), A("OW"), 64.0, OP.mult, 64.0, OP.add)
    ts(A("K1"), A("iB", 0, 16), 256.0 - 8192.0, OP.add)
    ts(A("Kr"), A("uF", 0, 16), 0.0, OP.mult, A("rF"), OP.add)
    SP = ts(new("tu", 128), A("iA"), A("rF"), OP.add)
    ts(A("POS"), A("uF", 0, 128), 16.0, OP.mult, A("rF"), OP.add)
    ts(A("POS"), A("POS"), 1.0 / 2048, OP.mult)
    ts(A("PI"), A("uF", 0, 8), 2.0, OP.mult, ts(new("tw", 1), A("kF"), 16.0, OP.mult, A("hi8"), OP.add), OP.add)
    ts(A("PO"), A("uF", 0, 8), ts(new("tw", 1), A("rF"), 8.0, OP.mult), OP.add)
    c3 = ts(new("tw", 1), A("bF"), 16.0, OP.mult)
    ts(A("X1"), A("uF", 0, 16), c3, OP.add)
    ts(A("X2"), A("uF", 0, 16), 2.0, OP.mult, 1.0, OP.add)
    ts(A("M01"), A("M01"), 0.0, OP.is_gt)
    ts(A("RS"), A("M01"), -16384.0 - 8388608.0, OP.mult, 8388608.0, OP.add)
    ts(A("HS"), A("M01"), 8388608.0, OP.mult, BASE, OP.add)
    ts(A("ZB"), A("uF", 0, 144), A("g15"), OP.is_equal)
    ts(A("ZA"), A("ZB"), A("lo8"), OP.mult)
    ts(A("ZH"), A("ZB"), A("hi8"), OP.mult)
    ts(A("ZX"), A("ZB"), ts(new("tw", 1), A("hi8"), 2047.0, OP.mult, 1.0, OP.add), OP.mult)
    zc = ts(new("tb", 144), A("uF", 0, 144), A("g7"), OP.is_equal)
    tt(A("ZC"), zc, A("ZB"), OP.add)
    ts(A("BO"), A("mG"), A("gF"), OP.is_equal)
    op("g", lambda: g.affine_select(T.LL[:], T.BO[:], [[-1, 128]], OP.is_ge, 0.0, 0, 1), [A("LL")], [A("BO")], 0.4)
    ts(A("ID"), A("uF", 0, 128), A("pF"), OP.is_equal)
    ts(A("IN"), A("ID"), -1.0, OP.mult)
    ts(A("HI"), A("ID"), HELD, OP.mult)
    ts(A("DL"), A("ID"), A("lo8"), OP.mult)
    ts(A("DH"), A("ID"), A("hi8"), OP.mult)
    dr = ts(new("tb", 128), A("IN"), A("rF"), OP.mult)
    tt(A("TRI"), dr, A("LL"), OP.subtract)
    ts(A("RM"), A("uF", 0, 16), A("rF"), OP.is_equal)
    ts(A("WY"), A("BO"), A("r1"), OP.mult)
    for i in range(16):
        ts(A("WR", 128 * i, 128 * i + 128), A("BO"), A("RM", i, i + 1), OP.mult)
        ts(A("Z2", 144 * i, 144 * i + 136), A("ZC", 0, 136), A("RM", i, i + 1), OP.mult)
    c4 = ts(new("tw", 1), A("rF"), 112.0, OP.add)
    ts(A("DW"), A("uF", 0, 240), c4, OP.is_equal, -2.0, OP.mult)
    ts(A("GI"), A("uF", 0, 8), A("gx"), OP.is_equal)
    ts(A("WG"), A("GI"), A("r1"), OP.mult)
    ts(A("MX"), A("u2F"), A("gF"), OP.is_equal)
    ts(A("NM"), A("u16F"), A("rF"), OP.not_equal, -9e29, OP.mult)
    ts(A("OHb"), A("u16F"), A("rF"), OP.is_equal)
    ts(A("OHa", 0, 256), A("u3F"), A("rF"), OP.is_equal)
    ms(A("OHa", 256, 512), 0.0)
    ts(A("u3F"), A("u16F"), 0.0, OP.is_gt)
    ts(A("X3"), A("uF", 0, 4), 64.0, OP.mult, A("pF"), OP.add)
    c5 = ts(new("tw", 1), A("kF"), 32.0, OP.mult, 8192.0 + 64.0, OP.add)
    ts(A("CK", 256, 288), A("uF", 0, 32), c5, OP.add)
    iota(A("PK"), [[128, 16], [1, 16]], 64, 0)
    ts(A("PK"), A("PK"), ts(new("tw", 1), A("kF"), 16.0, OP.mult), OP.add)
    ms(A("SM", 0, 32), 64.0)
    ms(A("z32"), 0.0)
    ms(A("thR"), -0.5)
    ms(A("thR", 0, 1), 1000.0)
    ms(A("VW", 8192, 8448), 0.0)
    c6, c7 = ms(new("tx", 128), 0.4), ms(new("tx", 128), 0.0)
    scan(A("wr"), c6, c7, 2.0 ** 85, OP.mult, OP.add)
    mm([(A("psM2", 0, 8), win("ZA", i), A("wr", i, 128, 16)) for i in range(16)])
    for h in range(2):
        cp(A("wT", 8 * h, 8 * h + 8), A("psM2", 0, 8))
    for t in range(NS):
        s = (16 * t, 16 * t + 16)
        ts(A("awI", *s), A("wI"), t, OP.arith_shift_right, 1, OP.bitwise_and)
        c8 = ts(new("tw", 1), A("hi8"), t - 1.0, OP.mult, 33.0, OP.add)
        ts(A("WHT", 256 * t, 256 * t + 256), A("uF"), A("lo8"), OP.mult, c8, OP.add)
    ts(A("naw"), A("awI"), -1.0, OP.mult, 1.0, OP.add)
    o1 = ts(new("tw"), A("OW"), 1.0, OP.add)
    for t in range(NS):
        s = (16 * t, 16 * t + 16)
        tt(A("ct", *s), A("naw", *s), o1, OP.subtract)
    tt(A("wa", 0, 16), A("awI", 0, 16), A("wT"), OP.mult)
    ts(A("wa", 16, 16 * NS), A("naw", 16, 16 * NS), 256.0, OP.mult)
    mm([(A("psM2", 8, 9), A("wr"), A("ID", 0, 1))])
    cp(A("wc"), A("psM2", 8, 9))

    x = ts(new("tx", 128), IND(A("hI"), A("PI")), HELD, OP.mult, BASE, OP.add)
    KH = tt(new("ti", 128), IND(A("cI"), A("PI")), x, OP.add)
    cU = cp(new("tu", 128), ts(new("ti", 128), KH, 8191, OP.bitwise_and))
    un = ts(new("tx", 128), KH, HELD, OP.is_lt)
    n = cp(new("tw"), part(scan(new("tx", 128), A("M01"), un, 0.0, OP.mult, OP.add), 7, 128, 8))
    FT = send(0, ts(A("FL", 0, 16), n, 0.0, OP.is_equal), "FR", "f")
    x = tt(new("tx", 128), A("cI"), A("JO"), OP.subtract)
    x = tt(new("tx", 128), x, A("hI"), OP.mult)
    tl = cp(new("tu", 128), tt(new("tx", 128), x, A("JO"), OP.add))
    for k in range(8):
        act(IND(A("TT"), part(tl, 16 * k, 16 * k + 16)), A("WHT", 0, 256), AF.Silu)
    for p in range(4):
        act(A("EW", EA + 512 * p, EA + 512 * p + 512), IND(A("EW", EB, EB + 2048), part(SP, 32 * p, 32 * p + 32)))
    chi = cp(new("tb", 128), A("cI"))
    clo = tt(new("tb", 128), A("cI"), chi, OP.subtract)
    for i in range(16):
        mm([(A("psD", 256 + i, 512, 16), A("Z2", 144 * i + 7 - k, 144 * i + 135 - k), part(c, 16 * k, 16 * k + 16)) for k in range(8) for c in (chi, clo)])
    act(A("CK", 0, 256), A("psD", 256, 512), AF.Copy, 64.0)
    tW = ms(new("tb"), 0.0)
    cur = cp(new("ti"), A("OW"))
    curU = cp(new("tu"), A("OW"))

    def hashes(src, o):
        for h in range(2):
            mm([(A("psM1", 256 + 64 * h, 320 + 64 * h), win("ZX", i), A("EW", src + 1024 * h + i, src + 1024 * h + 1024, 16)) for i in range(16)])
        xi = cp(new("ti", 128), A("psM1", 256, 384))
        pr = tt(new("ti", 128), ts(new("ti", 128), xi, 11, OP.arith_shift_right), ts(new("ti", 128), xi, 2047, OP.bitwise_and), OP.mult)
        h1 = ts(new("ti", 128), pr, 3, OP.arith_shift_right, 1023, OP.bitwise_and)
        h2 = ts(new("ti", 128), h1, 1.0, OP.add)
        ts(part(h2, 0, 128, 8), part(pr, 0, 128, 8), 3, OP.arith_shift_right, 8191, OP.bitwise_and)
        return scan(o, A("HS"), h2, BASE, OP.min, OP.add)

    NE = hashes(EA, new("tx", 128))
    NR, GR = {}, {}
    thB = ms(new("tw"), 200.0)

    for t in range(NS):
        eb, GT = (EA, EA, EB, EA, EB)[t], (EB, EA)[t & 1] + 2048
        lastt = t == NS - 1
        s16 = (16 * t, 16 * t + 16)
        run = scan(new("ti", 128), A("RS"), KH, 0.0, OP.add, OP.min)
        cfI = ts(new("ti"), part(run, 7, 128, 8), 8191, OP.bitwise_and)
        kb = new("tb", 32)
        cp(part(kb, 0, 16), cfI)
        tt(part(kb, 16, 32), cfI, part(kb, 0, 16), OP.subtract)
        cfF, cfU = cp(new("tw"), cfI), cp(new("tu"), cfI)
        to_r("psM1", [part(kb, 0, 16), part(kb, 16, 32)])
        cp(A("cfR"), A("psM1", 0, 256))
        for q in range(16):
            ts(A("EQ", 256 * q, 256 * q + 256), A("cfR"), part(cfF, q, q + 1), OP.is_equal)
        fm = tt(new("tb", 128), KH, run, OP.is_le)
        act(A("tau"), IND(A("TT"), cfU), AF.Copy, -32.0)
        who8, held8 = A("psM2", 0, 16), A("psM2", 16, 32)
        to_w(who8, A("tau"), "ZA")
        whoU = ts(new("tu"), who8, 0.125, OP.mult)
        d = tt(new("tw"), who8, A("o8"), OP.subtract)
        tt(A("vR"), IND(A("thR"), whoU), A("tau"), OP.is_le)
        to_w(held8, A("vR"), "ZH")
        h1 = ts(new("tw"), held8, 0.125, OP.mult, 1.0, OP.add)
        nx = tt(new("tw"), tt(new("tw"), held8, d, OP.mult), A("o64"), OP.add)
        if not lastt:
            tn = tt(new("tw"), n, h1, OP.mult)
            pre = tt(new("tw"), cfF, A("J16"), OP.subtract)
        V = new("tb", 32)
        if t == 0:
            ms(V, 0.0)
            cp(part(V, 0, 8), A("wa", 0, 8))
            ts(part(V, 16, 24), A("wa", 0, 8), 0.0, OP.is_gt, BIG, OP.mult)
            cp(part(V, 24, 32), A("wa", 8, 16))
        else:
            act(A("G1"), IND(A("OHb"), curU))
            act(A("G2"), IND(A("OHa"), cp(new("tu"), tt(new("tw"), cur, A("wa", *s16), OP.add))))
            for a, b, j, c in (("G1", "psM2", 256, "T1"), ("G2", "psMK", 0, "T2")):
                mm([(A(b, j + 128 * h, j + 128 + 128 * h), A(a, 128 * h, 128 * h + 128), A("ID")) for h in range(2)])
                act(A(c), A(b, j, j + 256), AF.Copy, 0.0, A("wc") if c == "T1" else 1.0)
            mm([(A("psM2", 256 + 128 * h, 384 + 128 * h), A("T1", 128 * h, 128 * h + 128), A("T2", 128 * h, 128 * h + 128)) for h in range(2)])
            act(A("WO"), A("psM2", 256, 512))
            x = ts(new("tw"), IND(A("WO"), A("X3", 0, 1)), 0.0, OP.is_gt, BIG, OP.mult)
            cp(part(V, 0, 16), IND(A("WO"), A("X3", 0, 1)))
            tt(part(V, 16, 32), IND(A("WO"), A("X3", 2, 3)), x, OP.max)
        b0 = tt(new("tw"), tt(new("tw"), A("naw", *s16), cur, OP.mult), A("ct", *s16), OP.add)
        for p in range(4):
            j = 512 * p
            gt, x = A("EW", GT + j, GT + j + 512), A("psX%d" % (p + 1))
            (act if JENG[t][p] == "s" else cp)(gt, IND(A("VW", 0, 8192), part(cU, 32 * p, 32 * p + 32)))
            mm([(x, A("IN"), A("EW", eb + j, eb + j + 512))], True, False)
            mm([(x, A("ID"), gt)], False, True)
            act(A("ad", j, j + 512), x, AF.Abs)
            if p & 1:
                mm([(A("psD", 32 * p - 32, 32 * p + 32), win("ZB", i), A("ad", j - 512 + i, j + 512, 16)) for i in range(16)])
        md = scan(new("tx", 128), A("M01"), A("psD", 0, 128), 0.0, OP.mult, OP.max)
        ok = A("BL", 32 * t, 32 * t + 32)
        for h in range(2):
            tt(part(ok, 16 * h, 16 * h + 16), part(md, 7, 128, 8), thB, OP.is_le)
        if t == 0:
            GR[0] = send(0, A("EW", GT, GT + 2048), "GR", "c")
        okT = send(t, ok, "BR", "b")
        X = hashes(GT, A("NG", 128 * t, 128 * t + 128))
        if t == 0:
            NR[0] = send(0, X, "NR", "n")
        if not lastt:
            GR[t + 1] = send(t + 1, A("EW", GT, GT + 2048), "GR", "c")
            NR[t + 1] = send(t + 1, X, "NR", "n")
        if t > 0:
            x = tt(A("psMK", 256, 384), A("psMK", 256, 384), NE, OP.mult)
            y = tt(new("tx", 128), A("psMK", 384, 512), X, OP.mult)
            NE = tt(new("tx", 128), x, y, OP.add)
            if not lastt:
                EL = ts(new("tu", 128), tt(new("tx", 128), A("psMK", 384, 512), A("POS"), OP.add), 2048.0, OP.mult)
                for p in range(4):
                    o = EA + EB - eb + 512 * p
                    act(A("EW", o, o + 512), IND(A("EW", eb, eb + 4096), part(EL, 32 * p, 32 * p + 32)))
        if t == YS:
            for j in range(0, 64, 16):
                mm([(A("psX1", b, 512, 64), A("VW", b, 8192, 64), A("WG")) for b in range(j, j + 16)])
            act(A("YT"), A("psX1"))
            yo = (T.YY[0:128:16, 0:8192], (("YY", 0, 8192),), 8192, False, "sb")

            def spread():
                for b in range(8):
                    g.sync.dma_start(T.YY[16 * b:16 * b + 1, 0:8192], T.YT[:, 64 * b:64 * b + 64]).then_inc(T.sem.yt_, 16)
            op("y", spread, [yo], [A("YT")], 0.5, "yt_", 128, 9.0)
        mk, ncm = new("tb", 32), new("tb", 32)
        keep, dec = part(mk, 0, 16), part(mk, 16, 32)
        nab = tt(new("tb"), part(ok, 0, 16), part(okT, 0, 16), OP.mult)
        rdy = tt(new("tb"), A("FL", *s16), FT, OP.mult)
        if t == 0:
            rdy = tt(new("tb"), tt(new("tb"), rdy, part(ok, 0, 16), OP.mult), part(okT, 0, 16), OP.mult)
        cum = scan(new("tb"), rdy, A("z32", 0, 16), 0.0, OP.add, OP.add)
        rK = tt(new("tb"), rdy, A("K1"), OP.mult)
        off = A("psD", 128, 144)
        mm([(off, A(a), b) for a, b in (("ID", A("K1")), ("ID", A("Kr")), ("TRI", rdy), ("BO", cum), ("IN", rK))])
        offU = cp(new("tu"), off)
        for h in range(2):
            ts(part(ncm, 16 * h, 16 * h + 16), off, 31.5, OP.is_gt)
        act(A("SL", 0, 32), A("CK", 256, 288))
        act(IND(A("SM"), offU), A("PK"), AF.Silu)
        if t == 0:
            cp(IND(A("SL"), offU), A("CK", 0, 256))
        else:
            act(IND(A("SL"), offU), A("CK", 0, 256), AF.Silu)
        for a, c in (("SM", 160), ("SL", 144)):
            mm([(A("psD", c, c + 16), A("DL"), A(a, 0, 16)), (A("psD", c, c + 16), A("DH"), A(a, 16, 32))])
        pU, zU = [ts(new("tu"), A("psD", c, c + 16), -64.0, OP.add) for c in (160, 144)]
        CR = act(A("CR"), IND(GR[t], pU))
        tt(keep, nab, part(ncm, 0, 16), OP.mult)
        act(dec, keep, AF.Copy, 1.0, -1.0)
        m1, m2 = (okT, ncm) if t == 0 else (ncm, okT)
        vv = tt(new("tb", 32), V, tt(new("tb", 32), ok, m1, OP.mult), OP.mult)
        if lastt:
            tt(A("vX"), IND(m2, A("X1")), tt(A("G1"), IND(vv, A("X1")), A("MX"), OP.mult), OP.mult)
        else:
            tt(A("vX"), IND(tt(new("tb", 32), vv, m2, OP.mult), A("X1")), A("MX"), OP.mult)
        for h in range(2):
            o = A("psM2", 64 + 16 * h, 80 + 16 * h)
            mm([(o, A("EQ", 256 * q + 128 * h, 256 * q + 128 * h + 128), A("vX", 16 * q, 16 * q + 16)) for q in range(16)]
               + [(o, A("DW", 112 - 16 * q, 240 - 16 * q), A("vX", 128 * h + 16 * q, 128 * h + 16 * q + 16)) for q in range(8)])
        mn = scan(new("tb", 32), A("P01"), A("psM2", 64, 96), 0.0, OP.mult, OP.min)
        tt(A("Er"), IND(mn, A("X2")), A("NM"), OP.is_lt)
        wT = A("psM2", 96, 112)
        if not lastt:
            mm([(part(wT, 8 * h, 8 * h + 8), A("Er", 128 * h, 128 * h + 128), A("GI")) for h in range(2)])
            thr = tt(new("tw"), tn, act(new("tw"), keep, AF.Copy, 7.5, -8.0), OP.add)
            FT = send(t + 1, tt(A("FL", 16 * t + 16, 16 * t + 32), wT, thr, OP.is_ge), "FR", "f")
            wn = tt(new("tb"), wT, h1, OP.is_ge)
        KS = KH
        picks = ((A("psMK", 128, 256), part(ncm, 0, 16), NR[t]), (A("psMK", 0, 128), nab, NE))
        for j, (p, m, c) in enumerate(picks[::-1] if t == 0 else picks):
            rep(p[1][0][0], p[1][0][1], "ID", m, 8)
            tt(p, p, tt(new("tx", 128), c, KS, OP.subtract), OP.mult)
            KS = tt(new("ti", 128) if j else p, c, p, OP.subtract)
        if not lastt:
            rep("psMK", 256, "ID", mk, 8)
        cI = ts(new("ti", 128), KS, 8191, OP.bitwise_and)
        if lastt:
            x = ts(A("psMK", 256, 384), KS, HELD, OP.is_ge, -5.0, OP.mult)
            rep("psD", 256, "ID", ts(new("tb"), h1, 2.0, OP.mult), 8)
            y = tt(new("tx", 128), A("psD", 256, 384), ts(new("tb", 128), fm, -1.5, OP.mult), OP.add)
            z = cp(new("tx", 128), IND(tt(new("tx", 128), x, y, OP.add), A("PO")))
            mm([(A("psM2", 128 + 16 * k + 8 * h, 136 + 16 * k + 8 * h), A("Er", 128 * h, 128 * h + 128), A("GI")) for h in range(2) for k in range(8)],
               whole=A("psM2", 128, 256))
            tt(A("oh"), A("psM2", 128, 256), z, OP.is_gt)
        else:
            rep("psD", 256, "HI", wn, 8)
            KH = A("psD", 256, 384)
            tt(KH, tt(KH, KH, fm, OP.mult), KS, OP.add)
        ct = new("tb", 32)
        tt(part(ct, 0, 16), nx, keep, OP.mult)
        if lastt:
            to_r("psM1", [part(ct, 0, 16)])
        else:
            tW = tt(part(ct, 16, 32), act(new("tb"), tW, AF.Copy, 1.0), keep, OP.mult)
            to_r("psM1", [ct])
        act(A("cdR"), A("psM1", 0, 256), AF.Copy, 0.0, 1.0 / 64)
        tt(A("yR"), IND(A("cdR"), curU), A("OHb"), OP.mult)
        y8 = part(scan(new("tb", 256), A("u3F"), A("yR"), 0.0, OP.mult, OP.add), 15, 256, 16)
        a = tt(new("tw"), tt(new("tw"), y8, A("awI", *s16), OP.mult), A("OW"), OP.add)
        sb = tt(new("tw"), ts(new("tw"), y8, 0.0, OP.is_gt), b0, OP.mult)
        if t >= YS:
            x = A("psX2" if lastt else "psM2", 256, 512)
            mm([(x, A("WY"), CR)])
            act(A("ys8"), x)
            cp(IND(A("YY"), zU), A("ys8"))
        if lastt:
            tt(A("ol"), a, sb, OP.add)
            cp(A("oc"), IND(cI, A("PO")))
        else:
            cur = tt(new("ti"), a, sb, OP.add)
            curU = cp(new("tu"), cur)
            cU = cp(new("tu", 128), cI)
            act(A("thR", 1, 257), A("psM1", 256, 512), AF.Copy, t + 0.5, -1.0)
            thB = act(new("tw"), keep, AF.Copy, 100200.0, -100000.0)
            n = tt(new("tw"), tt(new("tw"), n, wn, OP.subtract), act(new("tw"), keep, AF.Copy, 8.0, -8.0), OP.max)
            l = cp(new("tu"), tt(new("tw"), tt(new("tw"), pre, wn, OP.mult), A("J16"), OP.add))
            act(IND(A("TT"), l), A("WHT", 256 * t + 256, 256 * t + 512), AF.Silu)
            cp(IND(A("VW"), zU), CR)
    for e, sem, tout, o in (("s", "oc_", T.yc[:], A("oc")), ("s", "ol_", T.yl[:], A("ol")), ("y", "oh_", T.yh[:], A("oh")), ("y", "oy_", T.ys[:], yo)):
        (lambda e, sem, tout, o: op(e, lambda: eng[e].dma_start(tout, o[0]), [], [o], 0.1, sem, 16, 5.5 if sem == "oy_" else 3.0))(e, sem, tout, o)

    n = len(ops)
    deps = [set() for _ in range(n)]
    log = {}
    for i, o in enumerate(ops):
        for w, acc in ((False, o["rd"]), (True, o["wr"])):
            for name, a, b in acc:
                for a2, b2, w2, k in log.get(name, []):
                    if k != i and a < b2 and a2 < b and (w or w2):
                        deps[i].add(k)
        for w, acc in ((False, o["rd"]), (True, o["wr"])):
            for name, a, b in acc:
                old = log.get(name, [])
                if w:
                    old = [r for r in old if not (a <= r[0] and r[1] <= b)]
                log[name] = old + [(a, b, w, i)]
        if "send" in o:
            deps[i].add(o["send"])
        o["banks"] = {x[0] for x in o["rd"] + o["wr"] if x[0][:2] == "ps"}
    if not PLAN:
        PLAN.append(plan(ops, deps))
    order = PLAN[0]

    cnt = {}
    known = {e: {} for e in "vstgya"}
    clocks = {}
    log = {}

    def waits(e, acc, w):
        own = esem.get(e)
        for name, a, b in acc:
            ps = name[:2] == "ps"
            for a2, b2, w2, sem, m in log.get(name, []):
                ov = a < b2 and a2 < b
                if (ov and (w or w2) and e != "t") if sem == own else (ps or (ov and (w or w2))):
                    if known[e].get(sem, 0) < m:
                        eng[e].wait_ge(T.sem[sem], m)
                        for q, v in list(clocks[(sem, m)].items()):
                            known[e][q] = max(known[e].get(q, 0), v)

    def note(sem, m, acc, w):
        for name, a, b in acc:
            ps = name[:2] == "ps"
            log[name] = [r for r in log.get(name, []) if not ((w and a <= r[0] and r[1] <= b) or (ps and r[3] != sem)
                                                              or (r[3] == sem and r[2] == w and a <= r[0] and r[1] <= b))] + [(a, b, w, sem, m)]

    for i in order:
        o = ops[i]
        e, sem = o["e"], o["sem"]
        m = cnt[sem] = cnt.get(sem, 0) + o["inc"]
        if e == "a":
            clocks[(sem, m)] = {sem: m}
            note(sem, m, o["wr"], True)
            note(sem, m, o["rd"], False)
            continue
        if o["mm"] is None:
            waits(e, o["rd"], False)
            waits(e, o["wr"], True)
            x = o["call"]()
            if sem not in ("lsem", "yt_"):
                x.then_inc(T.sem[sem], o["inc"])
        else:
            lst, first, last = o["mm"]
            for q, (po, pl, pr) in enumerate(lst):
                waits(e, pl[1] + pr[1], False)
                waits(e, po[1], True)
                x = g.tensor.matmul(po[0], pl[0], pr[0], first and q == 0, last and q == len(lst) - 1)
            x.then_inc(T.sem.st, 1)
        if sem == "lsem":
            continue
        clocks[(sem, m)] = dict(known[e])
        clocks[(sem, m)][sem] = m
        note(sem, m, o["rd"], False)
        note(sem, m, o["wr"], True)
    for s in ("oc_", "ol_", "oh_", "oy_"):
        g.sync.wait_ge(T.sem[s], 16)
    g.wait_ge(T.sem.lsem, nsent[0])
    for s in ("sv", "ss", "st", "sg", "l%d" % (NS - 1)):
        g.wait_ge(T.sem[s], cnt[s])
